import numpy as np
import ml_dtypes


def mxq(x, axis, fmt="e4m3"):
    dtype, down = {"e4m3": (ml_dtypes.float8_e4m3fn, 7), "e5m2": (ml_dtypes.float8_e5m2, 14)}[fmt]
    v = np.moveaxis(np.asarray(x, np.float32).astype(ml_dtypes.bfloat16).astype(np.float64), axis, -1)
    blocks = v.reshape(v.shape[:-1] + (-1, 32))
    amax = np.abs(blocks).max(-1, keepdims=True)
    byte = np.maximum(np.where(amax > 0, np.frexp(amax)[1] - 1 + 127, 0) - down, 1)
    scale = np.exp2(byte - 127.0)
    codes = (blocks / scale).astype(np.float32).astype(dtype).astype(np.float64)
    return np.moveaxis((codes * scale).reshape(v.shape), -1, axis)


WIDE = False


def mx_kscale(k):
    if not WIDE:
        return np.ones(k)
    levels = np.array([10, -10, 5, -5, 0])
    if k % 512:
        return np.exp2(np.random.permutation(np.resize(levels, k // 32))).repeat(32)
    a = np.empty((k // 512, 16))
    for p in range(k // 512):
        a[p, :8] = np.random.permutation(np.resize(levels, 8))
        for g in range(8):
            far = levels[np.abs(levels - a[p, g]) >= 10]
            a[p, g + 8] = far[np.random.randint(len(far))]
    return np.exp2(a.ravel()).repeat(32)


def f64(x):
    return np.asarray(x).astype(np.float64)


def striped(idx):
    return np.tile(np.asarray(idx).reshape(-1, 16).T, (8, 1)).astype(np.uint16)


def unstriped(offs):
    return offs[:16].T.reshape(-1).astype(np.int64)


E2M1 = np.array([0.0, 0.5, 1.0, 1.5, 2.0, 3.0, 4.0, 6.0, -0.0, -0.5, -1.0, -1.5, -2.0, -3.0, -4.0, -6.0])


def pack_weight(w, fmt):
    k, n = w.shape
    w = f64(np.asarray(w, np.float32).astype(ml_dtypes.bfloat16)).reshape(k // 32, 32, n)
    amax = np.abs(w).max(1)
    if fmt == "e4m3":
        byte = np.frexp(amax)[1] - 1 + 127 - 7
    else:
        mant, ex = np.frexp(amax / 6.0)
        byte = np.where(mant > 0.5, ex, ex - 1) + 127
    byte = np.clip(np.where(amax > 0, byte, 1), 1, 254)
    scaled = (w * np.exp2(127.0 - byte)[:, None, :]).reshape(k, n).astype(np.float32)
    by_word = np.ascontiguousarray(scaled.reshape(k // 512, 128, 4, n).transpose(0, 1, 3, 2))
    if fmt == "e4m3":
        words = by_word.astype(ml_dtypes.float8_e4m3fn).view(np.uint8)
    else:
        c = by_word.astype(ml_dtypes.float4_e2m1fn).view(np.uint8) & 0xF
        words = (c[..., 0::2] | (c[..., 1::2] << 4)).reshape(k // 512, 128, 2 * n)
    return np.ascontiguousarray(words), np.ascontiguousarray(byte.astype(np.uint8).reshape(k // 512, 16, n))


def unpack_weight(words, scales, fmt):
    g, _, n = scales.shape
    words = np.ascontiguousarray(words).reshape(g, 128, n, -1)
    if fmt == "e4m3":
        vals = words.view(ml_dtypes.float8_e4m3fn).astype(np.float64)
    else:
        nib = np.empty((g, 128, n, 4), np.uint8)
        nib[..., 0::2] = words & 0xF
        nib[..., 1::2] = words >> 4
        vals = E2M1[nib]
    vals = vals * np.repeat(np.exp2(scales.astype(np.float64) - 127.0), 8, axis=1)[..., None]
    return vals.transpose(0, 1, 3, 2).reshape(g * 512, n)


B, N, T, D, NQ = 1, 512, 2048, 512, 512
DV = 512


def sgn(shape):
    return np.random.uniform(0.5, 2.0, shape) * np.where(np.random.standard_normal(shape) < 0, -1.0, 1.0)


def setup_inputs():
    n = np.random.standard_normal
    idx = np.random.permutation(T)[:B * N]
    s = mx_kscale(D)[:, None]
    u = mx_kscale(N)
    ut = np.ones(T)
    ut[idx] = u
    kp = pack_weight(n((D, T)) / s, "e4m3")
    cp = pack_weight(n((D, T)) / s, "e4m3")
    return {
        "qT": (n((B, D, NQ)) * s * (0.40 / np.sqrt(D))).astype(np.float32),
        "k_words": kp[0],
        "k_scales": kp[1],
        "c_words": cp[0],
        "c_scales": cp[1],
        "vT": (n((DV, T)) / ut).astype(np.float32),
        "ls": (np.random.uniform(7.0, 7.6, (B, 1, NQ))).astype(np.float32),
        "us": (sgn((B, N, 1)) * u[:, None]).astype(np.float32),
        "offs": striped(idx),
    }


def reference(qT, k_words, k_scales, c_words, c_scales, vT, ls, us, offs):
    idx = unstriped(offs)
    pick = lambda x, which: x[:, which].reshape(x.shape[0], B, -1).transpose(1, 0, 2)
    k = unpack_weight(k_words, k_scales, "e4m3")
    kg = pick(k, idx)
    c = unpack_weight(c_words, c_scales, "e4m3")
    cg = pick(c, idx)
    qq = mxq(f64(qT), 1, "e4m3")
    a = kg.transpose(0, 2, 1) @ qq
    z = cg.transpose(0, 2, 1) @ qq
    y = np.exp(1.5 * a - 0.5 * z - f64(ls)) * f64(us)
    wq = mxq(y, 1, "e4m3")
    o = wq.transpose(0, 2, 1) @ mxq(pick(f64(vT), idx).transpose(0, 2, 1), 1, "e4m3")
    return o

@@ -1,0 +1,194 @@
+from contextlib import ExitStack
+
+import concourse.mybir as mybir
+from concourse.masks import make_identity
+
+F32 = mybir.dt.float32
+BF16 = mybir.dt.bfloat16
+I32 = mybir.dt.int32
+U32 = mybir.dt.uint32
+U16 = mybir.dt.uint16
+U8 = mybir.dt.uint8
+FP8X4 = mybir.dt.float8_e4m3fn_x4
+ACT = mybir.ActivationFunctionType
+ALU = mybir.AluOpType
+
+P = 128
+N, T, D, NQ, DV = 512, 2048, 512, 512, 512
+QB = NQ // P
+EB = DV // P
+FLOPS = 2 * 2 * N * D * NQ + 2 * N * NQ * DV
+RB = (2, 3)
+
+
+def tile_attend_at_cfg_topk_kernel(tc, qT, k_words, k_scales, c_words, c_scales, vT, ls, us, offs, out):
+    nc = tc.nc
+    with ExitStack() as ctx:
+        held = ctx.enter_context(tc.tile_pool(name="held", bufs=1))
+        big = ctx.enter_context(tc.tile_pool(name="big", bufs=4))
+        ring = ctx.enter_context(tc.tile_pool(name="ring", bufs=2))
+        psum = ctx.enter_context(tc.psum_pool(name="psum", bufs=1))
+
+        offsets = held.tile([P, N // 16], U16, name="offsets")
+        nc.sync.dma_start(offsets[:], offs)
+
+        ident = held.tile([P, P], F32, name="ident")
+        make_identity(nc, ident[:])
+        ks_win = held.tile([P, T // 4], I32, name="ks_win")
+        cs_win = held.tile([P, T // 4], I32, name="cs_win")
+        ls_rows = held.tile([P, P], F32, name="ls_rows")
+        warm_in = held.tile([P, 1], F32, name="warm_in")
+        warm_out = held.tile([P, 1], F32, name="warm_out")
+        nc.vector.memset(ks_win[:], 0)
+        nc.vector.memset(cs_win[:], 0)
+        nc.vector.memset(ls_rows[:], 0.0)
+        nc.vector.memset(warm_in[:], 0.0)
+
+        q_raw = big.tile([P, 4, NQ], F32, name="q_raw", tag="big")
+        nc.sync.dma_start(q_raw[:], qT[0].rearrange("(p t) q -> p t q", t=4))
+        for quad in range(4):
+            nc.scalar.dma_start(ks_win[32 * quad : 32 * quad + 4, :], k_scales[0, 4 * quad : 4 * quad + 4, :].bitcast(I32))
+        nc.scalar.activation(warm_out[:], warm_in[:], ACT.Exp)
+        k_win = big.tile([P, T], I32, name="k_win", tag="big")
+        nc.sync.dma_start(k_win[:], k_words[0].rearrange("p t r -> p (t r)").bitcast(I32))
+        c_win = big.tile([P, T], I32, name="c_win", tag="big")
+        nc.sync.dma_start(c_win[:], c_words[0].rearrange("p t r -> p (t r)").bitcast(I32))
+        for quad in range(4):
+            nc.gpsimd.dma_start(cs_win[32 * quad : 32 * quad + 4, :], c_scales[0, 4 * quad : 4 * quad + 4, :].bitcast(I32))
+        nc.gpsimd.dma_start(ls_rows[0:QB, :], ls[0, 0].rearrange("(j m) -> j m", j=QB))
+        us_sb = held.tile([P, 4], F32, name="us_sb")
+        nc.gpsimd.dma_start(us_sb[:], us[0].rearrange("(p t) o -> p (t o)", t=4))
+        v_win = []
+        for b in range(EB):
+            v_win.append(big.tile([P, T], F32, name=f"v_win{b}", tag="big"))
+            nc.sync.dma_start(v_win[b][:], vT[b * P : (b + 1) * P, :])
+
+
+        q_bf = held.tile([P, NQ, 4], BF16, name="q_bf", align_bytes=64)
+        q_codes = held.tile([P, NQ], U32, name="q_codes", align_bytes=64)
+        q_scale = held.tile([P, NQ], U8, name="q_scale", align_bytes=64)
+        nc.scalar.copy(q_bf[:, 0:256, :], q_raw[:, :, 0:256].rearrange("p t q -> p q t"))
+        ks_g = held.tile([P, N], U8, name="ks_g", align_bytes=64)
+        nc.vector.tensor_copy(ks_g[:], ks_win[:].bitcast(U8).indirect(offsets[:]))
+        nc.vector.tensor_copy(q_bf[:, 256:512, :], q_raw[:, :, 256:512].rearrange("p t q -> p q t"))
+        for h in range(2):
+            cols = slice(h * 256, (h + 1) * 256)
+            nc.vector.quantize_mx(q_codes[:, cols].bitcast(FP8X4), q_scale[:, cols], q_bf[:, cols, :].rearrange("p q t -> p (q t)"))
+
+
+        def scores(words, scale, j, first=False):
+            ps = psum.tile([P, N], F32, name="first_ps", tag="vt") if first else psum.tile([P, N], F32, name="score_ps", tag="wide", bufs=5)
+            cols = slice(j * P, (j + 1) * P)
+            nc.tensor.matmul_mx(ps[:], lhsT=q_codes[:, cols].bitcast(FP8X4), lhsT_scale=q_scale[:, cols],
+                                rhs=words[:].bitcast(FP8X4), rhs_scale=scale[:], start=True, stop=True)
+            return ps[:].rearrange("p (m t) -> p t m", t=4)
+
+        k_g = held.tile([P, N], U32, name="k_g", align_bytes=64)
+        nc.vector.tensor_copy(k_g[:], k_win[:].bitcast(U32).indirect(offsets[:]))
+        a_sb = held.tile([P, QB, 4, P], F32, name="a_sb")
+        for j in range(QB):
+            nc.scalar.mul(a_sb[:, j], scores(k_g, ks_g, j, j == 0), 1.5)
+        ls_ps = psum.tile([P, 2, P], F32, name="ls_ps", tag="vt")
+        nc.tensor.transpose(ls_ps[:, 0, :], ls_rows[:], ident[:])
+        neg_ls = held.tile([P, QB], F32, name="neg_ls")
+        nc.scalar.mul(neg_ls[:], ls_ps[:, 0, 0:QB], -1.0)
+        cs_g = held.tile([P, N], U8, name="cs_g", align_bytes=64)
+        nc.vector.tensor_copy(cs_g[:], cs_win[:].bitcast(U8).indirect(offsets[:]))
+        c_g = held.tile([P, N], U32, name="c_g", align_bytes=64)
+        nc.vector.tensor_copy(c_g[:], c_win[:].bitcast(U32).indirect(offsets[:]))
+
+        y_bf = held.tile([P, NQ, 2, 2], BF16, name="y_bf", align_bytes=64)
+        y_codes = held.tile([P, NQ], U32, name="y_codes", align_bytes=64)
+        y_scale = held.tile([P, NQ], U8, name="y_scale", align_bytes=64)
+        us_bc = us_sb[:].rearrange("p (a b) -> p b a", a=2).unsqueeze(1).to_broadcast([P, P, 2, 2])
+        v_codes = held.tile([P, DV], U32, name="v_codes", align_bytes=64)
+        v_scale = held.tile([P, DV], U8, name="v_scale", align_bytes=64)
+
+        def weights_front(j):
+            z_ps = scores(c_g, cs_g, j)
+            s_sb = ring.tile([P, 4, P], F32, name="s_sb")
+            if j in RB:
+                nc.scalar.activation(s_sb[:], z_ps, ACT.Identity, bias=neg_ls[:, j : j + 1], scale=-0.5)
+                return s_sb
+            nc.vector.scalar_tensor_tensor(s_sb[:], z_ps, -0.5, a_sb[:, j], ALU.mult, ALU.add)
+            e_sb = ring.tile([P, 4, P], F32, name="e_sb")
+            nc.scalar.activation(e_sb[:], s_sb[:], ACT.Exp, bias=neg_ls[:, j : j + 1])
+            return e_sb
+
+        def weights_back(j, src):
+            cols = slice(j * P, (j + 1) * P)
+            t_ps = psum.tile([P, 2, 2, P], F32, name="t_ps", tag="st", bufs=2)
+            for b in range(2):
+                for a in range(2):
+                    if j in RB:
+                        nc.tensor.matmul(t_ps[:, b, a, :], a_sb[:, j, 2 * a + b, :], ident[:], start=True, stop=False, is_transpose=True)
+                        nc.tensor.matmul(t_ps[:, b, a, :], src[:, 2 * a + b, :], ident[:], start=False, stop=True, is_transpose=True)
+                    else:
+                        nc.tensor.transpose(t_ps[:, b, a, :], src[:, 2 * a + b, :], ident[:])
+            turned = t_ps[:].rearrange("p b a q -> p q b a")
+            if j in RB:
+                e2 = ring.tile([P, P, 2, 2], F32, name="e2")
+                nc.scalar.activation(e2[:], turned, ACT.Exp)
+                turned = e2[:]
+            nc.vector.tensor_tensor(y_bf[:, cols], turned, us_bc, ALU.mult)
+
+        def weights_quant(j):
+            cols = slice(j * P, (j + 1) * P)
+            nc.vector.quantize_mx(y_codes[:, cols].bitcast(FP8X4), y_scale[:, cols], y_bf[:, cols].rearrange("p q b a -> p (q b a)"))
+
+        def values_front(e):
+            v_g = ring.tile([P, 2, P, 2], BF16, name="v_g")
+            nc.vector.tensor_copy(v_g[:].rearrange("p b m a -> p m a b"), v_win[e][:].indirect(offsets[:]))
+            words = v_g[:].rearrange("p b m a -> p (b m a)").bitcast(F32)
+            v_ps = psum.tile([P, 2, P], F32, name="v_ps", tag="vt")
+            for b in range(2):
+                nc.tensor.transpose(v_ps[:, b, :], words[:, b * P : (b + 1) * P], ident[:])
+            v_bf = ring.tile([P, 4 * P], BF16, name="v_bf", align_bytes=64)
+            nc.scalar.copy(v_bf[:].bitcast(F32).rearrange("p (e b) -> p e b", b=2), v_ps[:].rearrange("p b e -> p e b"))
+            return v_bf
+
+        def values_quant(e, v_bf):
+            cols = slice(e * P, (e + 1) * P)
+            nc.vector.quantize_mx(v_codes[:, cols].bitcast(FP8X4), v_scale[:, cols], v_bf[:])
+
+        out_rows = out[0].rearrange("(j p) e -> p j e", p=P)
+
+        def product(e0, width, groups):
+            cols = slice(e0 * P, e0 * P + width)
+            o_sb = held.tile([P, QB, width], F32, name=f"o_sb{e0}")
+            for g, js in enumerate(groups):
+                o_ps = psum.tile([P, len(js), width], F32, name="o_ps", tag="wide", bufs=5)
+                for i, j in enumerate(js):
+                    qc = slice(j * P, (j + 1) * P)
+                    nc.tensor.matmul_mx(o_ps[:, i, :], lhsT=y_codes[:, qc].bitcast(FP8X4), lhsT_scale=y_scale[:, qc],
+                                        rhs=v_codes[:, cols].bitcast(FP8X4), rhs_scale=v_scale[:, cols], start=True, stop=True)
+                dst = o_sb[:, js[0] : js[-1] + 1, :]
+                if g % 2 == 0:
+                    nc.scalar.copy(dst, o_ps[:])
+                else:
+                    nc.vector.tensor_copy(dst, o_ps[:])
+            nc.sync.dma_start(out_rows[:, :, cols], o_sb[:])
+
+        f0 = weights_front(0)
+        f1 = weights_front(1)
+        weights_back(0, f0)
+        vb0 = values_front(0)
+        f2 = weights_front(2)
+        weights_back(1, f1)
+        weights_quant(0)
+        f3 = weights_front(3)
+        weights_back(2, f2)
+        values_quant(0, vb0)
+        weights_quant(1)
+        vb1 = values_front(1)
+        weights_back(3, f3)
+        weights_quant(2)
+        values_quant(1, vb1)
+        weights_quant(3)
+        vb2 = values_front(2)
+        product(0, 256, [(0, 1), (2, 3)])
+        values_quant(2, vb2)
+        vb3 = values_front(3)
+        product(2, 128, [(0, 1, 2, 3)])
+        values_quant(3, vb3)
+        product(3, 128, [(0, 1), (2, 3)])

@@ -18,66 +18,68 @@ N, T, D, NQ, DV = 512, 2048, 512, 512, 512
 QB = NQ // P
 EB = DV // P
 FLOPS = 2 * 2 * N * D * NQ + 2 * N * NQ * DV
-RB = (2, 3)
+RB = (1, 2, 3,)
+W = 4 * T
+Q_SPLIT = 384
 
 
 def tile_attend_at_cfg_topk_kernel(tc, qT, k_words, k_scales, c_words, c_scales, vT, ls, us, offs, out):
     nc = tc.nc
     with ExitStack() as ctx:
         held = ctx.enter_context(tc.tile_pool(name="held", bufs=1))
-        big = ctx.enter_context(tc.tile_pool(name="big", bufs=4))
-        ring = ctx.enter_context(tc.tile_pool(name="ring", bufs=2))
+        placed = ctx.enter_context(tc.tile_pool(name="placed", bufs=1))
+        ring = ctx.enter_context(tc.tile_pool(name="ring", bufs=4))
         psum = ctx.enter_context(tc.psum_pool(name="psum", bufs=1))
 
         offsets = held.tile([P, N // 16], U16, name="offsets")
         nc.sync.dma_start(offsets[:], offs)
-
         ident = held.tile([P, P], F32, name="ident")
-        make_identity(nc, ident[:])
-        ks_win = held.tile([P, T // 4], I32, name="ks_win")
+        ks_win = placed.tile([P, T // 4], I32, name="ks_win", offset=EB * W)
         cs_win = held.tile([P, T // 4], I32, name="cs_win")
         ls_rows = held.tile([P, P], F32, name="ls_rows")
         warm_in = held.tile([P, 1], F32, name="warm_in")
         warm_out = held.tile([P, 1], F32, name="warm_out")
-        nc.vector.memset(ks_win[:], 0)
-        nc.vector.memset(cs_win[:], 0)
-        nc.vector.memset(ls_rows[:], 0.0)
         nc.vector.memset(warm_in[:], 0.0)
+        nc.vector.memset(ks_win[:], 0)
+        nc.vector.memset(ls_rows[:], 0.0)
+        nc.vector.memset(cs_win[:], 0)
+        make_identity(nc, ident[:])
+        nc.scalar.activation(warm_out[:], warm_in[:], ACT.Exp)
 
-        q_raw = big.tile([P, 4, NQ], F32, name="q_raw", tag="big")
+        q_raw = held.tile([P, 4, NQ], F32, name="q_raw")
         nc.sync.dma_start(q_raw[:], qT[0].rearrange("(p t) q -> p t q", t=4))
         for quad in range(4):
-            nc.scalar.dma_start(ks_win[32 * quad : 32 * quad + 4, :], k_scales[0, 4 * quad : 4 * quad + 4, :].bitcast(I32))
-        nc.scalar.activation(warm_out[:], warm_in[:], ACT.Exp)
-        k_win = big.tile([P, T], I32, name="k_win", tag="big")
+            nc.sync.dma_start(ks_win[32 * quad : 32 * quad + 4, :], k_scales[0, 4 * quad : 4 * quad + 4, :].bitcast(I32))
+        k_win = held.tile([P, T], I32, name="k_win")
         nc.sync.dma_start(k_win[:], k_words[0].rearrange("p t r -> p (t r)").bitcast(I32))
-        c_win = big.tile([P, T], I32, name="c_win", tag="big")
-        nc.sync.dma_start(c_win[:], c_words[0].rearrange("p t r -> p (t r)").bitcast(I32))
+        nc.sync.dma_start(ls_rows[0:QB, :], ls[0, 0].rearrange("(j m) -> j m", j=QB))
         for quad in range(4):
-            nc.gpsimd.dma_start(cs_win[32 * quad : 32 * quad + 4, :], c_scales[0, 4 * quad : 4 * quad + 4, :].bitcast(I32))
-        nc.gpsimd.dma_start(ls_rows[0:QB, :], ls[0, 0].rearrange("(j m) -> j m", j=QB))
+            nc.sync.dma_start(cs_win[32 * quad : 32 * quad + 4, :], c_scales[0, 4 * quad : 4 * quad + 4, :].bitcast(I32))
+        c_win = held.tile([P, T], I32, name="c_win")
+        nc.sync.dma_start(c_win[:], c_words[0].rearrange("p t r -> p (t r)").bitcast(I32))
         us_sb = held.tile([P, 4], F32, name="us_sb")
-        nc.gpsimd.dma_start(us_sb[:], us[0].rearrange("(p t) o -> p (t o)", t=4))
         v_win = []
         for b in range(EB):
-            v_win.append(big.tile([P, T], F32, name=f"v_win{b}", tag="big"))
+            v_win.append(placed.tile([P, T], F32, name=f"v_win{b}", offset=b * W))
             nc.sync.dma_start(v_win[b][:], vT[b * P : (b + 1) * P, :])
-
+            if b == 0:
+                nc.sync.dma_start(us_sb[:], us[0].rearrange("(p t) o -> p (t o)", t=4))
 
         q_bf = held.tile([P, NQ, 4], BF16, name="q_bf", align_bytes=64)
-        q_codes = held.tile([P, NQ], U32, name="q_codes", align_bytes=64)
         q_scale = held.tile([P, NQ], U8, name="q_scale", align_bytes=64)
-        nc.scalar.copy(q_bf[:, 0:256, :], q_raw[:, :, 0:256].rearrange("p t q -> p q t"))
+        q_turned = q_raw[:].rearrange("p t q -> p q t")
+        nc.scalar.copy(q_bf[:, 0:256, :], q_turned[:, 0:256, :])
+        nc.scalar.copy(q_bf[:, 256:Q_SPLIT, :], q_turned[:, 256:Q_SPLIT, :])
+        nc.vector.tensor_copy(q_bf[:, Q_SPLIT:NQ, :], q_turned[:, Q_SPLIT:NQ, :])
         ks_g = held.tile([P, N], U8, name="ks_g", align_bytes=64)
         nc.vector.tensor_copy(ks_g[:], ks_win[:].bitcast(U8).indirect(offsets[:]))
-        nc.vector.tensor_copy(q_bf[:, 256:512, :], q_raw[:, :, 256:512].rearrange("p t q -> p q t"))
+        q_codes = placed.tile([P, NQ], U32, name="q_codes", offset=EB * W, align_bytes=64)
         for h in range(2):
             cols = slice(h * 256, (h + 1) * 256)
             nc.vector.quantize_mx(q_codes[:, cols].bitcast(FP8X4), q_scale[:, cols], q_bf[:, cols, :].rearrange("p q t -> p (q t)"))
 
-
-        def scores(words, scale, j, first=False):
-            ps = psum.tile([P, N], F32, name="first_ps", tag="vt") if first else psum.tile([P, N], F32, name="score_ps", tag="wide", bufs=5)
+        def scores(words, scale, j, tag, bufs):
+            ps = psum.tile([P, N], F32, name="score_ps", tag=tag, bufs=bufs)
             cols = slice(j * P, (j + 1) * P)
             nc.tensor.matmul_mx(ps[:], lhsT=q_codes[:, cols].bitcast(FP8X4), lhsT_scale=q_scale[:, cols],
                                 rhs=words[:].bitcast(FP8X4), rhs_scale=scale[:], start=True, stop=True)
@@ -87,8 +89,8 @@ def tile_attend_at_cfg_topk_kernel(tc, qT, k_words, k_scales, c_words, c_scales,
         nc.vector.tensor_copy(k_g[:], k_win[:].bitcast(U32).indirect(offsets[:]))
         a_sb = held.tile([P, QB, 4, P], F32, name="a_sb")
         for j in range(QB):
-            nc.scalar.mul(a_sb[:, j], scores(k_g, ks_g, j, j == 0), 1.5)
-        ls_ps = psum.tile([P, 2, P], F32, name="ls_ps", tag="vt")
+            nc.scalar.mul(a_sb[:, j], scores(k_g, ks_g, j, "vt" if j == 0 else "wide", 2 if j == 0 else 4), 1.5)
+        ls_ps = psum.tile([P, 2, P], F32, name="ls_ps", tag="vt", bufs=2)
         nc.tensor.transpose(ls_ps[:, 0, :], ls_rows[:], ident[:])
         neg_ls = held.tile([P, QB], F32, name="neg_ls")
         nc.scalar.mul(neg_ls[:], ls_ps[:, 0, 0:QB], -1.0)
@@ -97,32 +99,31 @@ def tile_attend_at_cfg_topk_kernel(tc, qT, k_words, k_scales, c_words, c_scales,
         c_g = held.tile([P, N], U32, name="c_g", align_bytes=64)
         nc.vector.tensor_copy(c_g[:], c_win[:].bitcast(U32).indirect(offsets[:]))
 
-        y_bf = held.tile([P, NQ, 2, 2], BF16, name="y_bf", align_bytes=64)
-        y_codes = held.tile([P, NQ], U32, name="y_codes", align_bytes=64)
+        y_bf, y_codes, v_bf, v_codes, front = {}, {}, {}, {}, {}
         y_scale = held.tile([P, NQ], U8, name="y_scale", align_bytes=64)
         us_bc = us_sb[:].rearrange("p (a b) -> p b a", a=2).unsqueeze(1).to_broadcast([P, P, 2, 2])
-        v_codes = held.tile([P, DV], U32, name="v_codes", align_bytes=64)
         v_scale = held.tile([P, DV], U8, name="v_scale", align_bytes=64)
 
         def weights_front(j):
-            z_ps = scores(c_g, cs_g, j)
+            z_ps = scores(c_g, cs_g, j, "wide", 4)
             s_sb = ring.tile([P, 4, P], F32, name="s_sb")
             if j in RB:
                 nc.scalar.activation(s_sb[:], z_ps, ACT.Identity, bias=neg_ls[:, j : j + 1], scale=-0.5)
-                return s_sb
+                front[j] = s_sb
+                return
             nc.vector.scalar_tensor_tensor(s_sb[:], z_ps, -0.5, a_sb[:, j], ALU.mult, ALU.add)
             e_sb = ring.tile([P, 4, P], F32, name="e_sb")
             nc.scalar.activation(e_sb[:], s_sb[:], ACT.Exp, bias=neg_ls[:, j : j + 1])
-            return e_sb
+            front[j] = e_sb
 
-        def weights_back(j, src):
-            cols = slice(j * P, (j + 1) * P)
+        def weights_back(j, place):
+            src = front[j]
             t_ps = psum.tile([P, 2, 2, P], F32, name="t_ps", tag="st", bufs=2)
             for b in range(2):
                 for a in range(2):
                     if j in RB:
-                        nc.tensor.matmul(t_ps[:, b, a, :], a_sb[:, j, 2 * a + b, :], ident[:], start=True, stop=False, is_transpose=True)
-                        nc.tensor.matmul(t_ps[:, b, a, :], src[:, 2 * a + b, :], ident[:], start=False, stop=True, is_transpose=True)
+                        nc.tensor.matmul(t_ps[:, b, a, :], src[:, 2 * a + b, :], ident[:], start=True, stop=False, is_transpose=True)
+                        nc.tensor.matmul(t_ps[:, b, a, :], a_sb[:, j, 2 * a + b, :], ident[:], start=False, stop=True, is_transpose=True)
                     else:
                         nc.tensor.transpose(t_ps[:, b, a, :], src[:, 2 * a + b, :], ident[:])
             turned = t_ps[:].rearrange("p b a q -> p q b a")
@@ -130,65 +131,67 @@ def tile_attend_at_cfg_topk_kernel(tc, qT, k_words, k_scales, c_words, c_scales,
                 e2 = ring.tile([P, P, 2, 2], F32, name="e2")
                 nc.scalar.activation(e2[:], turned, ACT.Exp)
                 turned = e2[:]
-            nc.vector.tensor_tensor(y_bf[:, cols], turned, us_bc, ALU.mult)
+            y_bf[j] = placed.tile([P, P, 2, 2], BF16, name=f"y_bf{j}", offset=place, align_bytes=64)
+            nc.vector.tensor_tensor(y_bf[j][:], turned, us_bc, ALU.mult)
 
-        def weights_quant(j):
+        def weights_quant(j, place):
             cols = slice(j * P, (j + 1) * P)
-            nc.vector.quantize_mx(y_codes[:, cols].bitcast(FP8X4), y_scale[:, cols], y_bf[:, cols].rearrange("p q b a -> p (q b a)"))
+            y_codes[j] = placed.tile([P, P], U32, name=f"y_codes{j}", offset=place, align_bytes=64)
+            nc.vector.quantize_mx(y_codes[j][:].bitcast(FP8X4), y_scale[:, cols], y_bf[j][:].rearrange("p q b a -> p (q b a)"))
 
-        def values_front(e):
+        def values_front(e, dst):
             v_g = ring.tile([P, 2, P, 2], BF16, name="v_g")
             nc.vector.tensor_copy(v_g[:].rearrange("p b m a -> p m a b"), v_win[e][:].indirect(offsets[:]))
             words = v_g[:].rearrange("p b m a -> p (b m a)").bitcast(F32)
-            v_ps = psum.tile([P, 2, P], F32, name="v_ps", tag="vt")
+            v_ps = psum.tile([P, 2, P], F32, name="v_ps", tag="vt", bufs=2)
             for b in range(2):
                 nc.tensor.transpose(v_ps[:, b, :], words[:, b * P : (b + 1) * P], ident[:])
-            v_bf = ring.tile([P, 4 * P], BF16, name="v_bf", align_bytes=64)
-            nc.scalar.copy(v_bf[:].bitcast(F32).rearrange("p (e b) -> p e b", b=2), v_ps[:].rearrange("p b e -> p e b"))
-            return v_bf
+            nc.scalar.copy(dst.bitcast(F32).rearrange("p (e b) -> p e b", b=2), v_ps[:].rearrange("p b e -> p e b"))
 
-        def values_quant(e, v_bf):
-            cols = slice(e * P, (e + 1) * P)
-            nc.vector.quantize_mx(v_codes[:, cols].bitcast(FP8X4), v_scale[:, cols], v_bf[:])
+        def values_quant(e0, src, place):
+            width = src.shape[1] // 4
+            v_codes[e0] = placed.tile([P, width], U32, name=f"v_codes{e0}", offset=place, align_bytes=64)
+            nc.vector.quantize_mx(v_codes[e0][:].bitcast(FP8X4), v_scale[:, e0 * P : e0 * P + width], src)
 
         out_rows = out[0].rearrange("(j p) e -> p j e", p=P)
 
-        def product(e0, width, groups):
+        def product(e0, groups, engines):
+            width = v_codes[e0].shape[1]
             cols = slice(e0 * P, e0 * P + width)
             o_sb = held.tile([P, QB, width], F32, name=f"o_sb{e0}")
-            for g, js in enumerate(groups):
-                o_ps = psum.tile([P, len(js), width], F32, name="o_ps", tag="wide", bufs=5)
+            for js, engine in zip(groups, engines):
+                o_ps = psum.tile([P, len(js), width], F32, name="o_ps", tag="wide", bufs=4)
                 for i, j in enumerate(js):
-                    qc = slice(j * P, (j + 1) * P)
-                    nc.tensor.matmul_mx(o_ps[:, i, :], lhsT=y_codes[:, qc].bitcast(FP8X4), lhsT_scale=y_scale[:, qc],
-                                        rhs=v_codes[:, cols].bitcast(FP8X4), rhs_scale=v_scale[:, cols], start=True, stop=True)
+                    nc.tensor.matmul_mx(o_ps[:, i, :], lhsT=y_codes[j][:].bitcast(FP8X4), lhsT_scale=y_scale[:, j * P : (j + 1) * P],
+                                        rhs=v_codes[e0][:].bitcast(FP8X4), rhs_scale=v_scale[:, cols], start=True, stop=True)
                 dst = o_sb[:, js[0] : js[-1] + 1, :]
-                if g % 2 == 0:
+                if engine == "scalar":
                     nc.scalar.copy(dst, o_ps[:])
                 else:
                     nc.vector.tensor_copy(dst, o_ps[:])
             nc.sync.dma_start(out_rows[:, :, cols], o_sb[:])
 
-        f0 = weights_front(0)
-        f1 = weights_front(1)
-        weights_back(0, f0)
-        vb0 = values_front(0)
-        f2 = weights_front(2)
-        weights_back(1, f1)
-        weights_quant(0)
-        f3 = weights_front(3)
-        weights_back(2, f2)
-        values_quant(0, vb0)
-        weights_quant(1)
-        vb1 = values_front(1)
-        weights_back(3, f3)
-        weights_quant(2)
-        values_quant(1, vb1)
-        weights_quant(3)
-        vb2 = values_front(2)
-        product(0, 256, [(0, 1), (2, 3)])
-        values_quant(2, vb2)
-        vb3 = values_front(3)
-        product(2, 128, [(0, 1, 2, 3)])
-        values_quant(3, vb3)
-        product(3, 128, [(0, 1), (2, 3)])
+        v_bf = held.tile([P, 4 * DV], BF16, name="v_bf", align_bytes=64)
+        free = EB * W + 2048
+        values_front(0, v_bf[:, 0:512])
+        values_front(1, v_bf[:, 512:1024])
+        weights_front(0)
+        values_front(2, v_bf[:, 1024:1536])
+        weights_front(2)
+        values_front(3, v_bf[:, 1536:2048])
+        weights_front(1)
+        weights_back(0, free + 0)
+        weights_back(1, 1 * W + 0)
+        values_quant(0, v_bf[:, 0:1024], 2 * W + 0)
+        weights_quant(0, 1 * W + 1024)
+        weights_quant(1, 0 * W + 0)
+        weights_front(3)
+        weights_back(2, 1 * W + 2048)
+        values_quant(2, v_bf[:, 1024:1536], 3 * W + 0)
+        values_quant(3, v_bf[:, 1536:2048], 2 * W + 1024)
+        weights_back(3, 2 * W + 2048)
+        weights_quant(3, 2 * W + 3072)
+        weights_quant(2, 2 * W + 4096)
+        product(0, [(0, 1), (2, 3)], ["scalar","scalar"])
+        product(2, [(0, 1), (2, 3)], ["scalar","scalar"])
+        product(3, [(0, 1), (2, 3)], ["vector","scalar"])

@@ -15,183 +15,215 @@ ALU = mybir.AluOpType
 
 P = 128
 N, T, D, NQ, DV = 512, 2048, 512, 512, 512
-QB = NQ // P
-EB = DV // P
+BLOCKS = 4
 FLOPS = 2 * 2 * N * D * NQ + 2 * N * NQ * DV
-RB = (1, 2, 3,)
-W = 4 * T
-Q_SPLIT = 384
+
+WINDOW_BYTES = 4 * T
+GUEST_BYTES = 1024
+BANK_BYTES = 2048
+Q_SCALAR_END = 384
+VECTOR_SUMMED = (0, 1)
 
 
 def tile_attend_at_cfg_topk_kernel(tc, qT, k_words, k_scales, c_words, c_scales, vT, ls, us, offs, out):
     nc = tc.nc
     with ExitStack() as ctx:
         held = ctx.enter_context(tc.tile_pool(name="held", bufs=1))
-        placed = ctx.enter_context(tc.tile_pool(name="placed", bufs=1))
-        ring = ctx.enter_context(tc.tile_pool(name="ring", bufs=4))
+        reused = ctx.enter_context(tc.tile_pool(name="reused", bufs=1))
         psum = ctx.enter_context(tc.psum_pool(name="psum", bufs=1))
+
+        def bank(number, shape, name):
+            return psum.tile(shape, F32, name=name, offset=number * BANK_BYTES)
+
+        def guest(window, place, shape, dtype, name):
+            return reused.tile(shape, dtype, name=name, offset=window * WINDOW_BYTES + place * GUEST_BYTES, align_bytes=64)
 
         offsets = held.tile([P, N // 16], U16, name="offsets")
         nc.sync.dma_start(offsets[:], offs)
         ident = held.tile([P, P], F32, name="ident")
-        ks_win = placed.tile([P, T // 4], I32, name="ks_win", offset=EB * W)
+        ks_win = reused.tile([P, T // 4], I32, name="ks_win", offset=BLOCKS * WINDOW_BYTES)
         cs_win = held.tile([P, T // 4], I32, name="cs_win")
         ls_rows = held.tile([P, P], F32, name="ls_rows")
-        warm_in = held.tile([P, 1], F32, name="warm_in")
-        warm_out = held.tile([P, 1], F32, name="warm_out")
-        nc.vector.memset(warm_in[:], 0.0)
         nc.vector.memset(ks_win[:], 0)
         nc.vector.memset(ls_rows[:], 0.0)
         nc.vector.memset(cs_win[:], 0)
         make_identity(nc, ident[:])
-        nc.scalar.activation(warm_out[:], warm_in[:], ACT.Exp)
+
+        def load_scales(win, scales):
+            for quad in range(4):
+                nc.sync.dma_start(win[32 * quad : 32 * quad + 4, :], scales[0, 4 * quad : 4 * quad + 4, :].bitcast(I32))
+
+        def load_words(packed, name):
+            win = held.tile([P, T], I32, name=name)
+            nc.sync.dma_start(win[:], packed[0].rearrange("p t r -> p (t r)").bitcast(I32))
+            return win
 
         q_raw = held.tile([P, 4, NQ], F32, name="q_raw")
         nc.sync.dma_start(q_raw[:], qT[0].rearrange("(p t) q -> p t q", t=4))
-        for quad in range(4):
-            nc.sync.dma_start(ks_win[32 * quad : 32 * quad + 4, :], k_scales[0, 4 * quad : 4 * quad + 4, :].bitcast(I32))
-        k_win = held.tile([P, T], I32, name="k_win")
-        nc.sync.dma_start(k_win[:], k_words[0].rearrange("p t r -> p (t r)").bitcast(I32))
-        nc.sync.dma_start(ls_rows[0:QB, :], ls[0, 0].rearrange("(j m) -> j m", j=QB))
-        for quad in range(4):
-            nc.sync.dma_start(cs_win[32 * quad : 32 * quad + 4, :], c_scales[0, 4 * quad : 4 * quad + 4, :].bitcast(I32))
-        c_win = held.tile([P, T], I32, name="c_win")
-        nc.sync.dma_start(c_win[:], c_words[0].rearrange("p t r -> p (t r)").bitcast(I32))
+        load_scales(ks_win, k_scales)
+        k_win = load_words(k_words, "k_win")
+        nc.sync.dma_start(ls_rows[0:BLOCKS, :], ls[0, 0].rearrange("(j m) -> j m", j=BLOCKS))
+        load_scales(cs_win, c_scales)
+        c_win = load_words(c_words, "c_win")
         us_sb = held.tile([P, 4], F32, name="us_sb")
-        v_win = []
-        for b in range(EB):
-            v_win.append(placed.tile([P, T], F32, name=f"v_win{b}", offset=b * W))
-            nc.sync.dma_start(v_win[b][:], vT[b * P : (b + 1) * P, :])
-            if b == 0:
-                nc.sync.dma_start(us_sb[:], us[0].rearrange("(p t) o -> p (t o)", t=4))
+        v_win = [reused.tile([P, T], F32, name=f"v_win{e}", offset=e * WINDOW_BYTES) for e in range(BLOCKS)]
+        nc.sync.dma_start(v_win[0][:], vT[0:P, :])
+        nc.sync.dma_start(us_sb[:], us[0].rearrange("(p s) o -> p (s o)", s=4))
+        for e in range(1, BLOCKS):
+            nc.sync.dma_start(v_win[e][:], vT[e * P : (e + 1) * P, :])
 
+        def gather(win, dtype, name):
+            picked = held.tile([P, N], dtype, name=name, align_bytes=64)
+            nc.vector.tensor_copy(picked[:], win[:].bitcast(dtype).indirect(offsets[:]))
+            return picked
+
+        half = NQ // 2
         q_bf = held.tile([P, NQ, 4], BF16, name="q_bf", align_bytes=64)
-        q_scale = held.tile([P, NQ], U8, name="q_scale", align_bytes=64)
         q_turned = q_raw[:].rearrange("p t q -> p q t")
-        nc.scalar.copy(q_bf[:, 0:256, :], q_turned[:, 0:256, :])
-        nc.scalar.copy(q_bf[:, 256:Q_SPLIT, :], q_turned[:, 256:Q_SPLIT, :])
-        nc.vector.tensor_copy(q_bf[:, Q_SPLIT:NQ, :], q_turned[:, Q_SPLIT:NQ, :])
-        ks_g = held.tile([P, N], U8, name="ks_g", align_bytes=64)
-        nc.vector.tensor_copy(ks_g[:], ks_win[:].bitcast(U8).indirect(offsets[:]))
-        q_codes = placed.tile([P, NQ], U32, name="q_codes", offset=EB * W, align_bytes=64)
-        for h in range(2):
-            cols = slice(h * 256, (h + 1) * 256)
+        nc.scalar.copy(q_bf[:, 0:half, :], q_turned[:, 0:half, :])
+        nc.scalar.copy(q_bf[:, half:Q_SCALAR_END, :], q_turned[:, half:Q_SCALAR_END, :])
+        nc.vector.tensor_copy(q_bf[:, Q_SCALAR_END:NQ, :], q_turned[:, Q_SCALAR_END:NQ, :])
+        k_scale = gather(ks_win, U8, "k_scale")
+        q_codes = reused.tile([P, NQ], U32, name="q_codes", offset=BLOCKS * WINDOW_BYTES, align_bytes=64)
+        q_scale = held.tile([P, NQ], U8, name="q_scale", align_bytes=64)
+        for cols in (slice(0, half), slice(half, NQ)):
             nc.vector.quantize_mx(q_codes[:, cols].bitcast(FP8X4), q_scale[:, cols], q_bf[:, cols, :].rearrange("p q t -> p (q t)"))
 
-        def scores(words, scale, j, tag, bufs):
-            ps = psum.tile([P, N], F32, name="score_ps", tag=tag, bufs=bufs)
+        def scores(codes, scale, j, bank_number, name):
+            ps = bank(bank_number, [P, N], name)
             cols = slice(j * P, (j + 1) * P)
             nc.tensor.matmul_mx(ps[:], lhsT=q_codes[:, cols].bitcast(FP8X4), lhsT_scale=q_scale[:, cols],
-                                rhs=words[:].bitcast(FP8X4), rhs_scale=scale[:], start=True, stop=True)
-            return ps[:].rearrange("p (m t) -> p t m", t=4)
+                                rhs=codes[:].bitcast(FP8X4), rhs_scale=scale[:], start=True, stop=True)
+            return ps[:].rearrange("q (p s) -> q s p", s=4)
 
-        k_g = held.tile([P, N], U32, name="k_g", align_bytes=64)
-        nc.vector.tensor_copy(k_g[:], k_win[:].bitcast(U32).indirect(offsets[:]))
-        a_sb = held.tile([P, QB, 4, P], F32, name="a_sb")
-        for j in range(QB):
-            nc.scalar.mul(a_sb[:, j], scores(k_g, ks_g, j, "vt" if j == 0 else "wide", 2 if j == 0 else 4), 1.5)
-        ls_ps = psum.tile([P, 2, P], F32, name="ls_ps", tag="vt", bufs=2)
-        nc.tensor.transpose(ls_ps[:, 0, :], ls_rows[:], ident[:])
-        neg_ls = held.tile([P, QB], F32, name="neg_ls")
-        nc.scalar.mul(neg_ls[:], ls_ps[:, 0, 0:QB], -1.0)
-        cs_g = held.tile([P, N], U8, name="cs_g", align_bytes=64)
-        nc.vector.tensor_copy(cs_g[:], cs_win[:].bitcast(U8).indirect(offsets[:]))
-        c_g = held.tile([P, N], U32, name="c_g", align_bytes=64)
-        nc.vector.tensor_copy(c_g[:], c_win[:].bitcast(U32).indirect(offsets[:]))
+        k_codes = gather(k_win, U32, "k_codes")
+        neg_ls = held.tile([P, BLOCKS], F32, name="neg_ls")
+        first = []
+        for j in range(BLOCKS):
+            first.append(held.tile([P, 4, P], F32, name=f"first{j}"))
+            nc.scalar.mul(first[j][:], scores(k_codes, k_scale, j, j, f"a{j}"), 1.5)
+            if j == 0:
+                ls_ps = bank(0, [P, P], "ls_ps")
+                nc.tensor.transpose(ls_ps[:], ls_rows[:], ident[:])
+                nc.scalar.mul(neg_ls[:], ls_ps[:, 0:BLOCKS], -1.0)
+        c_scale = gather(cs_win, U8, "c_scale")
+        c_codes = gather(c_win, U32, "c_codes")
 
-        y_bf, y_codes, v_bf, v_codes, front = {}, {}, {}, {}, {}
         y_scale = held.tile([P, NQ], U8, name="y_scale", align_bytes=64)
-        us_bc = us_sb[:].rearrange("p (a b) -> p b a", a=2).unsqueeze(1).to_broadcast([P, P, 2, 2])
         v_scale = held.tile([P, DV], U8, name="v_scale", align_bytes=64)
+        v_bf = held.tile([P, 4 * DV], BF16, name="v_bf", align_bytes=64)
+        us_places = us_sb[:].rearrange("p (a b) -> p b a", a=2).unsqueeze(1).to_broadcast([P, P, 2, 2])
+        to_turn, exps, y_bf, y_codes, v_picked, v_codes = {}, {}, {}, {}, {}, {}
 
-        def weights_front(j):
-            z_ps = scores(c_g, cs_g, j, "wide", 4)
-            s_sb = ring.tile([P, 4, P], F32, name="s_sb")
-            if j in RB:
-                nc.scalar.activation(s_sb[:], z_ps, ACT.Identity, bias=neg_ls[:, j : j + 1], scale=-0.5)
-                front[j] = s_sb
-                return
-            nc.vector.scalar_tensor_tensor(s_sb[:], z_ps, -0.5, a_sb[:, j], ALU.mult, ALU.add)
-            e_sb = ring.tile([P, 4, P], F32, name="e_sb")
-            nc.scalar.activation(e_sb[:], s_sb[:], ACT.Exp, bias=neg_ls[:, j : j + 1])
-            front[j] = e_sb
+        def second_scores(j, bank_number):
+            z_ps = scores(c_codes, c_scale, j, bank_number, f"z{j}")
+            second = held.tile([P, 4, P], F32, name=f"second{j}")
+            if j in VECTOR_SUMMED:
+                nc.vector.scalar_tensor_tensor(second[:], z_ps, -0.5, first[j][:], ALU.mult, ALU.add)
+                exp_sb = held.tile([P, 4, P], F32, name=f"exp{j}")
+                nc.scalar.activation(exp_sb[:], second[:], ACT.Exp, bias=neg_ls[:, j : j + 1])
+                to_turn[j] = [exp_sb]
+            else:
+                nc.scalar.activation(second[:], z_ps, ACT.Identity, bias=neg_ls[:, j : j + 1], scale=-0.5)
+                to_turn[j] = [second, first[j]]
 
-        def weights_back(j, place):
-            src = front[j]
-            t_ps = psum.tile([P, 2, 2, P], F32, name="t_ps", tag="st", bufs=2)
+        def weights_turn(j, bank_number):
+            ps = bank(bank_number, [P, 2, 2, P], f"t{j}")
+            terms = to_turn[j]
             for b in range(2):
                 for a in range(2):
-                    if j in RB:
-                        nc.tensor.matmul(t_ps[:, b, a, :], src[:, 2 * a + b, :], ident[:], start=True, stop=False, is_transpose=True)
-                        nc.tensor.matmul(t_ps[:, b, a, :], a_sb[:, j, 2 * a + b, :], ident[:], start=False, stop=True, is_transpose=True)
-                    else:
-                        nc.tensor.transpose(t_ps[:, b, a, :], src[:, 2 * a + b, :], ident[:])
-            turned = t_ps[:].rearrange("p b a q -> p q b a")
-            if j in RB:
-                e2 = ring.tile([P, P, 2, 2], F32, name="e2")
-                nc.scalar.activation(e2[:], turned, ACT.Exp)
-                turned = e2[:]
-            y_bf[j] = placed.tile([P, P, 2, 2], BF16, name=f"y_bf{j}", offset=place, align_bytes=64)
-            nc.vector.tensor_tensor(y_bf[j][:], turned, us_bc, ALU.mult)
+                    for n, term in enumerate(terms):
+                        nc.tensor.matmul(ps[:, b, a, :], term[:, 2 * a + b, :], ident[:], start=n == 0,
+                                         stop=n == len(terms) - 1, is_transpose=True)
+            exps[j] = ps[:].rearrange("p b a q -> p q b a")
+            if j not in VECTOR_SUMMED:
+                exp_sb = held.tile([P, P, 2, 2], F32, name=f"exp{j}")
+                nc.scalar.activation(exp_sb[:], exps[j], ACT.Exp)
+                exps[j] = exp_sb[:]
 
-        def weights_quant(j, place):
-            cols = slice(j * P, (j + 1) * P)
-            y_codes[j] = placed.tile([P, P], U32, name=f"y_codes{j}", offset=place, align_bytes=64)
-            nc.vector.quantize_mx(y_codes[j][:].bitcast(FP8X4), y_scale[:, cols], y_bf[j][:].rearrange("p q b a -> p (q b a)"))
+        def weights_scale(j, window, place):
+            y_bf[j] = guest(window, place, [P, P, 2, 2], BF16, f"y_bf{j}")
+            nc.vector.tensor_tensor(y_bf[j][:], exps[j], us_places, ALU.mult)
 
-        def values_front(e, dst):
-            v_g = ring.tile([P, 2, P, 2], BF16, name="v_g")
-            nc.vector.tensor_copy(v_g[:].rearrange("p b m a -> p m a b"), v_win[e][:].indirect(offsets[:]))
-            words = v_g[:].rearrange("p b m a -> p (b m a)").bitcast(F32)
-            v_ps = psum.tile([P, 2, P], F32, name="v_ps", tag="vt", bufs=2)
+        def weights_quantise(j, codes):
+            y_codes[j] = codes
+            nc.vector.quantize_mx(codes[:].bitcast(FP8X4), y_scale[:, j * P : (j + 1) * P], y_bf[j][:].rearrange("p q b a -> p (q b a)"))
+
+        def values_gather(e):
+            v_picked[e] = held.tile([P, 2, P, 2], BF16, name=f"v_picked{e}")
+            nc.vector.tensor_copy(v_picked[e][:].rearrange("e b p a -> e p a b"), v_win[e][:].indirect(offsets[:]))
+
+        def values_turn(e, bank_number):
+            pairs = v_picked[e][:].rearrange("e b p a -> e (b p a)").bitcast(F32)
+            ps = bank(bank_number, [P, 2, P], f"v{e}")
             for b in range(2):
-                nc.tensor.transpose(v_ps[:, b, :], words[:, b * P : (b + 1) * P], ident[:])
-            nc.scalar.copy(dst.bitcast(F32).rearrange("p (e b) -> p e b", b=2), v_ps[:].rearrange("p b e -> p e b"))
+                nc.tensor.transpose(ps[:, b, :], pairs[:, b * P : (b + 1) * P], ident[:])
+            dst = v_bf[:, 4 * P * e : 4 * P * (e + 1)].bitcast(F32).rearrange("p (e b) -> p e b", b=2)
+            nc.scalar.copy(dst, ps[:].rearrange("p b e -> p e b"))
 
-        def values_quant(e0, src, place):
-            width = src.shape[1] // 4
-            v_codes[e0] = placed.tile([P, width], U32, name=f"v_codes{e0}", offset=place, align_bytes=64)
-            nc.vector.quantize_mx(v_codes[e0][:].bitcast(FP8X4), v_scale[:, e0 * P : e0 * P + width], src)
+        def values_quantise(e, codes):
+            v_codes[e] = codes
+            end = e * P + codes.shape[1]
+            nc.vector.quantize_mx(codes[:].bitcast(FP8X4), v_scale[:, e * P : end], v_bf[:, 4 * P * e : 4 * end])
 
-        out_rows = out[0].rearrange("(j p) e -> p j e", p=P)
+        def word_tile(width, name):
+            return held.tile([P, width], U32, name=name, align_bytes=64)
 
-        def product(e0, groups, engines):
-            width = v_codes[e0].shape[1]
-            cols = slice(e0 * P, e0 * P + width)
-            o_sb = held.tile([P, QB, width], F32, name=f"o_sb{e0}")
-            for js, engine in zip(groups, engines):
-                o_ps = psum.tile([P, len(js), width], F32, name="o_ps", tag="wide", bufs=4)
-                for i, j in enumerate(js):
-                    nc.tensor.matmul_mx(o_ps[:, i, :], lhsT=y_codes[j][:].bitcast(FP8X4), lhsT_scale=y_scale[:, j * P : (j + 1) * P],
-                                        rhs=v_codes[e0][:].bitcast(FP8X4), rhs_scale=v_scale[:, cols], start=True, stop=True)
-                dst = o_sb[:, js[0] : js[-1] + 1, :]
-                if engine == "scalar":
-                    nc.scalar.copy(dst, o_ps[:])
-                else:
-                    nc.vector.tensor_copy(dst, o_ps[:])
-            nc.sync.dma_start(out_rows[:, :, cols], o_sb[:])
+        out_rows = out[0].rearrange("(j m) e -> m j e", m=P)
 
-        v_bf = held.tile([P, 4 * DV], BF16, name="v_bf", align_bytes=64)
-        free = EB * W + 2048
-        values_front(0, v_bf[:, 0:512])
-        values_front(1, v_bf[:, 512:1024])
-        weights_front(0)
-        values_front(2, v_bf[:, 1024:1536])
-        weights_front(2)
-        values_front(3, v_bf[:, 1536:2048])
-        weights_front(1)
-        weights_back(0, free + 0)
-        weights_back(1, 1 * W + 0)
-        values_quant(0, v_bf[:, 0:1024], 2 * W + 0)
-        weights_quant(0, 1 * W + 1024)
-        weights_quant(1, 0 * W + 0)
-        weights_front(3)
-        weights_back(2, 1 * W + 2048)
-        values_quant(2, v_bf[:, 1024:1536], 3 * W + 0)
-        values_quant(3, v_bf[:, 1536:2048], 2 * W + 1024)
-        weights_back(3, 2 * W + 2048)
-        weights_quant(3, 2 * W + 3072)
-        weights_quant(2, 2 * W + 4096)
-        product(0, [(0, 1), (2, 3)], ["scalar","scalar"])
-        product(2, [(0, 1), (2, 3)], ["scalar","scalar"])
-        product(3, [(0, 1), (2, 3)], ["vector","scalar"])
+        def product(ps, js, es):
+            for n, j in enumerate(js):
+                for e in es:
+                    width = v_codes[e].shape[1]
+                    start = (e - es[0]) * P
+                    nc.tensor.matmul_mx(ps[:, n, start : start + width], lhsT=y_codes[j][:].bitcast(FP8X4),
+                                        lhsT_scale=y_scale[:, j * P : (j + 1) * P], rhs=v_codes[e][:].bitcast(FP8X4),
+                                        rhs_scale=v_scale[:, e * P : e * P + width], start=True, stop=True)
+
+        def product_and_store(js, es, bank_number):
+            width = sum(v_codes[e].shape[1] for e in es)
+            name = f"out{js[0]}{es[0]}"
+            staged = held.tile([P, len(js), width], F32, name=name)
+            ps = bank(bank_number, [P, len(js), width], name + "_ps")
+            product(ps, js, es)
+            nc.scalar.copy(staged[:], ps[:])
+            nc.sync.dma_start(out_rows[:, js[0] : js[-1] + 1, es[0] * P : es[0] * P + width], staged[:])
+
+        second_scores(0, 4)
+        second_scores(1, 5)
+        values_gather(0)
+        weights_turn(0, 6)
+        weights_turn(1, 7)
+        second_scores(2, 0)
+        second_scores(3, 1)
+        values_gather(1)
+        values_turn(0, 2)
+        weights_scale(0, 1, 0)
+        weights_turn(2, 3)
+        weights_scale(1, 1, 1)
+        values_turn(1, 4)
+        values_gather(2)
+        weights_turn(3, 5)
+        weights_scale(2, 2, 0)
+        weights_quantise(0, guest(2, 1, [P, P], U32, "y_codes0"))
+        values_turn(2, 0)
+        values_quantise(0, guest(2, 2, [P, 2 * P], U32, "v_codes0"))
+        weights_quantise(1, guest(2, 3, [P, P], U32, "y_codes1"))
+        weights_quantise(2, word_tile(P, "y_codes2"))
+        values_quantise(2, word_tile(P, "v_codes2"))
+        product_and_store([0, 1], [0], 1)
+        product_and_store([2], [0, 2], 2)
+        product_and_store([0, 1], [2], 6)
+        values_gather(3)
+        values_turn(3, 7)
+        weights_scale(3, 3, 0)
+        weights_quantise(3, word_tile(P, "y_codes3"))
+        values_quantise(3, word_tile(P, "v_codes3"))
+        product_and_store([3], [0, 2], 4)
+        last = held.tile([P, BLOCKS, P], F32, name="last")
+        low, high = bank(3, [P, 2, P], "low_ps"), bank(0, [P, 2, P], "high_ps")
+        product(low, [0, 1], [3])
+        nc.scalar.copy(last[:, 0:2, :], low[:])
+        product(high, [2, 3], [3])
+        nc.vector.tensor_copy(last[:, 2:4, :], high[:])
+        nc.sync.dma_start(out_rows[:, :, 3 * P : DV], last[:])

@@ -23,6 +23,7 @@ GUEST_BYTES = 1024
 BANK_BYTES = 2048
 Q_SCALAR_END = 384
 VECTOR_SUMMED = (0, 1)
+C_SCALE_ROW = 4
 
 
 def tile_attend_at_cfg_topk_kernel(tc, qT, k_words, k_scales, c_words, c_scales, vT, ls, us, offs, out):
@@ -49,9 +50,10 @@ def tile_attend_at_cfg_topk_kernel(tc, qT, k_words, k_scales, c_words, c_scales,
         nc.vector.memset(cs_win[:], 0)
         make_identity(nc, ident[:])
 
-        def load_scales(win, scales):
+        def load_scales(win, scales, first_row):
             for quad in range(4):
-                nc.sync.dma_start(win[32 * quad : 32 * quad + 4, :], scales[0, 4 * quad : 4 * quad + 4, :].bitcast(I32))
+                row = 32 * quad + first_row
+                nc.sync.dma_start(win[row : row + 4, :], scales[0, 4 * quad : 4 * quad + 4, :].bitcast(I32))
 
         def load_words(packed, name):
             win = held.tile([P, T], I32, name=name)
@@ -60,10 +62,10 @@ def tile_attend_at_cfg_topk_kernel(tc, qT, k_words, k_scales, c_words, c_scales,
 
         q_raw = held.tile([P, 4, NQ], F32, name="q_raw")
         nc.sync.dma_start(q_raw[:], qT[0].rearrange("(p t) q -> p t q", t=4))
-        load_scales(ks_win, k_scales)
+        load_scales(ks_win, k_scales, 0)
         k_win = load_words(k_words, "k_win")
         nc.sync.dma_start(ls_rows[0:BLOCKS, :], ls[0, 0].rearrange("(j m) -> j m", j=BLOCKS))
-        load_scales(cs_win, c_scales)
+        load_scales(cs_win, c_scales, C_SCALE_ROW)
         c_win = load_words(c_words, "c_win")
         us_sb = held.tile([P, 4], F32, name="us_sb")
         v_win = [reused.tile([P, T], F32, name=f"v_win{e}", offset=e * WINDOW_BYTES) for e in range(BLOCKS)]
@@ -93,7 +95,7 @@ def tile_attend_at_cfg_topk_kernel(tc, qT, k_words, k_scales, c_words, c_scales,
             ps = bank(bank_number, [P, N], name)
             cols = slice(j * P, (j + 1) * P)
             nc.tensor.matmul_mx(ps[:], lhsT=q_codes[:, cols].bitcast(FP8X4), lhsT_scale=q_scale[:, cols],
-                                rhs=codes[:].bitcast(FP8X4), rhs_scale=scale[:], start=True, stop=True)
+                                rhs=codes[:].bitcast(FP8X4), rhs_scale=scale, start=True, stop=True)
             return ps[:].rearrange("q (p s) -> q s p", s=4)
 
         k_codes = gather(k_win, U32, "k_codes")
@@ -101,7 +103,7 @@ def tile_attend_at_cfg_topk_kernel(tc, qT, k_words, k_scales, c_words, c_scales,
         first = []
         for j in range(BLOCKS):
             first.append(held.tile([P, 4, P], F32, name=f"first{j}"))
-            nc.scalar.mul(first[j][:], scores(k_codes, k_scale, j, j, f"a{j}"), 1.5)
+            nc.scalar.mul(first[j][:], scores(k_codes, k_scale[:], j, j, f"a{j}"), 1.5)
             if j == 0:
                 ls_ps = bank(0, [P, P], "ls_ps")
                 nc.tensor.transpose(ls_ps[:], ls_rows[:], ident[:])
@@ -112,11 +114,11 @@ def tile_attend_at_cfg_topk_kernel(tc, qT, k_words, k_scales, c_words, c_scales,
         y_scale = held.tile([P, NQ], U8, name="y_scale", align_bytes=64)
         v_scale = held.tile([P, DV], U8, name="v_scale", align_bytes=64)
         v_bf = held.tile([P, 4 * DV], BF16, name="v_bf", align_bytes=64)
-        us_places = us_sb[:].rearrange("p (a b) -> p b a", a=2).unsqueeze(1).to_broadcast([P, P, 2, 2])
+        us_places = us_sb[:].unsqueeze(1).to_broadcast([P, P, 4])
         to_turn, exps, y_bf, y_codes, v_picked, v_codes = {}, {}, {}, {}, {}, {}
 
         def second_scores(j, bank_number):
-            z_ps = scores(c_codes, c_scale, j, bank_number, f"z{j}")
+            z_ps = scores(c_codes, c_scale[C_SCALE_ROW:P, :], j, bank_number, f"z{j}")
             second = held.tile([P, 4, P], F32, name=f"second{j}")
             if j in VECTOR_SUMMED:
                 nc.vector.scalar_tensor_tensor(second[:], z_ps, -0.5, first[j][:], ALU.mult, ALU.add)
@@ -128,36 +130,35 @@ def tile_attend_at_cfg_topk_kernel(tc, qT, k_words, k_scales, c_words, c_scales,
                 to_turn[j] = [second, first[j]]
 
         def weights_turn(j, bank_number):
-            ps = bank(bank_number, [P, 2, 2, P], f"t{j}")
+            ps = bank(bank_number, [P, 4, P], f"t{j}")
             terms = to_turn[j]
-            for b in range(2):
-                for a in range(2):
-                    for n, term in enumerate(terms):
-                        nc.tensor.matmul(ps[:, b, a, :], term[:, 2 * a + b, :], ident[:], start=n == 0,
-                                         stop=n == len(terms) - 1, is_transpose=True)
-            exps[j] = ps[:].rearrange("p b a q -> p q b a")
+            for s in range(4):
+                for n, term in enumerate(terms):
+                    nc.tensor.matmul(ps[:, s, :], term[:, s, :], ident[:], start=n == 0,
+                                     stop=n == len(terms) - 1, is_transpose=True)
+            exps[j] = ps[:].rearrange("p s q -> p q s")
             if j not in VECTOR_SUMMED:
-                exp_sb = held.tile([P, P, 2, 2], F32, name=f"exp{j}")
+                exp_sb = held.tile([P, P, 4], F32, name=f"exp{j}")
                 nc.scalar.activation(exp_sb[:], exps[j], ACT.Exp)
                 exps[j] = exp_sb[:]
 
         def weights_scale(j, window, place):
-            y_bf[j] = guest(window, place, [P, P, 2, 2], BF16, f"y_bf{j}")
+            y_bf[j] = guest(window, place, [P, P, 4], BF16, f"y_bf{j}")
             nc.vector.tensor_tensor(y_bf[j][:], exps[j], us_places, ALU.mult)
 
         def weights_quantise(j, codes):
             y_codes[j] = codes
-            nc.vector.quantize_mx(codes[:].bitcast(FP8X4), y_scale[:, j * P : (j + 1) * P], y_bf[j][:].rearrange("p q b a -> p (q b a)"))
+            nc.vector.quantize_mx(codes[:].bitcast(FP8X4), y_scale[:, j * P : (j + 1) * P], y_bf[j][:].rearrange("p q s -> p (q s)"))
 
         def values_gather(e):
-            v_picked[e] = held.tile([P, 2, P, 2], BF16, name=f"v_picked{e}")
-            nc.vector.tensor_copy(v_picked[e][:].rearrange("e b p a -> e p a b"), v_win[e][:].indirect(offsets[:]))
+            v_picked[e] = held.tile([P, N], BF16, name=f"v_picked{e}")
+            nc.vector.tensor_copy(v_picked[e][:], v_win[e][:].indirect(offsets[:]))
 
         def values_turn(e, bank_number):
-            pairs = v_picked[e][:].rearrange("e b p a -> e (b p a)").bitcast(F32)
+            pairs = v_picked[e][:].bitcast(F32)
             ps = bank(bank_number, [P, 2, P], f"v{e}")
             for b in range(2):
-                nc.tensor.transpose(ps[:, b, :], pairs[:, b * P : (b + 1) * P], ident[:])
+                nc.tensor.transpose(ps[:, b, :], pairs[:, b : 2 * P : 2], ident[:])
             dst = v_bf[:, 4 * P * e : 4 * P * (e + 1)].bitcast(F32).rearrange("p (e b) -> p e b", b=2)
             nc.scalar.copy(dst, ps[:].rearrange("p b e -> p e b"))
 

@@ -19,10 +19,11 @@ BLOCKS = 4
 FLOPS = 2 * 2 * N * D * NQ + 2 * N * NQ * DV
 
 WINDOW_BYTES = 4 * T
+K_WINDOW, C_WINDOW = 6, 7
 GUEST_BYTES = 1024
 BANK_BYTES = 2048
 Q_SCALAR_END = 384
-VECTOR_SUMMED = (0, 1)
+VECTOR_SUMMED = (0,)
 C_SCALE_ROW = 4
 
 
@@ -55,18 +56,18 @@ def tile_attend_at_cfg_topk_kernel(tc, qT, k_words, k_scales, c_words, c_scales,
                 row = 32 * quad + first_row
                 nc.sync.dma_start(win[row : row + 4, :], scales[0, 4 * quad : 4 * quad + 4, :].bitcast(I32))
 
-        def load_words(packed, name):
-            win = held.tile([P, T], I32, name=name)
+        def load_words(packed, window, name):
+            win = reused.tile([P, T], I32, name=name, offset=window * WINDOW_BYTES)
             nc.sync.dma_start(win[:], packed[0].rearrange("p t r -> p (t r)").bitcast(I32))
             return win
 
         q_raw = held.tile([P, 4, NQ], F32, name="q_raw")
         nc.sync.dma_start(q_raw[:], qT[0].rearrange("(p t) q -> p t q", t=4))
         load_scales(ks_win, k_scales, 0)
-        k_win = load_words(k_words, "k_win")
         nc.sync.dma_start(ls_rows[0:BLOCKS, :], ls[0, 0].rearrange("(j m) -> j m", j=BLOCKS))
+        k_win = load_words(k_words, K_WINDOW, "k_win")
         load_scales(cs_win, c_scales, C_SCALE_ROW)
-        c_win = load_words(c_words, "c_win")
+        c_win = load_words(c_words, C_WINDOW, "c_win")
         us_sb = held.tile([P, 4], F32, name="us_sb")
         v_win = [reused.tile([P, T], F32, name=f"v_win{e}", offset=e * WINDOW_BYTES) for e in range(BLOCKS)]
         nc.sync.dma_start(v_win[0][:], vT[0:P, :])
@@ -74,59 +75,56 @@ def tile_attend_at_cfg_topk_kernel(tc, qT, k_words, k_scales, c_words, c_scales,
         for e in range(1, BLOCKS):
             nc.sync.dma_start(v_win[e][:], vT[e * P : (e + 1) * P, :])
 
-        def gather(win, dtype, name):
-            picked = held.tile([P, N], dtype, name=name, align_bytes=64)
+        def gather(win, dtype, picked):
             nc.vector.tensor_copy(picked[:], win[:].bitcast(dtype).indirect(offsets[:]))
             return picked
 
-        half = NQ // 2
         q_bf = held.tile([P, NQ, 4], BF16, name="q_bf", align_bytes=64)
         q_turned = q_raw[:].rearrange("p t q -> p q t")
-        nc.scalar.copy(q_bf[:, 0:half, :], q_turned[:, 0:half, :])
-        nc.scalar.copy(q_bf[:, half:Q_SCALAR_END, :], q_turned[:, half:Q_SCALAR_END, :])
+        nc.scalar.copy(q_bf[:, 0:Q_SCALAR_END, :], q_turned[:, 0:Q_SCALAR_END, :])
         nc.vector.tensor_copy(q_bf[:, Q_SCALAR_END:NQ, :], q_turned[:, Q_SCALAR_END:NQ, :])
-        k_scale = gather(ks_win, U8, "k_scale")
-        q_codes = reused.tile([P, NQ], U32, name="q_codes", offset=BLOCKS * WINDOW_BYTES, align_bytes=64)
+        k_scale = gather(ks_win, U8, held.tile([P, N], U8, name="k_scale", align_bytes=64))
+        q_words = guest(BLOCKS, 0, [P, NQ], U32, "q_words")
         q_scale = held.tile([P, NQ], U8, name="q_scale", align_bytes=64)
-        for cols in (slice(0, half), slice(half, NQ)):
-            nc.vector.quantize_mx(q_codes[:, cols].bitcast(FP8X4), q_scale[:, cols], q_bf[:, cols, :].rearrange("p q t -> p (q t)"))
+        nc.vector.quantize_mx(q_words[:].bitcast(FP8X4), q_scale[:], q_bf[:].rearrange("p q t -> p (q t)"))
+        k_codes = gather(k_win, U32, held.tile([P, N], U32, name="k_codes", align_bytes=64))
 
         def scores(codes, scale, j, bank_number, name):
             ps = bank(bank_number, [P, N], name)
             cols = slice(j * P, (j + 1) * P)
-            nc.tensor.matmul_mx(ps[:], lhsT=q_codes[:, cols].bitcast(FP8X4), lhsT_scale=q_scale[:, cols],
+            nc.tensor.matmul_mx(ps[:], lhsT=q_words[:, cols].bitcast(FP8X4), lhsT_scale=q_scale[:, cols],
                                 rhs=codes[:].bitcast(FP8X4), rhs_scale=scale, start=True, stop=True)
             return ps[:].rearrange("q (p s) -> q s p", s=4)
 
-        k_codes = gather(k_win, U32, "k_codes")
         neg_ls = held.tile([P, BLOCKS], F32, name="neg_ls")
+        ls_ps = bank(4, [P, P], "ls_ps")
+        nc.tensor.transpose(ls_ps[:], ls_rows[:], ident[:])
+        nc.scalar.mul(neg_ls[:], ls_ps[:, 0:BLOCKS], -1.0)
         first = []
         for j in range(BLOCKS):
             first.append(held.tile([P, 4, P], F32, name=f"first{j}"))
             nc.scalar.mul(first[j][:], scores(k_codes, k_scale[:], j, j, f"a{j}"), 1.5)
-            if j == 0:
-                ls_ps = bank(0, [P, P], "ls_ps")
-                nc.tensor.transpose(ls_ps[:], ls_rows[:], ident[:])
-                nc.scalar.mul(neg_ls[:], ls_ps[:, 0:BLOCKS], -1.0)
-        c_scale = gather(cs_win, U8, "c_scale")
-        c_codes = gather(c_win, U32, "c_codes")
+        c_scale = gather(cs_win, U8, guest(K_WINDOW, 0, [P, N], U8, "c_scale"))
+        c_codes = gather(c_win, U32, held.tile([P, N], U32, name="c_codes", align_bytes=64))
 
         y_scale = held.tile([P, NQ], U8, name="y_scale", align_bytes=64)
         v_scale = held.tile([P, DV], U8, name="v_scale", align_bytes=64)
-        v_bf = held.tile([P, 4 * DV], BF16, name="v_bf", align_bytes=64)
+        v_bf = {}
         us_places = us_sb[:].unsqueeze(1).to_broadcast([P, P, 4])
         to_turn, exps, y_bf, y_codes, v_picked, v_codes = {}, {}, {}, {}, {}, {}
 
-        def second_scores(j, bank_number):
+        def second_scores(j, bank_number, second, by_vector):
             z_ps = scores(c_codes, c_scale[C_SCALE_ROW:P, :], j, bank_number, f"z{j}")
-            second = held.tile([P, 4, P], F32, name=f"second{j}")
             if j in VECTOR_SUMMED:
                 nc.vector.scalar_tensor_tensor(second[:], z_ps, -0.5, first[j][:], ALU.mult, ALU.add)
                 exp_sb = held.tile([P, 4, P], F32, name=f"exp{j}")
                 nc.scalar.activation(exp_sb[:], second[:], ACT.Exp, bias=neg_ls[:, j : j + 1])
                 to_turn[j] = [exp_sb]
             else:
-                nc.scalar.activation(second[:], z_ps, ACT.Identity, bias=neg_ls[:, j : j + 1], scale=-0.5)
+                if by_vector:
+                    nc.vector.tensor_scalar(second[:], z_ps, -0.5, neg_ls[:, j : j + 1], ALU.mult, ALU.add)
+                else:
+                    nc.scalar.activation(second[:], z_ps, ACT.Identity, bias=neg_ls[:, j : j + 1], scale=-0.5)
                 to_turn[j] = [second, first[j]]
 
         def weights_turn(j, bank_number):
@@ -142,9 +140,9 @@ def tile_attend_at_cfg_topk_kernel(tc, qT, k_words, k_scales, c_words, c_scales,
                 nc.scalar.activation(exp_sb[:], exps[j], ACT.Exp)
                 exps[j] = exp_sb[:]
 
-        def weights_scale(j, window, place):
+        def weights_scale(j, window, place, engine):
             y_bf[j] = guest(window, place, [P, P, 4], BF16, f"y_bf{j}")
-            nc.vector.tensor_tensor(y_bf[j][:], exps[j], us_places, ALU.mult)
+            engine.tensor_tensor(y_bf[j][:], exps[j], us_places, ALU.mult)
 
         def weights_quantise(j, codes):
             y_codes[j] = codes
@@ -154,18 +152,22 @@ def tile_attend_at_cfg_topk_kernel(tc, qT, k_words, k_scales, c_words, c_scales,
             v_picked[e] = held.tile([P, N], BF16, name=f"v_picked{e}")
             nc.vector.tensor_copy(v_picked[e][:], v_win[e][:].indirect(offsets[:]))
 
-        def values_turn(e, bank_number):
+        def values_turn(e, bank_number, window, place):
             pairs = v_picked[e][:].bitcast(F32)
             ps = bank(bank_number, [P, 2, P], f"v{e}")
             for b in range(2):
                 nc.tensor.transpose(ps[:, b, :], pairs[:, b : 2 * P : 2], ident[:])
-            dst = v_bf[:, 4 * P * e : 4 * P * (e + 1)].bitcast(F32).rearrange("p (e b) -> p e b", b=2)
+            v_bf[e] = guest(window, place, [P, 4 * P], BF16, f"v_bf{e}")
+            dst = v_bf[e][:].bitcast(F32).rearrange("p (e b) -> p e b", b=2)
             nc.scalar.copy(dst, ps[:].rearrange("p b e -> p e b"))
 
         def values_quantise(e, codes):
             v_codes[e] = codes
             end = e * P + codes.shape[1]
-            nc.vector.quantize_mx(codes[:].bitcast(FP8X4), v_scale[:, e * P : end], v_bf[:, 4 * P * e : 4 * end])
+            nc.vector.quantize_mx(codes[:].bitcast(FP8X4), v_scale[:, e * P : end], v_bf[e][:])
+
+        def plain(name):
+            return held.tile([P, 4, P], F32, name=name)
 
         def word_tile(width, name):
             return held.tile([P, width], U32, name=name, align_bytes=64)
@@ -190,39 +192,41 @@ def tile_attend_at_cfg_topk_kernel(tc, qT, k_words, k_scales, c_words, c_scales,
             nc.scalar.copy(staged[:], ps[:])
             nc.sync.dma_start(out_rows[:, js[0] : js[-1] + 1, es[0] * P : es[0] * P + width], staged[:])
 
-        second_scores(0, 4)
-        second_scores(1, 5)
+        SPARE = BLOCKS + 1
+        second_scores(0, 4, plain("second0"), True)
         values_gather(0)
-        weights_turn(0, 6)
-        weights_turn(1, 7)
-        second_scores(2, 0)
-        second_scores(3, 1)
+        second_scores(1, 5, plain("second1"), False)
+        weights_turn(1, 1)
+        weights_turn(0, 0)
+        second_scores(2, 6, plain("second2"), False)
+        weights_scale(1, SPARE, 4, nc.gpsimd)
+        second_scores(3, 7, plain("second3"), False)
+        values_turn(0, 4, SPARE, 0)
         values_gather(1)
-        values_turn(0, 2)
-        weights_scale(0, 1, 0)
-        weights_turn(2, 3)
-        weights_scale(1, 1, 1)
-        values_turn(1, 4)
+        weights_turn(2, 2)
+        weights_scale(0, 1, 0, nc.vector)
+        values_quantise(0, guest(1, 1, [P, P], U32, "v_codes0"))
+        values_turn(1, 5, SPARE, 1)
+        weights_turn(3, 3)
+        weights_scale(2, SPARE, 0, nc.gpsimd)
         values_gather(2)
-        weights_turn(3, 5)
-        weights_scale(2, 2, 0)
-        weights_quantise(0, guest(2, 1, [P, P], U32, "y_codes0"))
-        values_turn(2, 0)
-        values_quantise(0, guest(2, 2, [P, 2 * P], U32, "v_codes0"))
-        weights_quantise(1, guest(2, 3, [P, P], U32, "y_codes1"))
-        weights_quantise(2, word_tile(P, "y_codes2"))
-        values_quantise(2, word_tile(P, "v_codes2"))
-        product_and_store([0, 1], [0], 1)
-        product_and_store([2], [0, 2], 2)
-        product_and_store([0, 1], [2], 6)
+        values_turn(2, 6, SPARE, 2)
+        weights_quantise(0, guest(2, 3, [P, P], U32, "y_codes0"))
+        weights_quantise(1, guest(2, 0, [P, P], U32, "y_codes1"))
+        values_quantise(1, guest(2, 1, [P, P], U32, "v_codes1"))
+        weights_quantise(2, guest(2, 2, [P, P], U32, "y_codes2"))
+        weights_scale(3, SPARE, 0, nc.gpsimd)
+        product_and_store([0, 1], [0, 1], 0)
+        product_and_store([2], [0, 1], 1)
         values_gather(3)
-        values_turn(3, 7)
-        weights_scale(3, 3, 0)
-        weights_quantise(3, word_tile(P, "y_codes3"))
+        values_turn(3, 7, SPARE, 3)
+        values_quantise(2, guest(3, 1, [P, P], U32, "v_codes2"))
+        weights_quantise(3, guest(3, 0, [P, P], U32, "y_codes3"))
         values_quantise(3, word_tile(P, "v_codes3"))
-        product_and_store([3], [0, 2], 4)
+        product_and_store([0, 1, 2], [2], 2)
+        product_and_store([3], [0, 1, 2], 3)
         last = held.tile([P, BLOCKS, P], F32, name="last")
-        low, high = bank(3, [P, 2, P], "low_ps"), bank(0, [P, 2, P], "high_ps")
+        low, high = bank(4, [P, 2, P], "low_ps"), bank(5, [P, 2, P], "high_ps")
         product(low, [0, 1], [3])
         nc.scalar.copy(last[:, 0:2, :], low[:])
         product(high, [2, 3], [3])

@@ -19,11 +19,10 @@ BLOCKS = 4
 FLOPS = 2 * 2 * N * D * NQ + 2 * N * NQ * DV
 
 WINDOW_BYTES = 4 * T
-K_WINDOW, C_WINDOW = 6, 7
+SPARE, K_WINDOW, C_WINDOW, Q_WINDOW = 5, 6, 7, 8
 GUEST_BYTES = 1024
 BANK_BYTES = 2048
-Q_SCALAR_END = 384
-VECTOR_SUMMED = (0,)
+APART = 1
 C_SCALE_ROW = 4
 
 
@@ -79,33 +78,55 @@ def tile_attend_at_cfg_topk_kernel(tc, qT, k_words, k_scales, c_words, c_scales,
             nc.vector.tensor_copy(picked[:], win[:].bitcast(dtype).indirect(offsets[:]))
             return picked
 
-        q_bf = held.tile([P, NQ, 4], BF16, name="q_bf", align_bytes=64)
+        half = NQ // 2
         q_turned = q_raw[:].rearrange("p t q -> p q t")
-        nc.scalar.copy(q_bf[:, 0:Q_SCALAR_END, :], q_turned[:, 0:Q_SCALAR_END, :])
-        nc.vector.tensor_copy(q_bf[:, Q_SCALAR_END:NQ, :], q_turned[:, Q_SCALAR_END:NQ, :])
+        q_words, q_scales = {}, {}
+
+        def queries_quantise(rounded, codes, names):
+            scale = held.tile([P, len(names) * P], U8, name=f"q_scale{names[0]}", align_bytes=64)
+            nc.vector.quantize_mx(codes[:].bitcast(FP8X4), scale[:], rounded)
+            for n, name in enumerate(names):
+                q_words[name], q_scales[name] = codes[:, n * P : (n + 1) * P], scale[:, n * P : (n + 1) * P]
+
+        low_bf = guest(Q_WINDOW, 0, [P, 4 * half], BF16, "low_bf")
+        low_times = held.tile([P, 4 * P], BF16, name="low_times", align_bytes=64)
+        high_bf = guest(Q_WINDOW, 0, [P, 2, 4 * half], BF16, "high_bf")
+        nc.scalar.copy(low_bf[:].rearrange("p (q t) -> p q t", t=4), q_turned[:, 0:half, :])
+        nc.scalar.mul(low_times[:], low_bf[:, 0 : 4 * P], -4.0)
         k_scale = gather(ks_win, U8, held.tile([P, N], U8, name="k_scale", align_bytes=64))
-        q_words = guest(BLOCKS, 0, [P, NQ], U32, "q_words")
-        q_scale = held.tile([P, NQ], U8, name="q_scale", align_bytes=64)
-        nc.vector.quantize_mx(q_words[:].bitcast(FP8X4), q_scale[:], q_bf[:].rearrange("p q t -> p (q t)"))
-        k_codes = gather(k_win, U32, held.tile([P, N], U32, name="k_codes", align_bytes=64))
-
-        def scores(codes, scale, j, bank_number, name):
-            ps = bank(bank_number, [P, N], name)
-            cols = slice(j * P, (j + 1) * P)
-            nc.tensor.matmul_mx(ps[:], lhsT=q_words[:, cols].bitcast(FP8X4), lhsT_scale=q_scale[:, cols],
-                                rhs=codes[:].bitcast(FP8X4), rhs_scale=scale, start=True, stop=True)
-            return ps[:].rearrange("q (p s) -> q s p", s=4)
-
+        queries_quantise(low_bf[:], guest(BLOCKS, 0, [P, half], U32, "q_low"), ["q0", "q1"])
+        queries_quantise(low_times[:], guest(BLOCKS, 1, [P, P], U32, "q_low_times"), ["m0"])
+        nc.scalar.copy(high_bf[:, 0, :].rearrange("p (q t) -> p q t", t=4), q_turned[:, half:NQ, :])
+        nc.scalar.mul(high_bf[:, 1, :], high_bf[:, 0, :], -4.0)
         neg_ls = held.tile([P, BLOCKS], F32, name="neg_ls")
         ls_ps = bank(4, [P, P], "ls_ps")
         nc.tensor.transpose(ls_ps[:], ls_rows[:], ident[:])
         nc.scalar.mul(neg_ls[:], ls_ps[:, 0:BLOCKS], -1.0)
-        first = []
-        for j in range(BLOCKS):
-            first.append(held.tile([P, 4, P], F32, name=f"first{j}"))
-            nc.scalar.mul(first[j][:], scores(k_codes, k_scale[:], j, j, f"a{j}"), 1.5)
+
+        def score_pass(ps, queries, keys, start, stop):
+            codes, scale = keys
+            nc.tensor.matmul_mx(ps[:], lhsT=q_words[queries].bitcast(FP8X4), lhsT_scale=q_scales[queries],
+                                rhs=codes[:].bitcast(FP8X4), rhs_scale=scale, start=start, stop=stop)
+
+        def by_place(ps):
+            return ps[:].rearrange("q (p s) -> q s p", s=4)
+
+        def plain(name):
+            return held.tile([P, 4, P], F32, name=name)
+
+        k_codes = gather(k_win, U32, held.tile([P, N], U32, name="k_codes", align_bytes=64))
+        k_keys = (k_codes, k_scale[:])
+        joint = {0: bank(0, [P, N], "joint0")}
+        score_pass(joint[0], "q0", k_keys, True, False)
+        score_pass(joint[0], "m0", k_keys, False, False)
+        a_ps = bank(1, [P, N], "a_apart")
+        score_pass(a_ps, "q1", k_keys, True, True)
+        first = plain("first")
+        nc.scalar.mul(first[:], by_place(a_ps), 1.5)
         c_scale = gather(cs_win, U8, guest(K_WINDOW, 0, [P, N], U8, "c_scale"))
         c_codes = gather(c_win, U32, held.tile([P, N], U32, name="c_codes", align_bytes=64))
+        c_keys = (c_codes, c_scale[C_SCALE_ROW:P, :])
+        queries_quantise(high_bf[:].rearrange("p a b -> p (a b)"), guest(C_WINDOW, 0, [P, NQ], U32, "q_high"), ["q2", "q3", "m2", "m3"])
 
         y_scale = held.tile([P, NQ], U8, name="y_scale", align_bytes=64)
         v_scale = held.tile([P, DV], U8, name="v_scale", align_bytes=64)
@@ -113,19 +134,23 @@ def tile_attend_at_cfg_topk_kernel(tc, qT, k_words, k_scales, c_words, c_scales,
         us_places = us_sb[:].unsqueeze(1).to_broadcast([P, P, 4])
         to_turn, exps, y_bf, y_codes, v_picked, v_codes = {}, {}, {}, {}, {}, {}
 
-        def second_scores(j, bank_number, second, by_vector):
-            z_ps = scores(c_codes, c_scale[C_SCALE_ROW:P, :], j, bank_number, f"z{j}")
-            if j in VECTOR_SUMMED:
-                nc.vector.scalar_tensor_tensor(second[:], z_ps, -0.5, first[j][:], ALU.mult, ALU.add)
-                exp_sb = held.tile([P, 4, P], F32, name=f"exp{j}")
-                nc.scalar.activation(exp_sb[:], second[:], ACT.Exp, bias=neg_ls[:, j : j + 1])
-                to_turn[j] = [exp_sb]
-            else:
-                if by_vector:
-                    nc.vector.tensor_scalar(second[:], z_ps, -0.5, neg_ls[:, j : j + 1], ALU.mult, ALU.add)
-                else:
-                    nc.scalar.activation(second[:], z_ps, ACT.Identity, bias=neg_ls[:, j : j + 1], scale=-0.5)
-                to_turn[j] = [second, first[j]]
+        def joint_open(j, bank_number):
+            joint[j] = bank(bank_number, [P, N], f"joint{j}")
+            score_pass(joint[j], f"q{j}", k_keys, True, False)
+            score_pass(joint[j], f"m{j}", k_keys, False, False)
+
+        def joint_close(j):
+            score_pass(joint[j], f"q{j}", c_keys, False, True)
+            exp_sb = plain(f"exp{j}")
+            nc.scalar.activation(exp_sb[:], by_place(joint[j]), ACT.Exp, bias=neg_ls[:, j : j + 1], scale=-0.5)
+            to_turn[j] = [exp_sb]
+
+        def apart_close(bank_number):
+            z_ps = bank(bank_number, [P, N], "z_apart")
+            score_pass(z_ps, f"q{APART}", c_keys, True, True)
+            second = plain("second")
+            nc.scalar.activation(second[:], by_place(z_ps), ACT.Identity, bias=neg_ls[:, APART : APART + 1], scale=-0.5)
+            to_turn[APART] = [second, first]
 
         def weights_turn(j, bank_number):
             ps = bank(bank_number, [P, 4, P], f"t{j}")
@@ -135,7 +160,7 @@ def tile_attend_at_cfg_topk_kernel(tc, qT, k_words, k_scales, c_words, c_scales,
                     nc.tensor.matmul(ps[:, s, :], term[:, s, :], ident[:], start=n == 0,
                                      stop=n == len(terms) - 1, is_transpose=True)
             exps[j] = ps[:].rearrange("p s q -> p q s")
-            if j not in VECTOR_SUMMED:
+            if j == APART:
                 exp_sb = held.tile([P, P, 4], F32, name=f"exp{j}")
                 nc.scalar.activation(exp_sb[:], exps[j], ACT.Exp)
                 exps[j] = exp_sb[:]
@@ -166,9 +191,6 @@ def tile_attend_at_cfg_topk_kernel(tc, qT, k_words, k_scales, c_words, c_scales,
             end = e * P + codes.shape[1]
             nc.vector.quantize_mx(codes[:].bitcast(FP8X4), v_scale[:, e * P : end], v_bf[e][:])
 
-        def plain(name):
-            return held.tile([P, 4, P], F32, name=name)
-
         def word_tile(width, name):
             return held.tile([P, width], U32, name=name, align_bytes=64)
 
@@ -192,43 +214,45 @@ def tile_attend_at_cfg_topk_kernel(tc, qT, k_words, k_scales, c_words, c_scales,
             nc.scalar.copy(staged[:], ps[:])
             nc.sync.dma_start(out_rows[:, js[0] : js[-1] + 1, es[0] * P : es[0] * P + width], staged[:])
 
-        SPARE = BLOCKS + 1
-        second_scores(0, 4, plain("second0"), True)
+        joint_close(0)
+        apart_close(2)
         values_gather(0)
-        second_scores(1, 5, plain("second1"), False)
-        weights_turn(1, 1)
-        weights_turn(0, 0)
-        second_scores(2, 6, plain("second2"), False)
-        weights_scale(1, SPARE, 4, nc.gpsimd)
-        second_scores(3, 7, plain("second3"), False)
+        weights_turn(0, 5)
+        weights_scale(0, 0, 0, nc.vector)
+        weights_turn(1, 6)
         values_turn(0, 4, SPARE, 0)
+        joint_open(2, 3)
+        joint_close(2)
         values_gather(1)
-        weights_turn(2, 2)
-        weights_scale(0, 1, 0, nc.vector)
-        values_quantise(0, guest(1, 1, [P, P], U32, "v_codes0"))
-        values_turn(1, 5, SPARE, 1)
-        weights_turn(3, 3)
-        weights_scale(2, SPARE, 0, nc.gpsimd)
+        weights_quantise(0, guest(1, 0, [P, P], U32, "y_codes0"))
+        weights_scale(1, 1, 1, nc.vector)
+        values_quantise(0, guest(1, 2, [P, P], U32, "v_codes0"))
+        weights_turn(2, 7)
+        values_turn(1, 0, SPARE, 1)
+        joint_open(3, 5)
+        joint_close(3)
+        weights_turn(3, 1)
         values_gather(2)
-        values_turn(2, 6, SPARE, 2)
-        weights_quantise(0, guest(2, 3, [P, P], U32, "y_codes0"))
+        values_turn(2, 2, SPARE, 2)
         weights_quantise(1, guest(2, 0, [P, P], U32, "y_codes1"))
-        values_quantise(1, guest(2, 1, [P, P], U32, "v_codes1"))
-        weights_quantise(2, guest(2, 2, [P, P], U32, "y_codes2"))
-        weights_scale(3, SPARE, 0, nc.gpsimd)
-        product_and_store([0, 1], [0, 1], 0)
-        product_and_store([2], [0, 1], 1)
+        weights_scale(2, 2, 1, nc.vector)
+        values_quantise(1, guest(2, 2, [P, P], U32, "v_codes1"))
+        weights_quantise(2, word_tile(P, "y_codes2"))
+        product_and_store([0, 1], [0, 1], 3)
+        product_and_store([2], [0, 1], 6)
         values_gather(3)
-        values_turn(3, 7, SPARE, 3)
+        values_turn(3, 4, SPARE, 3)
+        weights_scale(3, 3, 0, nc.vector)
         values_quantise(2, guest(3, 1, [P, P], U32, "v_codes2"))
-        weights_quantise(3, guest(3, 0, [P, P], U32, "y_codes3"))
+        weights_quantise(3, word_tile(P, "y_codes3"))
         values_quantise(3, word_tile(P, "v_codes3"))
-        product_and_store([0, 1, 2], [2], 2)
-        product_and_store([3], [0, 1, 2], 3)
+        product_and_store([0, 1, 2], [2], 0)
+        product_and_store([3], [0, 1, 2], 5)
         last = held.tile([P, BLOCKS, P], F32, name="last")
-        low, high = bank(4, [P, 2, P], "low_ps"), bank(5, [P, 2, P], "high_ps")
+        low, high = bank(2, [P, 2, P], "low_ps"), bank(7, [P, 2, P], "high_ps")
         product(low, [0, 1], [3])
         nc.scalar.copy(last[:, 0:2, :], low[:])
+        nc.scalar.dma_start(out_rows[:, 0:2, 3 * P : DV], last[:, 0:2, :])
         product(high, [2, 3], [3])
         nc.vector.tensor_copy(last[:, 2:4, :], high[:])
-        nc.sync.dma_start(out_rows[:, :, 3 * P : DV], last[:])
+        nc.sync.dma_start(out_rows[:, 2:4, 3 * P : DV], last[:, 2:4, :])

@@ -169,6 +169,11 @@ def tile_attend_at_cfg_topk_kernel(tc, qT, k_words, k_scales, c_words, c_scales,
             y_bf[j] = guest(window, place, [P, P, 4], BF16, f"y_bf{j}")
             engine.tensor_tensor(y_bf[j][:], exps[j], us_places, ALU.mult)
 
+        def weights_scale_by_place(j):
+            y_bf[j] = held.tile([P, P, 4], BF16, name=f"y_bf{j}", align_bytes=64)
+            for s in range(4):
+                nc.scalar.activation(y_bf[j][:, :, s], exps[j][:, :, s], ACT.Copy, scale=us_sb[:, s : s + 1])
+
         def weights_quantise(j, codes):
             y_codes[j] = codes
             nc.vector.quantize_mx(codes[:].bitcast(FP8X4), y_scale[:, j * P : (j + 1) * P], y_bf[j][:].rearrange("p q s -> p (q s)"))
@@ -205,54 +210,48 @@ def tile_attend_at_cfg_topk_kernel(tc, qT, k_words, k_scales, c_words, c_scales,
                                         lhsT_scale=y_scale[:, j * P : (j + 1) * P], rhs=v_codes[e][:].bitcast(FP8X4),
                                         rhs_scale=v_scale[:, e * P : e * P + width], start=True, stop=True)
 
-        def product_and_store(js, es, bank_number):
+        def product_and_store(js, es, bank_number, copy=nc.scalar.copy, queue=nc.sync):
             width = sum(v_codes[e].shape[1] for e in es)
             name = f"out{js[0]}{es[0]}"
             staged = held.tile([P, len(js), width], F32, name=name)
             ps = bank(bank_number, [P, len(js), width], name + "_ps")
             product(ps, js, es)
-            nc.scalar.copy(staged[:], ps[:])
-            nc.sync.dma_start(out_rows[:, js[0] : js[-1] + 1, es[0] * P : es[0] * P + width], staged[:])
+            copy(staged[:], ps[:])
+            queue.dma_start(out_rows[:, js[0] : js[-1] + 1, es[0] * P : es[0] * P + width], staged[:])
 
         joint_close(0)
         apart_close(2)
         values_gather(0)
         weights_turn(0, 5)
         weights_scale(0, 0, 0, nc.vector)
-        weights_turn(1, 6)
-        values_turn(0, 4, SPARE, 0)
         joint_open(2, 3)
         joint_close(2)
+        weights_turn(1, 6)
+        weights_turn(2, 7)
+        values_turn(0, 4, SPARE, 0)
         values_gather(1)
         weights_quantise(0, guest(1, 0, [P, P], U32, "y_codes0"))
         weights_scale(1, 1, 1, nc.vector)
-        values_quantise(0, guest(1, 2, [P, P], U32, "v_codes0"))
-        weights_turn(2, 7)
         values_turn(1, 0, SPARE, 1)
+        weights_scale_by_place(2)
         joint_open(3, 5)
         joint_close(3)
-        weights_turn(3, 1)
         values_gather(2)
         values_turn(2, 2, SPARE, 2)
+        weights_turn(3, 1)
         weights_quantise(1, guest(2, 0, [P, P], U32, "y_codes1"))
-        weights_scale(2, 2, 1, nc.vector)
+        values_quantise(0, guest(2, 1, [P, P], U32, "v_codes0"))
+        weights_quantise(2, guest(2, 3, [P, P], U32, "y_codes2"))
         values_quantise(1, guest(2, 2, [P, P], U32, "v_codes1"))
-        weights_quantise(2, word_tile(P, "y_codes2"))
         product_and_store([0, 1], [0, 1], 3)
         product_and_store([2], [0, 1], 6)
         values_gather(3)
         values_turn(3, 4, SPARE, 3)
-        weights_scale(3, 3, 0, nc.vector)
         values_quantise(2, guest(3, 1, [P, P], U32, "v_codes2"))
+        weights_scale(3, 3, 0, nc.vector)
+        product_and_store([0, 1, 2], [2], 0)
         weights_quantise(3, word_tile(P, "y_codes3"))
         values_quantise(3, word_tile(P, "v_codes3"))
-        product_and_store([0, 1, 2], [2], 0)
         product_and_store([3], [0, 1, 2], 5)
-        last = held.tile([P, BLOCKS, P], F32, name="last")
-        low, high = bank(2, [P, 2, P], "low_ps"), bank(7, [P, 2, P], "high_ps")
-        product(low, [0, 1], [3])
-        nc.scalar.copy(last[:, 0:2, :], low[:])
-        nc.scalar.dma_start(out_rows[:, 0:2, 3 * P : DV], last[:, 0:2, :])
-        product(high, [2, 3], [3])
-        nc.vector.tensor_copy(last[:, 2:4, :], high[:])
-        nc.sync.dma_start(out_rows[:, 2:4, 3 * P : DV], last[:, 2:4, :])
+        product_and_store([0, 1], [3], 2, nc.vector.tensor_copy)
+        product_and_store([2, 3], [3], 7, nc.scalar.copy, nc.scalar)

@@ -16,10 +16,11 @@ ALU = mybir.AluOpType
 P = 128
 N, T, D, NQ, DV = 512, 2048, 512, 512, 512
 BLOCKS = 4
+PLACES = 4
 FLOPS = 2 * 2 * N * D * NQ + 2 * N * NQ * DV
 
 WINDOW_BYTES = 4 * T
-SPARE, K_WINDOW, C_WINDOW, Q_WINDOW = 5, 6, 7, 8
+K_WINDOW, C_WINDOW = BLOCKS, BLOCKS + 1
 GUEST_BYTES = 1024
 BANK_BYTES = 2048
 APART = 1
@@ -36,19 +37,24 @@ def tile_attend_at_cfg_topk_kernel(tc, qT, k_words, k_scales, c_words, c_scales,
         def bank(number, shape, name):
             return psum.tile(shape, F32, name=name, offset=number * BANK_BYTES)
 
-        def guest(window, place, shape, dtype, name):
-            return reused.tile(shape, dtype, name=name, offset=window * WINDOW_BYTES + place * GUEST_BYTES, align_bytes=64)
+        def guest(window, room, shape, dtype, name):
+            return reused.tile(shape, dtype, name=name, offset=window * WINDOW_BYTES + room * GUEST_BYTES, align_bytes=64)
+
+        def aligned(shape, dtype, name):
+            return held.tile(shape, dtype, name=name, align_bytes=64)
 
         offsets = held.tile([P, N // 16], U16, name="offsets")
         nc.sync.dma_start(offsets[:], offs)
         ident = held.tile([P, P], F32, name="ident")
-        ks_win = reused.tile([P, T // 4], I32, name="ks_win", offset=BLOCKS * WINDOW_BYTES)
+        ks_win = held.tile([P, T // 4], I32, name="ks_win")
         cs_win = held.tile([P, T // 4], I32, name="cs_win")
         ls_rows = held.tile([P, P], F32, name="ls_rows")
         nc.vector.memset(ks_win[:], 0)
         nc.vector.memset(ls_rows[:], 0.0)
         nc.vector.memset(cs_win[:], 0)
         make_identity(nc, ident[:])
+        warm = held.tile([P, 8], F32, name="warm")
+        nc.scalar.activation(warm[32:64, 0:1], ls_rows[32:64, 0:1], ACT.Exp)
 
         def load_scales(win, scales, first_row):
             for quad in range(4):
@@ -60,17 +66,19 @@ def tile_attend_at_cfg_topk_kernel(tc, qT, k_words, k_scales, c_words, c_scales,
             nc.sync.dma_start(win[:], packed[0].rearrange("p t r -> p (t r)").bitcast(I32))
             return win
 
-        q_raw = held.tile([P, 4, NQ], F32, name="q_raw")
-        nc.sync.dma_start(q_raw[:], qT[0].rearrange("(p t) q -> p t q", t=4))
+        q_raw = held.tile([P, PLACES, NQ], F32, name="q_raw")
+        q_rows = qT[0].rearrange("(p t) q -> p t q", t=PLACES)
+        nc.sync.dma_start(q_raw[:, 0:2, :], q_rows[:, 0:2, :])
         load_scales(ks_win, k_scales, 0)
-        nc.sync.dma_start(ls_rows[0:BLOCKS, :], ls[0, 0].rearrange("(j m) -> j m", j=BLOCKS))
+        nc.sync.dma_start(q_raw[:, 2:4, :], q_rows[:, 2:4, :])
         k_win = load_words(k_words, K_WINDOW, "k_win")
+        nc.sync.dma_start(ls_rows[0:BLOCKS, :], ls[0, 0].rearrange("(j m) -> j m", j=BLOCKS))
         load_scales(cs_win, c_scales, C_SCALE_ROW)
         c_win = load_words(c_words, C_WINDOW, "c_win")
-        us_sb = held.tile([P, 4], F32, name="us_sb")
+        us_sb = held.tile([P, PLACES], F32, name="us_sb")
         v_win = [reused.tile([P, T], F32, name=f"v_win{e}", offset=e * WINDOW_BYTES) for e in range(BLOCKS)]
         nc.sync.dma_start(v_win[0][:], vT[0:P, :])
-        nc.sync.dma_start(us_sb[:], us[0].rearrange("(p s) o -> p (s o)", s=4))
+        nc.sync.dma_start(us_sb[:], us[0].rearrange("(p t) o -> p (t o)", t=PLACES))
         for e in range(1, BLOCKS):
             nc.sync.dma_start(v_win[e][:], vT[e * P : (e + 1) * P, :])
 
@@ -78,26 +86,30 @@ def tile_attend_at_cfg_topk_kernel(tc, qT, k_words, k_scales, c_words, c_scales,
             nc.vector.tensor_copy(picked[:], win[:].bitcast(dtype).indirect(offsets[:]))
             return picked
 
-        half = NQ // 2
         q_turned = q_raw[:].rearrange("p t q -> p q t")
         q_words, q_scales = {}, {}
 
+        def queries_round(copy, rounded, j):
+            copy(rounded.rearrange("p (q t) -> p q t", t=PLACES), q_turned[:, j * P : (j + 1) * P, :])
+
         def queries_quantise(rounded, codes, names):
-            scale = held.tile([P, len(names) * P], U8, name=f"q_scale{names[0]}", align_bytes=64)
+            scale = aligned([P, len(names) * P], U8, f"q_scale_{names[0]}")
             nc.vector.quantize_mx(codes[:].bitcast(FP8X4), scale[:], rounded)
             for n, name in enumerate(names):
                 q_words[name], q_scales[name] = codes[:, n * P : (n + 1) * P], scale[:, n * P : (n + 1) * P]
 
-        low_bf = guest(Q_WINDOW, 0, [P, 4 * half], BF16, "low_bf")
-        low_times = held.tile([P, 4 * P], BF16, name="low_times", align_bytes=64)
-        high_bf = guest(Q_WINDOW, 0, [P, 2, 4 * half], BF16, "high_bf")
-        nc.scalar.copy(low_bf[:].rearrange("p (q t) -> p q t", t=4), q_turned[:, 0:half, :])
-        nc.scalar.mul(low_times[:], low_bf[:, 0 : 4 * P], -4.0)
-        k_scale = gather(ks_win, U8, held.tile([P, N], U8, name="k_scale", align_bytes=64))
-        queries_quantise(low_bf[:], guest(BLOCKS, 0, [P, half], U32, "q_low"), ["q0", "q1"])
-        queries_quantise(low_times[:], guest(BLOCKS, 1, [P, P], U32, "q_low_times"), ["m0"])
-        nc.scalar.copy(high_bf[:, 0, :].rearrange("p (q t) -> p q t", t=4), q_turned[:, half:NQ, :])
-        nc.scalar.mul(high_bf[:, 1, :], high_bf[:, 0, :], -4.0)
+        k_scale = gather(ks_win, U8, aligned([P, N], U8, "k_scale"))
+        early_bf = aligned([P, 4, PLACES * P], BF16, "early_bf")
+        apart_bf = aligned([P, PLACES * P], BF16, "apart_bf")
+        late_bf = aligned([P, 2, PLACES * P], BF16, "late_bf")
+        queries_round(nc.vector.tensor_copy, early_bf[:, 0, :], 0)
+        queries_round(nc.scalar.copy, early_bf[:, 1, :], 2)
+        queries_round(nc.scalar.copy, apart_bf[:], APART)
+        queries_round(nc.scalar.copy, late_bf[:, 0, :], 3)
+        nc.vector.tensor_scalar_mul(early_bf[:, 2:4, :], early_bf[:, 0:2, :], -0.25)
+        nc.scalar.mul(late_bf[:, 1, :], late_bf[:, 0, :], -0.25)
+        queries_quantise(early_bf[:].rearrange("p a b -> p (a b)"), aligned([P, 4 * P], U32, "q_early"), ["q0", "q2", "m0", "m2"])
+        queries_quantise(apart_bf[:], aligned([P, P], U32, "q_apart"), ["q1"])
         neg_ls = held.tile([P, BLOCKS], F32, name="neg_ls")
         ls_ps = bank(4, [P, P], "ls_ps")
         nc.tensor.transpose(ls_ps[:], ls_rows[:], ident[:])
@@ -109,149 +121,144 @@ def tile_attend_at_cfg_topk_kernel(tc, qT, k_words, k_scales, c_words, c_scales,
                                 rhs=codes[:].bitcast(FP8X4), rhs_scale=scale, start=start, stop=stop)
 
         def by_place(ps):
-            return ps[:].rearrange("q (p s) -> q s p", s=4)
+            return ps[:].rearrange("q (p t) -> q t p", t=PLACES)
 
-        def plain(name):
-            return held.tile([P, 4, P], F32, name=name)
+        def planes(name):
+            return held.tile([P, PLACES, P], F32, name=name)
 
-        k_codes = gather(k_win, U32, held.tile([P, N], U32, name="k_codes", align_bytes=64))
-        k_keys = (k_codes, k_scale[:])
-        joint = {0: bank(0, [P, N], "joint0")}
-        score_pass(joint[0], "q0", k_keys, True, False)
-        score_pass(joint[0], "m0", k_keys, False, False)
-        a_ps = bank(1, [P, N], "a_apart")
-        score_pass(a_ps, "q1", k_keys, True, True)
-        first = plain("first")
-        nc.scalar.mul(first[:], by_place(a_ps), 1.5)
-        c_scale = gather(cs_win, U8, guest(K_WINDOW, 0, [P, N], U8, "c_scale"))
-        c_codes = gather(c_win, U32, held.tile([P, N], U32, name="c_codes", align_bytes=64))
-        c_keys = (c_codes, c_scale[C_SCALE_ROW:P, :])
-        queries_quantise(high_bf[:].rearrange("p a b -> p (a b)"), guest(C_WINDOW, 0, [P, NQ], U32, "q_high"), ["q2", "q3", "m2", "m3"])
-
-        y_scale = held.tile([P, NQ], U8, name="y_scale", align_bytes=64)
-        v_scale = held.tile([P, DV], U8, name="v_scale", align_bytes=64)
-        v_bf = {}
-        us_places = us_sb[:].unsqueeze(1).to_broadcast([P, P, 4])
-        to_turn, exps, y_bf, y_codes, v_picked, v_codes = {}, {}, {}, {}, {}, {}
+        k_keys = (gather(k_win, U32, aligned([P, N], U32, "k_codes")), k_scale[:])
+        joint = {}
 
         def joint_open(j, bank_number):
             joint[j] = bank(bank_number, [P, N], f"joint{j}")
             score_pass(joint[j], f"q{j}", k_keys, True, False)
             score_pass(joint[j], f"m{j}", k_keys, False, False)
 
-        def joint_close(j):
-            score_pass(joint[j], f"q{j}", c_keys, False, True)
-            exp_sb = plain(f"exp{j}")
-            nc.scalar.activation(exp_sb[:], by_place(joint[j]), ACT.Exp, bias=neg_ls[:, j : j + 1], scale=-0.5)
+        a_ps = bank(1, [P, N], "a_apart")
+        score_pass(a_ps, f"q{APART}", k_keys, True, True)
+        a_term = planes("a_term")
+        nc.scalar.mul(a_term[:], by_place(a_ps), 1.5)
+        joint_open(0, 0)
+        joint_open(2, 3)
+        c_scale = gather(cs_win, U8, guest(K_WINDOW, 0, [P, N], U8, "c_scale"))
+        c_keys = (gather(c_win, U32, aligned([P, N], U32, "c_codes")), c_scale[C_SCALE_ROW:P, :])
+        queries_quantise(late_bf[:].rearrange("p a b -> p (a b)"), guest(C_WINDOW, 0, [P, 2 * P], U32, "q_late"), ["q3", "m3"])
+
+        y_scale = aligned([P, NQ], U8, "y_scale")
+        v_scale = aligned([P, DV], U8, "v_scale")
+        us_places = us_sb[:].unsqueeze(1).to_broadcast([P, P, PLACES])
+        to_turn, exps, y_bf, y_codes, v_picked, v_bf, v_codes = {}, {}, {}, {}, {}, {}, {}
+
+        def joint_close(j, pieces):
+            score_pass(joint[j], f"m{j}", c_keys, False, True)
+            exp_sb = planes(f"exp{j}")
+            for n in range(pieces):
+                part = slice(PLACES * n // pieces, PLACES * (n + 1) // pieces)
+                nc.scalar.activation(exp_sb[:, part, :], by_place(joint[j])[:, part, :], ACT.Exp, bias=neg_ls[:, j : j + 1], scale=2.0)
             to_turn[j] = [exp_sb]
 
         def apart_close(bank_number):
             z_ps = bank(bank_number, [P, N], "z_apart")
             score_pass(z_ps, f"q{APART}", c_keys, True, True)
-            second = plain("second")
-            nc.scalar.activation(second[:], by_place(z_ps), ACT.Identity, bias=neg_ls[:, APART : APART + 1], scale=-0.5)
-            to_turn[APART] = [second, first]
+            z_term = planes("z_term")
+            nc.scalar.activation(z_term[:], by_place(z_ps), ACT.Identity, bias=neg_ls[:, APART : APART + 1], scale=-0.5)
+            to_turn[APART] = [z_term, a_term]
 
         def weights_turn(j, bank_number):
-            ps = bank(bank_number, [P, 4, P], f"t{j}")
+            ps = bank(bank_number, [P, PLACES, P], f"turned{j}")
             terms = to_turn[j]
-            for s in range(4):
+            for t in range(PLACES):
                 for n, term in enumerate(terms):
-                    nc.tensor.matmul(ps[:, s, :], term[:, s, :], ident[:], start=n == 0,
+                    nc.tensor.matmul(ps[:, t, :], term[:, t, :], ident[:], start=n == 0,
                                      stop=n == len(terms) - 1, is_transpose=True)
-            exps[j] = ps[:].rearrange("p s q -> p q s")
+            exps[j] = ps[:].rearrange("p t q -> p q t")
             if j == APART:
-                exp_sb = held.tile([P, P, 4], F32, name=f"exp{j}")
+                exp_sb = held.tile([P, P, PLACES], F32, name=f"exp{j}")
                 nc.scalar.activation(exp_sb[:], exps[j], ACT.Exp)
                 exps[j] = exp_sb[:]
 
-        def weights_scale(j, window, place, engine):
-            y_bf[j] = guest(window, place, [P, P, 4], BF16, f"y_bf{j}")
-            engine.tensor_tensor(y_bf[j][:], exps[j], us_places, ALU.mult)
+        def weights_scale(j, window, room):
+            y_bf[j] = guest(window, room, [P, P, PLACES], BF16, f"y_bf{j}")
+            nc.vector.tensor_tensor(y_bf[j][:], exps[j], us_places, ALU.mult)
 
         def weights_scale_by_place(j):
-            y_bf[j] = held.tile([P, P, 4], BF16, name=f"y_bf{j}", align_bytes=64)
-            for s in range(4):
-                nc.scalar.activation(y_bf[j][:, :, s], exps[j][:, :, s], ACT.Copy, scale=us_sb[:, s : s + 1])
+            y_bf[j] = aligned([P, P, PLACES], BF16, f"y_bf{j}")
+            for t in range(PLACES):
+                nc.scalar.activation(y_bf[j][:, :, t], exps[j][:, :, t], ACT.Copy, scale=us_sb[:, t : t + 1])
 
         def weights_quantise(j, codes):
             y_codes[j] = codes
-            nc.vector.quantize_mx(codes[:].bitcast(FP8X4), y_scale[:, j * P : (j + 1) * P], y_bf[j][:].rearrange("p q s -> p (q s)"))
+            nc.vector.quantize_mx(codes[:].bitcast(FP8X4), y_scale[:, j * P : (j + 1) * P], y_bf[j][:].rearrange("p q t -> p (q t)"))
 
         def values_gather(e):
             v_picked[e] = held.tile([P, N], BF16, name=f"v_picked{e}")
             nc.vector.tensor_copy(v_picked[e][:], v_win[e][:].indirect(offsets[:]))
 
-        def values_turn(e, bank_number, window, place):
+        def values_turn(e, bank_number):
             pairs = v_picked[e][:].bitcast(F32)
             ps = bank(bank_number, [P, 2, P], f"v{e}")
-            for b in range(2):
-                nc.tensor.transpose(ps[:, b, :], pairs[:, b : 2 * P : 2], ident[:])
-            v_bf[e] = guest(window, place, [P, 4 * P], BF16, f"v_bf{e}")
-            dst = v_bf[e][:].bitcast(F32).rearrange("p (e b) -> p e b", b=2)
-            nc.scalar.copy(dst, ps[:].rearrange("p b e -> p e b"))
+            for u in range(2):
+                nc.tensor.transpose(ps[:, u, :], pairs[:, u : 2 * P : 2], ident[:])
+            v_bf[e] = aligned([P, PLACES * P], BF16, f"v_bf{e}")
+            nc.scalar.copy(v_bf[e][:].bitcast(F32).rearrange("p (e u) -> p e u", u=2), ps[:].rearrange("p u e -> p e u"))
 
         def values_quantise(e, codes):
             v_codes[e] = codes
-            end = e * P + codes.shape[1]
-            nc.vector.quantize_mx(codes[:].bitcast(FP8X4), v_scale[:, e * P : end], v_bf[e][:])
+            nc.vector.quantize_mx(codes[:].bitcast(FP8X4), v_scale[:, e * P : (e + 1) * P], v_bf[e][:])
 
-        def word_tile(width, name):
-            return held.tile([P, width], U32, name=name, align_bytes=64)
+        def guest_words(window, room, name):
+            return guest(window, room, [P, P], U32, name)
 
         out_rows = out[0].rearrange("(j m) e -> m j e", m=P)
 
-        def product(ps, js, es):
+        def product(js, es, bank_number):
+            ps = bank(bank_number, [P, len(js), len(es) * P], f"out_ps{js[0]}{es[0]}")
             for n, j in enumerate(js):
-                for e in es:
-                    width = v_codes[e].shape[1]
-                    start = (e - es[0]) * P
-                    nc.tensor.matmul_mx(ps[:, n, start : start + width], lhsT=y_codes[j][:].bitcast(FP8X4),
+                for m, e in enumerate(es):
+                    nc.tensor.matmul_mx(ps[:, n, m * P : (m + 1) * P], lhsT=y_codes[j][:].bitcast(FP8X4),
                                         lhsT_scale=y_scale[:, j * P : (j + 1) * P], rhs=v_codes[e][:].bitcast(FP8X4),
-                                        rhs_scale=v_scale[:, e * P : e * P + width], start=True, stop=True)
+                                        rhs_scale=v_scale[:, e * P : (e + 1) * P], start=True, stop=True)
+            return ps
 
-        def product_and_store(js, es, bank_number, copy=nc.scalar.copy, queue=nc.sync):
-            width = sum(v_codes[e].shape[1] for e in es)
-            name = f"out{js[0]}{es[0]}"
-            staged = held.tile([P, len(js), width], F32, name=name)
-            ps = bank(bank_number, [P, len(js), width], name + "_ps")
-            product(ps, js, es)
-            copy(staged[:], ps[:])
-            queue.dma_start(out_rows[:, js[0] : js[-1] + 1, es[0] * P : es[0] * P + width], staged[:])
+        def product_and_store(js, es, bank_number, copy, queue):
+            staged = held.tile([P, len(js), len(es) * P], F32, name=f"out{js[0]}{es[0]}")
+            copy(staged[:], product(js, es, bank_number)[:])
+            queue.dma_start(out_rows[:, js[0] : js[-1] + 1, es[0] * P : (es[-1] + 1) * P], staged[:])
 
-        joint_close(0)
+        joint_close(0, 2)
         apart_close(2)
         values_gather(0)
         weights_turn(0, 5)
-        weights_scale(0, 0, 0, nc.vector)
-        joint_open(2, 3)
-        joint_close(2)
+        weights_scale(0, 0, 0)
+        joint_close(2, 1)
         weights_turn(1, 6)
         weights_turn(2, 7)
-        values_turn(0, 4, SPARE, 0)
+        values_turn(0, 4)
         values_gather(1)
-        weights_quantise(0, guest(1, 0, [P, P], U32, "y_codes0"))
-        weights_scale(1, 1, 1, nc.vector)
-        values_turn(1, 0, SPARE, 1)
+        weights_quantise(0, guest_words(1, 0, "y_codes0"))
+        weights_scale(1, 1, 1)
+        values_turn(1, 0)
         weights_scale_by_place(2)
         joint_open(3, 5)
-        joint_close(3)
+        joint_close(3, 1)
         values_gather(2)
-        values_turn(2, 2, SPARE, 2)
+        values_turn(2, 2)
         weights_turn(3, 1)
-        weights_quantise(1, guest(2, 0, [P, P], U32, "y_codes1"))
-        values_quantise(0, guest(2, 1, [P, P], U32, "v_codes0"))
-        weights_quantise(2, guest(2, 3, [P, P], U32, "y_codes2"))
-        values_quantise(1, guest(2, 2, [P, P], U32, "v_codes1"))
-        product_and_store([0, 1], [0, 1], 3)
-        product_and_store([2], [0, 1], 6)
+        weights_quantise(1, guest_words(2, 0, "y_codes1"))
+        values_quantise(0, guest_words(2, 1, "v_codes0"))
+        weights_quantise(2, guest_words(2, 3, "y_codes2"))
+        values_quantise(1, guest_words(2, 2, "v_codes1"))
+        early_out = held.tile([P, 3, 2 * P], F32, name="early_out")
+        for js, bank_number in (([0, 1], 3), ([2], 6)):
+            nc.scalar.copy(early_out[:, js[0] : js[-1] + 1, :], product(js, [0, 1], bank_number)[:])
+        nc.sync.dma_start(out_rows[:, 0:3, 0 : 2 * P], early_out[:])
         values_gather(3)
-        values_turn(3, 4, SPARE, 3)
-        values_quantise(2, guest(3, 1, [P, P], U32, "v_codes2"))
-        weights_scale(3, 3, 0, nc.vector)
-        product_and_store([0, 1, 2], [2], 0)
-        weights_quantise(3, word_tile(P, "y_codes3"))
-        values_quantise(3, word_tile(P, "v_codes3"))
-        product_and_store([3], [0, 1, 2], 5)
-        product_and_store([0, 1], [3], 2, nc.vector.tensor_copy)
+        values_turn(3, 4)
+        values_quantise(2, guest_words(3, 1, "v_codes2"))
+        weights_scale(3, 3, 0)
+        product_and_store([0, 1, 2], [2], 0, nc.scalar.copy, nc.sync)
+        weights_quantise(3, aligned([P, P], U32, "y_codes3"))
+        values_quantise(3, guest_words(3, 0, "v_codes3"))
+        product_and_store([3], [0, 1, 2], 5, nc.scalar.copy, nc.sync)
+        product_and_store([0, 1], [3], 2, nc.vector.tensor_copy, nc.sync)
         product_and_store([2, 3], [3], 7, nc.scalar.copy, nc.scalar)

@@ -20,11 +20,13 @@ PLACES = 4
 FLOPS = 2 * 2 * N * D * NQ + 2 * N * NQ * DV
 
 WINDOW_BYTES = 4 * T
-K_WINDOW, C_WINDOW = BLOCKS, BLOCKS + 1
+OVERLAP = 64
+CHAIN = WINDOW_BYTES - OVERLAP
+K_AT, C_AT, S_AT = 0, 2 * WINDOW_BYTES, 4 * WINDOW_BYTES
+V_AT = [S_AT + T - OVERLAP, K_AT + CHAIN, C_AT + CHAIN, S_AT + T - OVERLAP + CHAIN]
 GUEST_BYTES = 1024
 BANK_BYTES = 2048
 APART = 1
-C_SCALE_ROW = 4
 
 
 def tile_attend_at_cfg_topk_kernel(tc, qT, k_words, k_scales, c_words, c_scales, vT, ls, us, offs, out):
@@ -38,7 +40,7 @@ def tile_attend_at_cfg_topk_kernel(tc, qT, k_words, k_scales, c_words, c_scales,
             return psum.tile(shape, F32, name=name, offset=number * BANK_BYTES)
 
         def guest(window, room, shape, dtype, name):
-            return reused.tile(shape, dtype, name=name, offset=window * WINDOW_BYTES + room * GUEST_BYTES, align_bytes=64)
+            return reused.tile(shape, dtype, name=name, offset=window + room * GUEST_BYTES, align_bytes=64)
 
         def aligned(shape, dtype, name):
             return held.tile(shape, dtype, name=name, align_bytes=64)
@@ -47,11 +49,13 @@ def tile_attend_at_cfg_topk_kernel(tc, qT, k_words, k_scales, c_words, c_scales,
         nc.sync.dma_start(offsets[:], offs)
         ident = held.tile([P, P], F32, name="ident")
         ks_win = held.tile([P, T // 4], I32, name="ks_win")
-        cs_win = held.tile([P, T // 4], I32, name="cs_win")
+        cs_win = reused.tile([P, T // 4], I32, name="cs_win", offset=S_AT)
+        c_plane = aligned([P, N // 4], I32, "c_plane")
         ls_rows = held.tile([P, P], F32, name="ls_rows")
         nc.vector.memset(ks_win[:], 0)
         nc.vector.memset(ls_rows[:], 0.0)
         nc.vector.memset(cs_win[:], 0)
+        nc.vector.memset(c_plane[:], 0)
         make_identity(nc, ident[:])
         warm = held.tile([P, 8], F32, name="warm")
         nc.scalar.activation(warm[32:64, 0:1], ls_rows[32:64, 0:1], ACT.Exp)
@@ -62,7 +66,7 @@ def tile_attend_at_cfg_topk_kernel(tc, qT, k_words, k_scales, c_words, c_scales,
                 nc.sync.dma_start(win[row : row + 4, :], scales[0, 4 * quad : 4 * quad + 4, :].bitcast(I32))
 
         def load_words(packed, window, name):
-            win = reused.tile([P, T], I32, name=name, offset=window * WINDOW_BYTES)
+            win = reused.tile([P, T], I32, name=name, offset=window)
             nc.sync.dma_start(win[:], packed[0].rearrange("p t r -> p (t r)").bitcast(I32))
             return win
 
@@ -71,20 +75,28 @@ def tile_attend_at_cfg_topk_kernel(tc, qT, k_words, k_scales, c_words, c_scales,
         nc.sync.dma_start(q_raw[:, 0:2, :], q_rows[:, 0:2, :])
         load_scales(ks_win, k_scales, 0)
         nc.sync.dma_start(q_raw[:, 2:4, :], q_rows[:, 2:4, :])
-        k_win = load_words(k_words, K_WINDOW, "k_win")
+        nc.sync.dma_start(cs_win[0:P:8, :], c_scales[0].bitcast(I32))
+        k_win = load_words(k_words, K_AT, "k_win")
         nc.sync.dma_start(ls_rows[0:BLOCKS, :], ls[0, 0].rearrange("(j m) -> j m", j=BLOCKS))
-        load_scales(cs_win, c_scales, C_SCALE_ROW)
-        c_win = load_words(c_words, C_WINDOW, "c_win")
-        us_sb = held.tile([P, PLACES], F32, name="us_sb")
-        v_win = [reused.tile([P, T], F32, name=f"v_win{e}", offset=e * WINDOW_BYTES) for e in range(BLOCKS)]
-        nc.sync.dma_start(v_win[0][:], vT[0:P, :])
-        nc.sync.dma_start(us_sb[:], us[0].rearrange("(p t) o -> p (t o)", t=PLACES))
-        for e in range(1, BLOCKS):
-            nc.sync.dma_start(v_win[e][:], vT[e * P : (e + 1) * P, :])
+        c_win = load_words(c_words, C_AT, "c_win")
 
         def gather(win, dtype, picked):
             nc.vector.tensor_copy(picked[:], win[:].bitcast(dtype).indirect(offsets[:]))
             return picked
+
+        k_scale = gather(ks_win, U8, aligned([P, N], U8, "k_scale"))
+        c_rows = gather(cs_win, U8, held.tile([P, N], U8, name="c_rows"))[:].bitcast(I32)
+        for r in range(4):
+            nc.sync.dma_start(c_plane[r:P:32, :], c_rows[8 * r : P : 32, :])
+        us_sb = held.tile([P, PLACES], F32, name="us_sb")
+        v_win = {}
+
+        def values_load(e):
+            v_win[e] = reused.tile([P, T], F32, name=f"v_win{e}", offset=V_AT[e])
+            nc.sync.dma_start(v_win[e][:], vT[e * P : (e + 1) * P, :])
+
+        values_load(0)
+        nc.sync.dma_start(us_sb[:], us[0].rearrange("(p t) o -> p (t o)", t=PLACES))
 
         q_turned = q_raw[:].rearrange("p t q -> p q t")
         q_words, q_scales = {}, {}
@@ -98,17 +110,15 @@ def tile_attend_at_cfg_topk_kernel(tc, qT, k_words, k_scales, c_words, c_scales,
             for n, name in enumerate(names):
                 q_words[name], q_scales[name] = codes[:, n * P : (n + 1) * P], scale[:, n * P : (n + 1) * P]
 
-        k_scale = gather(ks_win, U8, aligned([P, N], U8, "k_scale"))
-        early_bf = aligned([P, 4, PLACES * P], BF16, "early_bf")
+        first_bf = aligned([P, 2, PLACES * P], BF16, "first_bf")
         apart_bf = aligned([P, PLACES * P], BF16, "apart_bf")
         late_bf = aligned([P, 2, PLACES * P], BF16, "late_bf")
-        queries_round(nc.vector.tensor_copy, early_bf[:, 0, :], 0)
-        queries_round(nc.scalar.copy, early_bf[:, 1, :], 2)
+        queries_round(nc.scalar.copy, first_bf[:, 0, :], 0)
         queries_round(nc.scalar.copy, apart_bf[:], APART)
-        queries_round(nc.scalar.copy, late_bf[:, 0, :], 3)
-        nc.vector.tensor_scalar_mul(early_bf[:, 2:4, :], early_bf[:, 0:2, :], -0.25)
-        nc.scalar.mul(late_bf[:, 1, :], late_bf[:, 0, :], -0.25)
-        queries_quantise(early_bf[:].rearrange("p a b -> p (a b)"), aligned([P, 4 * P], U32, "q_early"), ["q0", "q2", "m0", "m2"])
+        queries_round(nc.scalar.copy, late_bf[:, 0, :], 2)
+        queries_round(nc.scalar.copy, late_bf[:, 1, :], 3)
+        nc.vector.tensor_scalar_mul(first_bf[:, 1, :], first_bf[:, 0, :], -0.25)
+        queries_quantise(first_bf[:].rearrange("p a b -> p (a b)"), aligned([P, 2 * P], U32, "q_first"), ["q0", "m0"])
         queries_quantise(apart_bf[:], aligned([P, P], U32, "q_apart"), ["q1"])
         neg_ls = held.tile([P, BLOCKS], F32, name="neg_ls")
         ls_ps = bank(4, [P, P], "ls_ps")
@@ -127,6 +137,11 @@ def tile_attend_at_cfg_topk_kernel(tc, qT, k_words, k_scales, c_words, c_scales,
             return held.tile([P, PLACES, P], F32, name=name)
 
         k_keys = (gather(k_win, U32, aligned([P, N], U32, "k_codes")), k_scale[:])
+        values_load(1)
+        scaled_bf = guest(K_AT, 0, [P, 2, PLACES * P], BF16, "scaled_bf")
+        nc.vector.tensor_scalar_mul(scaled_bf[:], late_bf[:], -0.25)
+        queries_quantise(late_bf[:].rearrange("p a b -> p (a b)"), guest(K_AT, 2, [P, 2 * P], U32, "q_late"), ["q2", "q3"])
+        queries_quantise(scaled_bf[:].rearrange("p a b -> p (a b)"), aligned([P, 2 * P], U32, "q_scaled"), ["m2", "m3"])
         joint = {}
 
         def joint_open(j, bank_number):
@@ -134,15 +149,14 @@ def tile_attend_at_cfg_topk_kernel(tc, qT, k_words, k_scales, c_words, c_scales,
             score_pass(joint[j], f"q{j}", k_keys, True, False)
             score_pass(joint[j], f"m{j}", k_keys, False, False)
 
+        joint_open(0, 0)
         a_ps = bank(1, [P, N], "a_apart")
         score_pass(a_ps, f"q{APART}", k_keys, True, True)
         a_term = planes("a_term")
         nc.scalar.mul(a_term[:], by_place(a_ps), 1.5)
-        joint_open(0, 0)
         joint_open(2, 3)
-        c_scale = gather(cs_win, U8, guest(K_WINDOW, 0, [P, N], U8, "c_scale"))
-        c_keys = (gather(c_win, U32, aligned([P, N], U32, "c_codes")), c_scale[C_SCALE_ROW:P, :])
-        queries_quantise(late_bf[:].rearrange("p a b -> p (a b)"), guest(C_WINDOW, 0, [P, 2 * P], U32, "q_late"), ["q3", "m3"])
+        c_keys = (gather(c_win, U32, aligned([P, N], U32, "c_codes")), c_plane[:].bitcast(U8))
+        values_load(2)
 
         y_scale = aligned([P, NQ], U8, "y_scale")
         v_scale = aligned([P, DV], U8, "v_scale")
@@ -228,37 +242,38 @@ def tile_attend_at_cfg_topk_kernel(tc, qT, k_words, k_scales, c_words, c_scales,
         joint_close(0, 2)
         apart_close(2)
         values_gather(0)
+        values_load(3)
         weights_turn(0, 5)
-        weights_scale(0, 0, 0)
+        weights_scale(0, V_AT[0], 0)
         joint_close(2, 1)
         weights_turn(1, 6)
         weights_turn(2, 7)
         values_turn(0, 4)
         values_gather(1)
-        weights_quantise(0, guest_words(1, 0, "y_codes0"))
-        weights_scale(1, 1, 1)
+        weights_quantise(0, guest_words(V_AT[1], 0, "y_codes0"))
+        weights_scale(1, V_AT[1], 1)
         values_turn(1, 0)
         weights_scale_by_place(2)
         joint_open(3, 5)
         joint_close(3, 1)
         values_gather(2)
         values_turn(2, 2)
-        weights_turn(3, 1)
-        weights_quantise(1, guest_words(2, 0, "y_codes1"))
-        values_quantise(0, guest_words(2, 1, "v_codes0"))
-        weights_quantise(2, guest_words(2, 3, "y_codes2"))
-        values_quantise(1, guest_words(2, 2, "v_codes1"))
+        weights_turn(3, 0)
+        weights_quantise(1, guest_words(V_AT[2], 0, "y_codes1"))
+        values_quantise(0, guest_words(V_AT[2], 1, "v_codes0"))
+        weights_quantise(2, guest_words(V_AT[2], 3, "y_codes2"))
+        values_quantise(1, guest_words(V_AT[2], 2, "v_codes1"))
         early_out = held.tile([P, 3, 2 * P], F32, name="early_out")
         for js, bank_number in (([0, 1], 3), ([2], 6)):
             nc.scalar.copy(early_out[:, js[0] : js[-1] + 1, :], product(js, [0, 1], bank_number)[:])
         nc.sync.dma_start(out_rows[:, 0:3, 0 : 2 * P], early_out[:])
         values_gather(3)
         values_turn(3, 4)
-        values_quantise(2, guest_words(3, 1, "v_codes2"))
-        weights_scale(3, 3, 0)
-        product_and_store([0, 1, 2], [2], 0, nc.scalar.copy, nc.sync)
+        values_quantise(2, guest_words(V_AT[3], 1, "v_codes2"))
+        weights_scale(3, V_AT[3], 0)
+        product_and_store([0, 1, 2], [2], 1, nc.scalar.copy, nc.sync)
         weights_quantise(3, aligned([P, P], U32, "y_codes3"))
-        values_quantise(3, guest_words(3, 0, "v_codes3"))
+        values_quantise(3, guest_words(V_AT[3], 0, "v_codes3"))
         product_and_store([3], [0, 1, 2], 5, nc.scalar.copy, nc.sync)
         product_and_store([0, 1], [3], 2, nc.vector.tensor_copy, nc.sync)
         product_and_store([2, 3], [3], 7, nc.scalar.copy, nc.scalar)

@@ -20,10 +20,9 @@ PLACES = 4
 FLOPS = 2 * 2 * N * D * NQ + 2 * N * NQ * DV
 
 WINDOW_BYTES = 4 * T
-OVERLAP = 64
-CHAIN = WINDOW_BYTES - OVERLAP
-K_AT, C_AT, S_AT = 0, 2 * WINDOW_BYTES, 4 * WINDOW_BYTES
-V_AT = [S_AT + T - OVERLAP, K_AT + CHAIN, C_AT + CHAIN, S_AT + T - OVERLAP + CHAIN]
+V_AT = [e * WINDOW_BYTES for e in range(BLOCKS)]
+K_AT, C_AT, SPARE_AT = 4 * WINDOW_BYTES, 5 * WINDOW_BYTES, 6 * WINDOW_BYTES
+C_SCALE_ROW = 4
 GUEST_BYTES = 1024
 BANK_BYTES = 2048
 APART = 1
@@ -46,16 +45,13 @@ def tile_attend_at_cfg_topk_kernel(tc, qT, k_words, k_scales, c_words, c_scales,
             return held.tile(shape, dtype, name=name, align_bytes=64)
 
         offsets = held.tile([P, N // 16], U16, name="offsets")
-        nc.sync.dma_start(offsets[:], offs)
         ident = held.tile([P, P], F32, name="ident")
         ks_win = held.tile([P, T // 4], I32, name="ks_win")
-        cs_win = reused.tile([P, T // 4], I32, name="cs_win", offset=S_AT)
-        c_plane = aligned([P, N // 4], I32, "c_plane")
+        cs_win = held.tile([P, T // 4], I32, name="cs_win")
         ls_rows = held.tile([P, P], F32, name="ls_rows")
         nc.vector.memset(ks_win[:], 0)
         nc.vector.memset(ls_rows[:], 0.0)
         nc.vector.memset(cs_win[:], 0)
-        nc.vector.memset(c_plane[:], 0)
         make_identity(nc, ident[:])
         warm = held.tile([P, 8], F32, name="warm")
         nc.scalar.activation(warm[32:64, 0:1], ls_rows[32:64, 0:1], ACT.Exp)
@@ -73,30 +69,23 @@ def tile_attend_at_cfg_topk_kernel(tc, qT, k_words, k_scales, c_words, c_scales,
         q_raw = held.tile([P, PLACES, NQ], F32, name="q_raw")
         q_rows = qT[0].rearrange("(p t) q -> p t q", t=PLACES)
         nc.sync.dma_start(q_raw[:, 0:2, :], q_rows[:, 0:2, :])
+        nc.sync.dma_start(offsets[:], offs)
         load_scales(ks_win, k_scales, 0)
         nc.sync.dma_start(q_raw[:, 2:4, :], q_rows[:, 2:4, :])
-        nc.sync.dma_start(cs_win[0:P:8, :], c_scales[0].bitcast(I32))
         k_win = load_words(k_words, K_AT, "k_win")
         nc.sync.dma_start(ls_rows[0:BLOCKS, :], ls[0, 0].rearrange("(j m) -> j m", j=BLOCKS))
+        load_scales(cs_win, c_scales, C_SCALE_ROW)
         c_win = load_words(c_words, C_AT, "c_win")
+        us_sb = held.tile([P, PLACES], F32, name="us_sb")
+        v_win = [reused.tile([P, T], F32, name=f"v_win{e}", offset=V_AT[e]) for e in range(BLOCKS)]
+        nc.sync.dma_start(v_win[0][:], vT[0:P, :])
+        nc.sync.dma_start(us_sb[:], us[0].rearrange("(p t) o -> p (t o)", t=PLACES))
+        for e in range(1, BLOCKS):
+            nc.sync.dma_start(v_win[e][:], vT[e * P : (e + 1) * P, :])
 
         def gather(win, dtype, picked):
             nc.vector.tensor_copy(picked[:], win[:].bitcast(dtype).indirect(offsets[:]))
             return picked
-
-        k_scale = gather(ks_win, U8, aligned([P, N], U8, "k_scale"))
-        c_rows = gather(cs_win, U8, held.tile([P, N], U8, name="c_rows"))[:].bitcast(I32)
-        for r in range(4):
-            nc.sync.dma_start(c_plane[r:P:32, :], c_rows[8 * r : P : 32, :])
-        us_sb = held.tile([P, PLACES], F32, name="us_sb")
-        v_win = {}
-
-        def values_load(e):
-            v_win[e] = reused.tile([P, T], F32, name=f"v_win{e}", offset=V_AT[e])
-            nc.sync.dma_start(v_win[e][:], vT[e * P : (e + 1) * P, :])
-
-        values_load(0)
-        nc.sync.dma_start(us_sb[:], us[0].rearrange("(p t) o -> p (t o)", t=PLACES))
 
         q_turned = q_raw[:].rearrange("p t q -> p q t")
         q_words, q_scales = {}, {}
@@ -110,16 +99,17 @@ def tile_attend_at_cfg_topk_kernel(tc, qT, k_words, k_scales, c_words, c_scales,
             for n, name in enumerate(names):
                 q_words[name], q_scales[name] = codes[:, n * P : (n + 1) * P], scale[:, n * P : (n + 1) * P]
 
-        first_bf = aligned([P, 2, PLACES * P], BF16, "first_bf")
+        k_scale = gather(ks_win, U8, aligned([P, N], U8, "k_scale"))
+        early_bf = aligned([P, 4, PLACES * P], BF16, "early_bf")
         apart_bf = aligned([P, PLACES * P], BF16, "apart_bf")
         late_bf = aligned([P, 2, PLACES * P], BF16, "late_bf")
-        queries_round(nc.scalar.copy, first_bf[:, 0, :], 0)
+        queries_round(nc.vector.tensor_copy, early_bf[:, 0, :], 0)
+        queries_round(nc.scalar.copy, early_bf[:, 1, :], 2)
         queries_round(nc.scalar.copy, apart_bf[:], APART)
-        queries_round(nc.scalar.copy, late_bf[:, 0, :], 2)
-        queries_round(nc.scalar.copy, late_bf[:, 1, :], 3)
-        nc.vector.tensor_scalar_mul(first_bf[:, 1, :], first_bf[:, 0, :], -0.25)
-        queries_quantise(first_bf[:].rearrange("p a b -> p (a b)"), aligned([P, 2 * P], U32, "q_first"), ["q0", "m0"])
-        queries_quantise(apart_bf[:], aligned([P, P], U32, "q_apart"), ["q1"])
+        queries_round(nc.scalar.copy, late_bf[:, 0, :], 3)
+        nc.vector.tensor_scalar_mul(early_bf[:, 2:4, :], early_bf[:, 0:2, :], -0.25)
+        nc.scalar.mul(late_bf[:, 1, :], late_bf[:, 0, :], -0.25)
+        queries_quantise(early_bf[:].rearrange("p a b -> p (a b)"), aligned([P, 4 * P], U32, "q_early"), ["q0", "q2", "m0", "m2"])
         neg_ls = held.tile([P, BLOCKS], F32, name="neg_ls")
         ls_ps = bank(4, [P, P], "ls_ps")
         nc.tensor.transpose(ls_ps[:], ls_rows[:], ident[:])
@@ -137,11 +127,6 @@ def tile_attend_at_cfg_topk_kernel(tc, qT, k_words, k_scales, c_words, c_scales,
             return held.tile([P, PLACES, P], F32, name=name)
 
         k_keys = (gather(k_win, U32, aligned([P, N], U32, "k_codes")), k_scale[:])
-        values_load(1)
-        scaled_bf = guest(K_AT, 0, [P, 2, PLACES * P], BF16, "scaled_bf")
-        nc.vector.tensor_scalar_mul(scaled_bf[:], late_bf[:], -0.25)
-        queries_quantise(late_bf[:].rearrange("p a b -> p (a b)"), guest(K_AT, 2, [P, 2 * P], U32, "q_late"), ["q2", "q3"])
-        queries_quantise(scaled_bf[:].rearrange("p a b -> p (a b)"), aligned([P, 2 * P], U32, "q_scaled"), ["m2", "m3"])
         joint = {}
 
         def joint_open(j, bank_number):
@@ -150,13 +135,11 @@ def tile_attend_at_cfg_topk_kernel(tc, qT, k_words, k_scales, c_words, c_scales,
             score_pass(joint[j], f"m{j}", k_keys, False, False)
 
         joint_open(0, 0)
-        a_ps = bank(1, [P, N], "a_apart")
-        score_pass(a_ps, f"q{APART}", k_keys, True, True)
-        a_term = planes("a_term")
-        nc.scalar.mul(a_term[:], by_place(a_ps), 1.5)
         joint_open(2, 3)
-        c_keys = (gather(c_win, U32, aligned([P, N], U32, "c_codes")), c_plane[:].bitcast(U8))
-        values_load(2)
+        c_scale = gather(cs_win, U8, guest(K_AT, 0, [P, N], U8, "c_scale"))
+        c_keys = (gather(c_win, U32, aligned([P, N], U32, "c_codes")), c_scale[C_SCALE_ROW:P, :])
+        queries_quantise(apart_bf[:], guest(C_AT, 1, [P, P], U32, "q_apart"), ["q1"])
+        queries_quantise(late_bf[:].rearrange("p a b -> p (a b)"), guest(C_AT, 0, [P, 2 * P], U32, "q_late"), ["q3", "m3"])
 
         y_scale = aligned([P, NQ], U8, "y_scale")
         v_scale = aligned([P, DV], U8, "v_scale")
@@ -171,7 +154,11 @@ def tile_attend_at_cfg_topk_kernel(tc, qT, k_words, k_scales, c_words, c_scales,
                 nc.scalar.activation(exp_sb[:, part, :], by_place(joint[j])[:, part, :], ACT.Exp, bias=neg_ls[:, j : j + 1], scale=2.0)
             to_turn[j] = [exp_sb]
 
-        def apart_close(bank_number):
+        def apart_scores(a_bank, bank_number):
+            a_ps = bank(a_bank, [P, N], "a_apart")
+            score_pass(a_ps, f"q{APART}", k_keys, True, True)
+            a_term = planes("a_term")
+            nc.scalar.mul(a_term[:], by_place(a_ps), 1.5)
             z_ps = bank(bank_number, [P, N], "z_apart")
             score_pass(z_ps, f"q{APART}", c_keys, True, True)
             z_term = planes("z_term")
@@ -195,8 +182,12 @@ def tile_attend_at_cfg_topk_kernel(tc, qT, k_words, k_scales, c_words, c_scales,
             y_bf[j] = guest(window, room, [P, P, PLACES], BF16, f"y_bf{j}")
             nc.vector.tensor_tensor(y_bf[j][:], exps[j], us_places, ALU.mult)
 
-        def weights_scale_by_place(j):
-            y_bf[j] = aligned([P, P, PLACES], BF16, f"y_bf{j}")
+        def weights_scale_aside(j, rounded):
+            y_bf[j] = rounded
+            nc.gpsimd.tensor_tensor(y_bf[j][:], exps[j], us_places, ALU.mult)
+
+        def weights_scale_by_place(j, rounded):
+            y_bf[j] = rounded
             for t in range(PLACES):
                 nc.scalar.activation(y_bf[j][:, :, t], exps[j][:, :, t], ACT.Copy, scale=us_sb[:, t : t + 1])
 
@@ -204,16 +195,16 @@ def tile_attend_at_cfg_topk_kernel(tc, qT, k_words, k_scales, c_words, c_scales,
             y_codes[j] = codes
             nc.vector.quantize_mx(codes[:].bitcast(FP8X4), y_scale[:, j * P : (j + 1) * P], y_bf[j][:].rearrange("p q t -> p (q t)"))
 
-        def values_gather(e):
-            v_picked[e] = held.tile([P, N], BF16, name=f"v_picked{e}")
+        def values_gather(e, picked):
+            v_picked[e] = picked
             nc.vector.tensor_copy(v_picked[e][:], v_win[e][:].indirect(offsets[:]))
 
-        def values_turn(e, bank_number):
+        def values_turn(e, bank_number, turned):
             pairs = v_picked[e][:].bitcast(F32)
             ps = bank(bank_number, [P, 2, P], f"v{e}")
             for u in range(2):
                 nc.tensor.transpose(ps[:, u, :], pairs[:, u : 2 * P : 2], ident[:])
-            v_bf[e] = aligned([P, PLACES * P], BF16, f"v_bf{e}")
+            v_bf[e] = turned
             nc.scalar.copy(v_bf[e][:].bitcast(F32).rearrange("p (e u) -> p e u", u=2), ps[:].rearrange("p u e -> p e u"))
 
         def values_quantise(e, codes):
@@ -239,41 +230,43 @@ def tile_attend_at_cfg_topk_kernel(tc, qT, k_words, k_scales, c_words, c_scales,
             copy(staged[:], product(js, es, bank_number)[:])
             queue.dma_start(out_rows[:, js[0] : js[-1] + 1, es[0] * P : (es[-1] + 1) * P], staged[:])
 
+        def own(name):
+            return aligned([P, N], BF16, name)
+
         joint_close(0, 2)
-        apart_close(2)
-        values_gather(0)
-        values_load(3)
-        weights_turn(0, 5)
-        weights_scale(0, V_AT[0], 0)
         joint_close(2, 1)
-        weights_turn(1, 6)
-        weights_turn(2, 7)
-        values_turn(0, 4)
-        values_gather(1)
-        weights_quantise(0, guest_words(V_AT[1], 0, "y_codes0"))
-        weights_scale(1, V_AT[1], 1)
-        values_turn(1, 0)
-        weights_scale_by_place(2)
-        joint_open(3, 5)
+        apart_scores(1, 2)
+        values_gather(0, own("v_picked0"))
+        weights_turn(0, 5)
+        weights_scale(0, SPARE_AT, 0)
+        joint_open(3, 0)
         joint_close(3, 1)
-        values_gather(2)
-        values_turn(2, 2)
-        weights_turn(3, 0)
-        weights_quantise(1, guest_words(V_AT[2], 0, "y_codes1"))
-        values_quantise(0, guest_words(V_AT[2], 1, "v_codes0"))
-        weights_quantise(2, guest_words(V_AT[2], 3, "y_codes2"))
-        values_quantise(1, guest_words(V_AT[2], 2, "v_codes1"))
+        weights_turn(2, 7)
+        weights_turn(1, 6)
+        values_turn(0, 2, own("v_bf0"))
+        values_gather(1, guest(SPARE_AT, 1, [P, N], BF16, "v_picked1"))
+        weights_scale(2, V_AT[1], 0)
+        weights_quantise(0, guest_words(V_AT[1], 1, "y_codes0"))
+        weights_scale_aside(1, guest(SPARE_AT, 0, [P, P, PLACES], BF16, "y_bf1"))
+        weights_turn(3, 1)
+        values_turn(1, 4, own("v_bf1"))
+        weights_scale_by_place(3, guest(SPARE_AT, 1, [P, P, PLACES], BF16, "y_bf3"))
+        values_gather(2, own("v_picked2"))
+        values_turn(2, 3, own("v_bf2"))
+        weights_quantise(2, guest_words(V_AT[2], 0, "y_codes2"))
+        values_quantise(0, guest_words(V_AT[2], 3, "v_codes0"))
+        values_quantise(1, guest_words(V_AT[2], 1, "v_codes1"))
+        weights_quantise(1, guest_words(V_AT[2], 2, "y_codes1"))
         early_out = held.tile([P, 3, 2 * P], F32, name="early_out")
-        for js, bank_number in (([0, 1], 3), ([2], 6)):
+        for js, bank_number in (([0, 1], 0), ([2], 5)):
             nc.scalar.copy(early_out[:, js[0] : js[-1] + 1, :], product(js, [0, 1], bank_number)[:])
         nc.sync.dma_start(out_rows[:, 0:3, 0 : 2 * P], early_out[:])
-        values_gather(3)
-        values_turn(3, 4)
+        values_gather(3, own("v_picked3"))
+        values_turn(3, 4, own("v_bf3"))
         values_quantise(2, guest_words(V_AT[3], 1, "v_codes2"))
-        weights_scale(3, V_AT[3], 0)
-        product_and_store([0, 1, 2], [2], 1, nc.scalar.copy, nc.sync)
-        weights_quantise(3, aligned([P, P], U32, "y_codes3"))
+        weights_quantise(3, guest_words(V_AT[3], 2, "y_codes3"))
+        product_and_store([0, 1, 2], [2], 6, nc.scalar.copy, nc.sync)
+        product_and_store([3], [0, 1, 2], 7, nc.scalar.copy, nc.sync)
         values_quantise(3, guest_words(V_AT[3], 0, "v_codes3"))
-        product_and_store([3], [0, 1, 2], 5, nc.scalar.copy, nc.sync)
         product_and_store([0, 1], [3], 2, nc.vector.tensor_copy, nc.sync)
-        product_and_store([2, 3], [3], 7, nc.scalar.copy, nc.scalar)
+        product_and_store([2, 3], [3], 3, nc.scalar.copy, nc.scalar)

@@ -20,9 +20,12 @@ PLACES = 4
 FLOPS = 2 * 2 * N * D * NQ + 2 * N * NQ * DV
 
 WINDOW_BYTES = 4 * T
-V_AT = [e * WINDOW_BYTES for e in range(BLOCKS)]
-K_AT, C_AT, SPARE_AT = 4 * WINDOW_BYTES, 5 * WINDOW_BYTES, 6 * WINDOW_BYTES
-C_SCALE_ROW = 4
+OVERLAP = 64
+CHAIN = WINDOW_BYTES - OVERLAP
+K_AT, C_AT, S_AT = 0, 2 * WINDOW_BYTES, 4 * WINDOW_BYTES
+V_AT = [S_AT + T - OVERLAP, K_AT + CHAIN, C_AT + CHAIN, S_AT + T - OVERLAP + CHAIN]
+ROWS_AT = 7 * WINDOW_BYTES
+SPARE_AT = ROWS_AT + 2048
 GUEST_BYTES = 1024
 BANK_BYTES = 2048
 APART = 1
@@ -47,11 +50,13 @@ def tile_attend_at_cfg_topk_kernel(tc, qT, k_words, k_scales, c_words, c_scales,
         offsets = held.tile([P, N // 16], U16, name="offsets")
         ident = held.tile([P, P], F32, name="ident")
         ks_win = held.tile([P, T // 4], I32, name="ks_win")
-        cs_win = held.tile([P, T // 4], I32, name="cs_win")
+        cs_win = reused.tile([P, T // 4], I32, name="cs_win", offset=S_AT)
+        c_plane = aligned([P, N // 4], I32, "c_plane")
         ls_rows = held.tile([P, P], F32, name="ls_rows")
         nc.vector.memset(ks_win[:], 0)
         nc.vector.memset(ls_rows[:], 0.0)
         nc.vector.memset(cs_win[:], 0)
+        nc.vector.memset(c_plane[:], 0)
         make_identity(nc, ident[:])
         warm = held.tile([P, 8], F32, name="warm")
         nc.scalar.activation(warm[32:64, 0:1], ls_rows[32:64, 0:1], ACT.Exp)
@@ -71,21 +76,29 @@ def tile_attend_at_cfg_topk_kernel(tc, qT, k_words, k_scales, c_words, c_scales,
         nc.sync.dma_start(q_raw[:, 0:2, :], q_rows[:, 0:2, :])
         nc.sync.dma_start(offsets[:], offs)
         load_scales(ks_win, k_scales, 0)
-        nc.sync.dma_start(q_raw[:, 2:4, :], q_rows[:, 2:4, :])
+        nc.sync.dma_start(cs_win[0:P:8, :], c_scales[0].bitcast(I32))
         k_win = load_words(k_words, K_AT, "k_win")
+        nc.sync.dma_start(q_raw[:, 2:4, :], q_rows[:, 2:4, :])
         nc.sync.dma_start(ls_rows[0:BLOCKS, :], ls[0, 0].rearrange("(j m) -> j m", j=BLOCKS))
-        load_scales(cs_win, c_scales, C_SCALE_ROW)
         c_win = load_words(c_words, C_AT, "c_win")
-        us_sb = held.tile([P, PLACES], F32, name="us_sb")
-        v_win = [reused.tile([P, T], F32, name=f"v_win{e}", offset=V_AT[e]) for e in range(BLOCKS)]
-        nc.sync.dma_start(v_win[0][:], vT[0:P, :])
-        nc.sync.dma_start(us_sb[:], us[0].rearrange("(p t) o -> p (t o)", t=PLACES))
-        for e in range(1, BLOCKS):
-            nc.sync.dma_start(v_win[e][:], vT[e * P : (e + 1) * P, :])
 
         def gather(win, dtype, picked):
             nc.vector.tensor_copy(picked[:], win[:].bitcast(dtype).indirect(offsets[:]))
             return picked
+
+        k_scale = gather(ks_win, U8, aligned([P, N], U8, "k_scale"))
+        c_rows = gather(cs_win, U8, guest(ROWS_AT, 0, [P, N], U8, "c_rows"))[:].bitcast(I32)
+        for r in range(4):
+            nc.sync.dma_start(c_plane[r:P:32, :], c_rows[8 * r : P : 32, :])
+        us_sb = held.tile([P, PLACES], F32, name="us_sb")
+        v_win = {}
+
+        def values_load(e):
+            v_win[e] = reused.tile([P, T], F32, name=f"v_win{e}", offset=V_AT[e])
+            nc.sync.dma_start(v_win[e][:], vT[e * P : (e + 1) * P, :])
+
+        values_load(0)
+        nc.sync.dma_start(us_sb[:], us[0].rearrange("(p t) o -> p (t o)", t=PLACES))
 
         q_turned = q_raw[:].rearrange("p t q -> p q t")
         q_words, q_scales = {}, {}
@@ -99,17 +112,21 @@ def tile_attend_at_cfg_topk_kernel(tc, qT, k_words, k_scales, c_words, c_scales,
             for n, name in enumerate(names):
                 q_words[name], q_scales[name] = codes[:, n * P : (n + 1) * P], scale[:, n * P : (n + 1) * P]
 
-        k_scale = gather(ks_win, U8, aligned([P, N], U8, "k_scale"))
-        early_bf = aligned([P, 4, PLACES * P], BF16, "early_bf")
+        k_keys = (gather(k_win, U32, aligned([P, N], U32, "k_codes")), k_scale[:])
+        values_load(1)
+        first_bf = aligned([P, 2, PLACES * P], BF16, "first_bf")
+        second_bf = aligned([P, 2, PLACES * P], BF16, "second_bf")
         apart_bf = aligned([P, PLACES * P], BF16, "apart_bf")
         late_bf = aligned([P, 2, PLACES * P], BF16, "late_bf")
-        queries_round(nc.vector.tensor_copy, early_bf[:, 0, :], 0)
-        queries_round(nc.scalar.copy, early_bf[:, 1, :], 2)
+        queries_round(nc.vector.tensor_copy, first_bf[:, 0, :], 0)
+        nc.scalar.mul(first_bf[:, 1, :].rearrange("p (q t) -> p q t", t=PLACES), q_turned[:, 0:P, :], -0.25)
+        queries_round(nc.scalar.copy, second_bf[:, 0, :], 2)
         queries_round(nc.scalar.copy, apart_bf[:], APART)
         queries_round(nc.scalar.copy, late_bf[:, 0, :], 3)
-        nc.vector.tensor_scalar_mul(early_bf[:, 2:4, :], early_bf[:, 0:2, :], -0.25)
         nc.scalar.mul(late_bf[:, 1, :], late_bf[:, 0, :], -0.25)
-        queries_quantise(early_bf[:].rearrange("p a b -> p (a b)"), aligned([P, 4 * P], U32, "q_early"), ["q0", "q2", "m0", "m2"])
+        queries_quantise(first_bf[:].rearrange("p a b -> p (a b)"), aligned([P, 2 * P], U32, "q_first"), ["q0", "m0"])
+        nc.vector.tensor_scalar_mul(second_bf[:, 1, :], second_bf[:, 0, :], -0.25)
+        queries_quantise(second_bf[:].rearrange("p a b -> p (a b)"), aligned([P, 2 * P], U32, "q_second"), ["q2", "m2"])
         neg_ls = held.tile([P, BLOCKS], F32, name="neg_ls")
         ls_ps = bank(4, [P, P], "ls_ps")
         nc.tensor.transpose(ls_ps[:], ls_rows[:], ident[:])
@@ -126,7 +143,6 @@ def tile_attend_at_cfg_topk_kernel(tc, qT, k_words, k_scales, c_words, c_scales,
         def planes(name):
             return held.tile([P, PLACES, P], F32, name=name)
 
-        k_keys = (gather(k_win, U32, aligned([P, N], U32, "k_codes")), k_scale[:])
         joint = {}
 
         def joint_open(j, bank_number):
@@ -136,10 +152,10 @@ def tile_attend_at_cfg_topk_kernel(tc, qT, k_words, k_scales, c_words, c_scales,
 
         joint_open(0, 0)
         joint_open(2, 3)
-        c_scale = gather(cs_win, U8, guest(K_AT, 0, [P, N], U8, "c_scale"))
-        c_keys = (gather(c_win, U32, aligned([P, N], U32, "c_codes")), c_scale[C_SCALE_ROW:P, :])
-        queries_quantise(apart_bf[:], guest(C_AT, 1, [P, P], U32, "q_apart"), ["q1"])
-        queries_quantise(late_bf[:].rearrange("p a b -> p (a b)"), guest(C_AT, 0, [P, 2 * P], U32, "q_late"), ["q3", "m3"])
+        c_keys = (gather(c_win, U32, aligned([P, N], U32, "c_codes")), c_plane[:].bitcast(U8))
+        values_load(2)
+        queries_quantise(apart_bf[:], guest(ROWS_AT - 256, 0, [P, P], U32, "q_apart"), ["q1"])
+        queries_quantise(late_bf[:].rearrange("p a b -> p (a b)"), guest(ROWS_AT + 256, 0, [P, 2 * P], U32, "q_late"), ["q3", "m3"])
 
         y_scale = aligned([P, NQ], U8, "y_scale")
         v_scale = aligned([P, DV], U8, "v_scale")
@@ -205,30 +221,33 @@ def tile_attend_at_cfg_topk_kernel(tc, qT, k_words, k_scales, c_words, c_scales,
             for u in range(2):
                 nc.tensor.transpose(ps[:, u, :], pairs[:, u : 2 * P : 2], ident[:])
             v_bf[e] = turned
-            nc.scalar.copy(v_bf[e][:].bitcast(F32).rearrange("p (e u) -> p e u", u=2), ps[:].rearrange("p u e -> p e u"))
+            nc.scalar.copy(v_bf[e].bitcast(F32).rearrange("p (e u) -> p e u", u=2), ps[:].rearrange("p u e -> p e u"))
 
         def values_quantise(e, codes):
             v_codes[e] = codes
-            nc.vector.quantize_mx(codes[:].bitcast(FP8X4), v_scale[:, e * P : (e + 1) * P], v_bf[e][:])
+            nc.vector.quantize_mx(codes[:].bitcast(FP8X4), v_scale[:, e * P : (e + 1) * P], v_bf[e])
 
         def guest_words(window, room, name):
             return guest(window, room, [P, P], U32, name)
 
         out_rows = out[0].rearrange("(j m) e -> m j e", m=P)
 
-        def product(js, es, bank_number):
-            ps = bank(bank_number, [P, len(js), len(es) * P], f"out_ps{js[0]}{es[0]}")
+        def product(ps, j, codes, first):
+            width = codes.shape[1]
+            nc.tensor.matmul_mx(ps, lhsT=y_codes[j][:].bitcast(FP8X4), lhsT_scale=y_scale[:, j * P : (j + 1) * P],
+                                rhs=codes.bitcast(FP8X4), rhs_scale=v_scale[:, first : first + width], start=True, stop=True)
+
+        def products(js, codes, first, bank_number):
+            ps = bank(bank_number, [P, len(js), codes.shape[1]], f"out_ps{js[0]}_{first}")
             for n, j in enumerate(js):
-                for m, e in enumerate(es):
-                    nc.tensor.matmul_mx(ps[:, n, m * P : (m + 1) * P], lhsT=y_codes[j][:].bitcast(FP8X4),
-                                        lhsT_scale=y_scale[:, j * P : (j + 1) * P], rhs=v_codes[e][:].bitcast(FP8X4),
-                                        rhs_scale=v_scale[:, e * P : (e + 1) * P], start=True, stop=True)
+                product(ps[:, n, :], j, codes, first)
             return ps
 
-        def product_and_store(js, es, bank_number, copy, queue):
-            staged = held.tile([P, len(js), len(es) * P], F32, name=f"out{js[0]}{es[0]}")
-            copy(staged[:], product(js, es, bank_number)[:])
-            queue.dma_start(out_rows[:, js[0] : js[-1] + 1, es[0] * P : (es[-1] + 1) * P], staged[:])
+        def store(ps, js, first, copy, queue):
+            width = ps.shape[2]
+            staged = held.tile([P, len(js), width], F32, name=f"out{js[0]}_{first}")
+            copy(staged[:], ps[:])
+            queue.dma_start(out_rows[:, js[0] : js[-1] + 1, first : first + width], staged[:])
 
         def own(name):
             return aligned([P, N], BF16, name)
@@ -237,36 +256,41 @@ def tile_attend_at_cfg_topk_kernel(tc, qT, k_words, k_scales, c_words, c_scales,
         joint_close(2, 1)
         apart_scores(1, 2)
         values_gather(0, own("v_picked0"))
+        values_load(3)
         weights_turn(0, 5)
         weights_scale(0, SPARE_AT, 0)
         joint_open(3, 0)
         joint_close(3, 1)
         weights_turn(2, 7)
         weights_turn(1, 6)
-        values_turn(0, 2, own("v_bf0"))
+        v01_bf = aligned([P, 2, N], BF16, "v01_bf")
+        values_turn(0, 2, v01_bf[:, 0, :])
         values_gather(1, guest(SPARE_AT, 1, [P, N], BF16, "v_picked1"))
         weights_scale(2, V_AT[1], 0)
         weights_quantise(0, guest_words(V_AT[1], 1, "y_codes0"))
         weights_scale_aside(1, guest(SPARE_AT, 0, [P, P, PLACES], BF16, "y_bf1"))
         weights_turn(3, 1)
-        values_turn(1, 4, own("v_bf1"))
+        values_turn(1, 4, v01_bf[:, 1, :])
         weights_scale_by_place(3, guest(SPARE_AT, 1, [P, P, PLACES], BF16, "y_bf3"))
         values_gather(2, own("v_picked2"))
-        values_turn(2, 3, own("v_bf2"))
+        values_turn(2, 3, own("v_bf2")[:])
         weights_quantise(2, guest_words(V_AT[2], 0, "y_codes2"))
-        values_quantise(0, guest_words(V_AT[2], 3, "v_codes0"))
-        values_quantise(1, guest_words(V_AT[2], 1, "v_codes1"))
+        v01_codes = guest(V_AT[2], 3, [P, 2 * P], U32, "v01_codes")
+        nc.vector.quantize_mx(v01_codes[:].bitcast(FP8X4), v_scale[:, 0 : 2 * P], v01_bf[:].rearrange("p a b -> p (a b)"))
         weights_quantise(1, guest_words(V_AT[2], 2, "y_codes1"))
         early_out = held.tile([P, 3, 2 * P], F32, name="early_out")
         for js, bank_number in (([0, 1], 0), ([2], 5)):
-            nc.scalar.copy(early_out[:, js[0] : js[-1] + 1, :], product(js, [0, 1], bank_number)[:])
+            nc.scalar.copy(early_out[:, js[0] : js[-1] + 1, :], products(js, v01_codes[:], 0, bank_number)[:])
         nc.sync.dma_start(out_rows[:, 0:3, 0 : 2 * P], early_out[:])
         values_gather(3, own("v_picked3"))
-        values_turn(3, 4, own("v_bf3"))
+        values_turn(3, 4, own("v_bf3")[:])
         values_quantise(2, guest_words(V_AT[3], 1, "v_codes2"))
         weights_quantise(3, guest_words(V_AT[3], 2, "y_codes3"))
-        product_and_store([0, 1, 2], [2], 6, nc.scalar.copy, nc.sync)
-        product_and_store([3], [0, 1, 2], 7, nc.scalar.copy, nc.sync)
+        store(products([0, 1, 2], v_codes[2][:], 2 * P, 6), [0, 1, 2], 2 * P, nc.scalar.copy, nc.sync)
+        rest_ps = bank(7, [P, 1, 3 * P], "rest_ps")
+        product(rest_ps[:, 0, 0 : 2 * P], 3, v01_codes[:], 0)
+        product(rest_ps[:, 0, 2 * P : 3 * P], 3, v_codes[2][:], 2 * P)
+        store(rest_ps, [3], 0, nc.scalar.copy, nc.sync)
         values_quantise(3, guest_words(V_AT[3], 0, "v_codes3"))
-        product_and_store([0, 1], [3], 2, nc.vector.tensor_copy, nc.sync)
-        product_and_store([2, 3], [3], 3, nc.scalar.copy, nc.scalar)
+        store(products([0, 1], v_codes[3][:], 3 * P, 2), [0, 1], 3 * P, nc.vector.tensor_copy, nc.sync)
+        store(products([2, 3], v_codes[3][:], 3 * P, 3), [2, 3], 3 * P, nc.scalar.copy, nc.scalar)

@@ -28,6 +28,8 @@ ROWS_AT = 7 * WINDOW_BYTES
 SPARE_AT = ROWS_AT + 2048
 GUEST_BYTES = 1024
 BANK_BYTES = 2048
+C_ROW = 8
+LS_ROW = 16
 APART = 1
 
 
@@ -76,10 +78,10 @@ def tile_attend_at_cfg_topk_kernel(tc, qT, k_words, k_scales, c_words, c_scales,
         nc.sync.dma_start(q_raw[:, 0:2, :], q_rows[:, 0:2, :])
         nc.sync.dma_start(offsets[:], offs)
         load_scales(ks_win, k_scales, 0)
-        nc.sync.dma_start(cs_win[0:P:8, :], c_scales[0].bitcast(I32))
+        nc.sync.dma_start(cs_win[4:P:8, :], c_scales[0].bitcast(I32))
         k_win = load_words(k_words, K_AT, "k_win")
         nc.sync.dma_start(q_raw[:, 2:4, :], q_rows[:, 2:4, :])
-        nc.sync.dma_start(ls_rows[0:BLOCKS, :], ls[0, 0].rearrange("(j m) -> j m", j=BLOCKS))
+        nc.sync.dma_start(ls_rows[LS_ROW : LS_ROW + BLOCKS, :], ls[0, 0].rearrange("(j m) -> j m", j=BLOCKS))
         c_win = load_words(c_words, C_AT, "c_win")
 
         def gather(win, dtype, picked):
@@ -89,7 +91,7 @@ def tile_attend_at_cfg_topk_kernel(tc, qT, k_words, k_scales, c_words, c_scales,
         k_scale = gather(ks_win, U8, aligned([P, N], U8, "k_scale"))
         c_rows = gather(cs_win, U8, guest(ROWS_AT, 0, [P, N], U8, "c_rows"))[:].bitcast(I32)
         for r in range(4):
-            nc.sync.dma_start(c_plane[r:P:32, :], c_rows[8 * r : P : 32, :])
+            nc.sync.dma_start(c_plane[C_ROW + r : P : 32, :], c_rows[4 + 8 * r : P : 32, :])
         us_sb = held.tile([P, PLACES], F32, name="us_sb")
         v_win = {}
 
@@ -130,7 +132,7 @@ def tile_attend_at_cfg_topk_kernel(tc, qT, k_words, k_scales, c_words, c_scales,
         neg_ls = held.tile([P, BLOCKS], F32, name="neg_ls")
         ls_ps = bank(4, [P, P], "ls_ps")
         nc.tensor.transpose(ls_ps[:], ls_rows[:], ident[:])
-        nc.scalar.mul(neg_ls[:], ls_ps[:, 0:BLOCKS], -1.0)
+        nc.scalar.mul(neg_ls[:], ls_ps[:, LS_ROW : LS_ROW + BLOCKS], -1.0)
 
         def score_pass(ps, queries, keys, start, stop):
             codes, scale = keys
@@ -152,7 +154,7 @@ def tile_attend_at_cfg_topk_kernel(tc, qT, k_words, k_scales, c_words, c_scales,
 
         joint_open(0, 0)
         joint_open(2, 3)
-        c_keys = (gather(c_win, U32, aligned([P, N], U32, "c_codes")), c_plane[:].bitcast(U8))
+        c_keys = (gather(c_win, U32, aligned([P, N], U32, "c_codes")), c_plane[C_ROW:P, :].bitcast(U8))
         values_load(2)
         queries_quantise(apart_bf[:], guest(ROWS_AT - 256, 0, [P, P], U32, "q_apart"), ["q1"])
         queries_quantise(late_bf[:].rearrange("p a b -> p (a b)"), guest(ROWS_AT + 256, 0, [P, 2 * P], U32, "q_late"), ["q3", "m3"])

@@ -20,17 +20,15 @@ PLACES = 4
 FLOPS = 2 * 2 * N * D * NQ + 2 * N * NQ * DV
 
 WINDOW_BYTES = 4 * T
-OVERLAP = 64
-CHAIN = WINDOW_BYTES - OVERLAP
-K_AT, C_AT, S_AT = 0, 2 * WINDOW_BYTES, 4 * WINDOW_BYTES
-V_AT = [S_AT + T - OVERLAP, K_AT + CHAIN, C_AT + CHAIN, S_AT + T - OVERLAP + CHAIN]
-ROWS_AT = 7 * WINDOW_BYTES
-SPARE_AT = ROWS_AT + 2048
-GUEST_BYTES = 1024
+C_AT = 0
+V_AT = [WINDOW_BYTES * (1 + e) for e in range(BLOCKS)]
+LAST_AT = 5 * WINDOW_BYTES
+EXPONENT_AT = LAST_AT + 2048
+ROOM = 2048
 BANK_BYTES = 2048
 C_ROW = 8
 LS_ROW = 16
-APART = 1
+APART = 2
 
 
 def tile_attend_at_cfg_topk_kernel(tc, qT, k_words, k_scales, c_words, c_scales, vT, ls, us, offs, out):
@@ -43,8 +41,8 @@ def tile_attend_at_cfg_topk_kernel(tc, qT, k_words, k_scales, c_words, c_scales,
         def bank(number, shape, name):
             return psum.tile(shape, F32, name=name, offset=number * BANK_BYTES)
 
-        def guest(window, room, shape, dtype, name):
-            return reused.tile(shape, dtype, name=name, offset=window + room * GUEST_BYTES, align_bytes=64)
+        def guest(at, shape, dtype, name):
+            return reused.tile(shape, dtype, name=name, offset=at, align_bytes=64)
 
         def aligned(shape, dtype, name):
             return held.tile(shape, dtype, name=name, align_bytes=64)
@@ -52,13 +50,11 @@ def tile_attend_at_cfg_topk_kernel(tc, qT, k_words, k_scales, c_words, c_scales,
         offsets = held.tile([P, N // 16], U16, name="offsets")
         ident = held.tile([P, P], F32, name="ident")
         ks_win = held.tile([P, T // 4], I32, name="ks_win")
-        cs_win = reused.tile([P, T // 4], I32, name="cs_win", offset=S_AT)
-        c_plane = aligned([P, N // 4], I32, "c_plane")
+        cs_win = held.tile([P, T // 4], I32, name="cs_win")
         ls_rows = held.tile([P, P], F32, name="ls_rows")
         nc.vector.memset(ks_win[:], 0)
         nc.vector.memset(ls_rows[:], 0.0)
         nc.vector.memset(cs_win[:], 0)
-        nc.vector.memset(c_plane[:], 0)
         make_identity(nc, ident[:])
         warm = held.tile([P, 8], F32, name="warm")
         nc.scalar.activation(warm[32:64, 0:1], ls_rows[32:64, 0:1], ACT.Exp)
@@ -68,71 +64,66 @@ def tile_attend_at_cfg_topk_kernel(tc, qT, k_words, k_scales, c_words, c_scales,
                 row = 32 * quad + first_row
                 nc.sync.dma_start(win[row : row + 4, :], scales[0, 4 * quad : 4 * quad + 4, :].bitcast(I32))
 
-        def load_words(packed, window, name):
-            win = reused.tile([P, T], I32, name=name, offset=window)
+        def load_words(win, packed):
             nc.sync.dma_start(win[:], packed[0].rearrange("p t r -> p (t r)").bitcast(I32))
-            return win
 
         q_raw = held.tile([P, PLACES, NQ], F32, name="q_raw")
         q_rows = qT[0].rearrange("(p t) q -> p t q", t=PLACES)
+        k_win = held.tile([P, T], I32, name="k_win")
+        c_win = guest(C_AT, [P, T], I32, "c_win")
+        us_sb = held.tile([P, PLACES], F32, name="us_sb")
+        v_win = [guest(V_AT[e], [P, T], F32, f"v_win{e}") for e in range(BLOCKS)]
         nc.sync.dma_start(q_raw[:, 0:2, :], q_rows[:, 0:2, :])
         nc.sync.dma_start(offsets[:], offs)
         load_scales(ks_win, k_scales, 0)
-        nc.sync.dma_start(cs_win[4:P:8, :], c_scales[0].bitcast(I32))
-        k_win = load_words(k_words, K_AT, "k_win")
         nc.sync.dma_start(q_raw[:, 2:4, :], q_rows[:, 2:4, :])
+        load_words(k_win, k_words)
         nc.sync.dma_start(ls_rows[LS_ROW : LS_ROW + BLOCKS, :], ls[0, 0].rearrange("(j m) -> j m", j=BLOCKS))
-        c_win = load_words(c_words, C_AT, "c_win")
+        load_scales(cs_win, c_scales, C_ROW)
+        load_words(c_win, c_words)
+        nc.sync.dma_start(us_sb[:], us[0].rearrange("(p t) o -> p (t o)", t=PLACES))
+        for e in range(BLOCKS):
+            nc.sync.dma_start(v_win[e][:], vT[e * P : (e + 1) * P, :])
 
-        def gather(win, dtype, picked):
+        def gather(win, dtype, name):
+            picked = aligned([P, N], dtype, name)
             nc.vector.tensor_copy(picked[:], win[:].bitcast(dtype).indirect(offsets[:]))
             return picked
 
-        k_scale = gather(ks_win, U8, aligned([P, N], U8, "k_scale"))
-        c_rows = gather(cs_win, U8, guest(ROWS_AT, 0, [P, N], U8, "c_rows"))[:].bitcast(I32)
-        for r in range(4):
-            nc.sync.dma_start(c_plane[C_ROW + r : P : 32, :], c_rows[4 + 8 * r : P : 32, :])
-        us_sb = held.tile([P, PLACES], F32, name="us_sb")
-        v_win = {}
-
-        def values_load(e):
-            v_win[e] = reused.tile([P, T], F32, name=f"v_win{e}", offset=V_AT[e])
-            nc.sync.dma_start(v_win[e][:], vT[e * P : (e + 1) * P, :])
-
-        values_load(0)
-        nc.sync.dma_start(us_sb[:], us[0].rearrange("(p t) o -> p (t o)", t=PLACES))
+        k_scale = gather(ks_win, U8, "k_scale")
 
         q_turned = q_raw[:].rearrange("p t q -> p q t")
         q_words, q_scales = {}, {}
 
-        def queries_round(copy, rounded, j):
-            copy(rounded.rearrange("p (q t) -> p q t", t=PLACES), q_turned[:, j * P : (j + 1) * P, :])
+        def queries_round(copy, rounded, j, count):
+            copy(rounded.rearrange("p (q t) -> p q t", t=PLACES), q_turned[:, j * P : (j + count) * P, :])
 
         def queries_quantise(rounded, codes, names):
             scale = aligned([P, len(names) * P], U8, f"q_scale_{names[0]}")
-            nc.vector.quantize_mx(codes[:].bitcast(FP8X4), scale[:], rounded)
+            nc.vector.quantize_mx(codes[:].bitcast(FP8X4), scale[:], rounded[:].rearrange("p a b -> p (a b)"))
             for n, name in enumerate(names):
                 q_words[name], q_scales[name] = codes[:, n * P : (n + 1) * P], scale[:, n * P : (n + 1) * P]
 
-        k_keys = (gather(k_win, U32, aligned([P, N], U32, "k_codes")), k_scale[:])
-        values_load(1)
-        first_bf = aligned([P, 2, PLACES * P], BF16, "first_bf")
+        first_bf = aligned([P, 3, PLACES * P], BF16, "first_bf")
         second_bf = aligned([P, 2, PLACES * P], BF16, "second_bf")
-        apart_bf = aligned([P, PLACES * P], BF16, "apart_bf")
         late_bf = aligned([P, 2, PLACES * P], BF16, "late_bf")
-        queries_round(nc.vector.tensor_copy, first_bf[:, 0, :], 0)
-        nc.scalar.mul(first_bf[:, 1, :].rearrange("p (q t) -> p q t", t=PLACES), q_turned[:, 0:P, :], -0.25)
-        queries_round(nc.scalar.copy, second_bf[:, 0, :], 2)
-        queries_round(nc.scalar.copy, apart_bf[:], APART)
-        queries_round(nc.scalar.copy, late_bf[:, 0, :], 3)
+        queries_round(nc.scalar.copy, first_bf[:, APART, :], APART, 1)
+        queries_round(nc.vector.tensor_copy, first_bf[:, 0:2, :].rearrange("p a b -> p (a b)"), 0, 2)
+        nc.vector.tensor_scalar_mul(second_bf[:], first_bf[:, 0:2, :], -0.25)
+        queries_round(nc.scalar.copy, late_bf[:, 0, :], 3, 1)
         nc.scalar.mul(late_bf[:, 1, :], late_bf[:, 0, :], -0.25)
-        queries_quantise(first_bf[:].rearrange("p a b -> p (a b)"), aligned([P, 2 * P], U32, "q_first"), ["q0", "m0"])
-        nc.vector.tensor_scalar_mul(second_bf[:, 1, :], second_bf[:, 0, :], -0.25)
-        queries_quantise(second_bf[:].rearrange("p a b -> p (a b)"), aligned([P, 2 * P], U32, "q_second"), ["q2", "m2"])
+        queries_quantise(first_bf, aligned([P, 3 * P], U32, "q_first"), ["q0", "q1", "q2"])
+        queries_quantise(second_bf, aligned([P, 2 * P], U32, "q_second"), ["m0", "m1"])
+
         neg_ls = held.tile([P, BLOCKS], F32, name="neg_ls")
-        ls_ps = bank(4, [P, P], "ls_ps")
+        ls_ps = bank(7, [P, P], "ls_ps")
         nc.tensor.transpose(ls_ps[:], ls_rows[:], ident[:])
         nc.scalar.mul(neg_ls[:], ls_ps[:, LS_ROW : LS_ROW + BLOCKS], -1.0)
+
+        k_keys = (gather(k_win, U32, "k_codes"), k_scale[:])
+        c_scale = gather(cs_win, U8, "c_scale")
+        c_keys = (gather(c_win, U32, "c_codes"), c_scale[C_ROW:P, :])
+        queries_quantise(late_bf, guest(C_AT, [P, 2 * P], U32, "q_late"), ["q3", "m3"])
 
         def score_pass(ps, queries, keys, start, stop):
             codes, scale = keys
@@ -145,154 +136,128 @@ def tile_attend_at_cfg_topk_kernel(tc, qT, k_words, k_scales, c_words, c_scales,
         def planes(name):
             return held.tile([P, PLACES, P], F32, name=name)
 
-        joint = {}
+        joint, to_turn, turned = {}, {}, {}
 
         def joint_open(j, bank_number):
             joint[j] = bank(bank_number, [P, N], f"joint{j}")
             score_pass(joint[j], f"q{j}", k_keys, True, False)
             score_pass(joint[j], f"m{j}", k_keys, False, False)
 
-        joint_open(0, 0)
-        joint_open(2, 3)
-        c_keys = (gather(c_win, U32, aligned([P, N], U32, "c_codes")), c_plane[C_ROW:P, :].bitcast(U8))
-        values_load(2)
-        queries_quantise(apart_bf[:], guest(ROWS_AT - 256, 0, [P, P], U32, "q_apart"), ["q1"])
-        queries_quantise(late_bf[:].rearrange("p a b -> p (a b)"), guest(ROWS_AT + 256, 0, [P, 2 * P], U32, "q_late"), ["q3", "m3"])
-
-        y_scale = aligned([P, NQ], U8, "y_scale")
-        v_scale = aligned([P, DV], U8, "v_scale")
-        us_places = us_sb[:].unsqueeze(1).to_broadcast([P, P, PLACES])
-        to_turn, exps, y_bf, y_codes, v_picked, v_bf, v_codes = {}, {}, {}, {}, {}, {}, {}
-
-        def joint_close(j, pieces):
+        def joint_close(j):
             score_pass(joint[j], f"m{j}", c_keys, False, True)
-            exp_sb = planes(f"exp{j}")
-            for n in range(pieces):
-                part = slice(PLACES * n // pieces, PLACES * (n + 1) // pieces)
-                nc.scalar.activation(exp_sb[:, part, :], by_place(joint[j])[:, part, :], ACT.Exp, bias=neg_ls[:, j : j + 1], scale=2.0)
-            to_turn[j] = [exp_sb]
 
-        def apart_scores(a_bank, bank_number):
-            a_ps = bank(a_bank, [P, N], "a_apart")
-            score_pass(a_ps, f"q{APART}", k_keys, True, True)
-            a_term = planes("a_term")
-            nc.scalar.mul(a_term[:], by_place(a_ps), 1.5)
-            z_ps = bank(bank_number, [P, N], "z_apart")
-            score_pass(z_ps, f"q{APART}", c_keys, True, True)
-            z_term = planes("z_term")
-            nc.scalar.activation(z_term[:], by_place(z_ps), ACT.Identity, bias=neg_ls[:, APART : APART + 1], scale=-0.5)
-            to_turn[APART] = [z_term, a_term]
+        def joint_exp(j, exps):
+            to_turn[j] = exps
+            nc.scalar.activation(to_turn[j][:], by_place(joint[j]), ACT.Exp, bias=neg_ls[:, j : j + 1], scale=2.0)
+
+        a_ps = bank(0, [P, N], "a_apart")
+        score_pass(a_ps, f"q{APART}", k_keys, True, True)
+        a_term = planes("a_term")
+        nc.scalar.activation(a_term[:], by_place(a_ps), ACT.Identity, bias=neg_ls[:, APART : APART + 1], scale=1.5)
+        joint_open(0, 1)
+        joint_open(1, 2)
+        z_ps = bank(4, [P, N], "z_apart")
+        score_pass(z_ps, f"q{APART}", c_keys, True, True)
+        to_turn[APART] = guest(EXPONENT_AT, [P, PLACES, P], F32, "exponent")
+        nc.vector.scalar_tensor_tensor(to_turn[APART][:], by_place(z_ps), -0.5, a_term[:], ALU.mult, ALU.add)
+        joint_close(0)
+        joint_exp(0, planes("exp0"))
+        joint_close(1)
+        joint_exp(1, planes("exp1"))
+        joint_open(3, 3)
+        joint_close(3)
 
         def weights_turn(j, bank_number):
             ps = bank(bank_number, [P, PLACES, P], f"turned{j}")
-            terms = to_turn[j]
             for t in range(PLACES):
-                for n, term in enumerate(terms):
-                    nc.tensor.matmul(ps[:, t, :], term[:, t, :], ident[:], start=n == 0,
-                                     stop=n == len(terms) - 1, is_transpose=True)
-            exps[j] = ps[:].rearrange("p t q -> p q t")
-            if j == APART:
-                exp_sb = held.tile([P, P, PLACES], F32, name=f"exp{j}")
-                nc.scalar.activation(exp_sb[:], exps[j], ACT.Exp)
-                exps[j] = exp_sb[:]
+                nc.tensor.transpose(ps[:, t, :], to_turn[j][:, t, :], ident[:])
+            turned[j] = ps[:].rearrange("p t q -> p q t")
 
-        def weights_scale(j, window, room):
-            y_bf[j] = guest(window, room, [P, P, PLACES], BF16, f"y_bf{j}")
-            nc.vector.tensor_tensor(y_bf[j][:], exps[j], us_places, ALU.mult)
+        us_places = us_sb[:].unsqueeze(1).to_broadcast([P, P, PLACES])
+        v_picked = {}
 
-        def weights_scale_aside(j, rounded):
-            y_bf[j] = rounded
-            nc.gpsimd.tensor_tensor(y_bf[j][:], exps[j], us_places, ALU.mult)
-
-        def weights_scale_by_place(j, rounded):
-            y_bf[j] = rounded
-            for t in range(PLACES):
-                nc.scalar.activation(y_bf[j][:, :, t], exps[j][:, :, t], ACT.Copy, scale=us_sb[:, t : t + 1])
-
-        def weights_quantise(j, codes):
-            y_codes[j] = codes
-            nc.vector.quantize_mx(codes[:].bitcast(FP8X4), y_scale[:, j * P : (j + 1) * P], y_bf[j][:].rearrange("p q t -> p (q t)"))
-
-        def values_gather(e, picked):
+        def values_gather(e, picked, engines):
             v_picked[e] = picked
-            nc.vector.tensor_copy(v_picked[e][:], v_win[e][:].indirect(offsets[:]))
+            share = N // len(engines)
+            for n, engine in enumerate(engines):
+                listed = v_win[e][:].indirect(offsets[:, n * share // 16 : (n + 1) * share // 16])
+                if engine == "vector":
+                    nc.vector.tensor_copy(picked[:, n * share : (n + 1) * share], listed)
+                else:
+                    nc.scalar.activation(picked[:, n * share : (n + 1) * share], listed, ACT.Copy)
 
-        def values_turn(e, bank_number, turned):
+        def values_turn(e, bank_number, rounded):
             pairs = v_picked[e][:].bitcast(F32)
             ps = bank(bank_number, [P, 2, P], f"v{e}")
             for u in range(2):
                 nc.tensor.transpose(ps[:, u, :], pairs[:, u : 2 * P : 2], ident[:])
-            v_bf[e] = turned
-            nc.scalar.copy(v_bf[e].bitcast(F32).rearrange("p (e u) -> p e u", u=2), ps[:].rearrange("p u e -> p e u"))
+            nc.scalar.copy(rounded.bitcast(F32).rearrange("p (e u) -> p e u", u=2), ps[:].rearrange("p u e -> p e u"))
 
-        def values_quantise(e, codes):
-            v_codes[e] = codes
-            nc.vector.quantize_mx(codes[:].bitcast(FP8X4), v_scale[:, e * P : (e + 1) * P], v_bf[e])
-
-        def guest_words(window, room, name):
-            return guest(window, room, [P, P], U32, name)
-
+        values_gather(0, aligned([P, N], BF16, "v_picked0"), ["vector"])
+        y_bf = guest(V_AT[0], [P, BLOCKS, P, PLACES], BF16, "y_bf")
+        joint_exp(3, planes("exp3"))
+        weights_turn(APART, 0)
+        exp_apart = held.tile([P, P, PLACES], F32, name="exp_apart")
+        nc.scalar.activation(exp_apart[:], turned[APART], ACT.Exp)
+        nc.gpsimd.tensor_tensor(y_bf[:, APART], exp_apart[:], us_places, ALU.mult)
+        for j, bank_number in ((0, 5), (1, 6), (3, 7)):
+            weights_turn(j, bank_number)
+            nc.vector.tensor_tensor(y_bf[:, j], turned[j], us_places, ALU.mult)
+        v_scale = aligned([P, DV], U8, "v_scale")
         out_rows = out[0].rearrange("(j m) e -> m j e", m=P)
 
-        def product(ps, j, codes, first):
-            width = codes.shape[1]
-            nc.tensor.matmul_mx(ps, lhsT=y_codes[j][:].bitcast(FP8X4), lhsT_scale=y_scale[:, j * P : (j + 1) * P],
-                                rhs=codes.bitcast(FP8X4), rhs_scale=v_scale[:, first : first + width], start=True, stop=True)
+        def values_quantise(rounded, codes, first):
+            nc.vector.quantize_mx(codes.bitcast(FP8X4), v_scale[:, first : first + codes.shape[1]], rounded)
 
         def products(js, codes, first, bank_number):
-            ps = bank(bank_number, [P, len(js), codes.shape[1]], f"out_ps{js[0]}_{first}")
+            width = codes.shape[1]
+            ps = bank(bank_number, [P, len(js), width], f"out_ps{js[0]}_{first}")
             for n, j in enumerate(js):
-                product(ps[:, n, :], j, codes, first)
+                cols = slice(j * P, (j + 1) * P)
+                nc.tensor.matmul_mx(ps[:, n, :], lhsT=y_codes[j].bitcast(FP8X4), lhsT_scale=y_scale[:, cols],
+                                    rhs=codes[:].bitcast(FP8X4), rhs_scale=v_scale[:, first : first + width], start=True, stop=True)
             return ps
 
-        def store(ps, js, first, copy, queue):
-            width = ps.shape[2]
-            staged = held.tile([P, len(js), width], F32, name=f"out{js[0]}_{first}")
+        def store(ps, staged, js, first, copy, queue):
             copy(staged[:], ps[:])
-            queue.dma_start(out_rows[:, js[0] : js[-1] + 1, first : first + width], staged[:])
+            queue.dma_start(out_rows[:, js[0] : js[-1] + 1, first : first + ps.shape[2]], staged[:])
 
-        def own(name):
-            return aligned([P, N], BF16, name)
+        y_scale = aligned([P, NQ], U8, "y_scale")
+        y_codes = {}
 
-        joint_close(0, 2)
-        joint_close(2, 1)
-        apart_scores(1, 2)
-        values_gather(0, own("v_picked0"))
-        values_load(3)
-        weights_turn(0, 5)
-        weights_scale(0, SPARE_AT, 0)
-        joint_open(3, 0)
-        joint_close(3, 1)
-        weights_turn(2, 7)
-        weights_turn(1, 6)
-        v01_bf = aligned([P, 2, N], BF16, "v01_bf")
-        values_turn(0, 2, v01_bf[:, 0, :])
-        values_gather(1, guest(SPARE_AT, 1, [P, N], BF16, "v_picked1"))
-        weights_scale(2, V_AT[1], 0)
-        weights_quantise(0, guest_words(V_AT[1], 1, "y_codes0"))
-        weights_scale_aside(1, guest(SPARE_AT, 0, [P, P, PLACES], BF16, "y_bf1"))
-        weights_turn(3, 1)
-        values_turn(1, 4, v01_bf[:, 1, :])
-        weights_scale_by_place(3, guest(SPARE_AT, 1, [P, P, PLACES], BF16, "y_bf3"))
-        values_gather(2, own("v_picked2"))
-        values_turn(2, 3, own("v_bf2")[:])
-        weights_quantise(2, guest_words(V_AT[2], 0, "y_codes2"))
-        v01_codes = guest(V_AT[2], 3, [P, 2 * P], U32, "v01_codes")
-        nc.vector.quantize_mx(v01_codes[:].bitcast(FP8X4), v_scale[:, 0 : 2 * P], v01_bf[:].rearrange("p a b -> p (a b)"))
-        weights_quantise(1, guest_words(V_AT[2], 2, "y_codes1"))
-        early_out = held.tile([P, 3, 2 * P], F32, name="early_out")
-        for js, bank_number in (([0, 1], 0), ([2], 5)):
-            nc.scalar.copy(early_out[:, js[0] : js[-1] + 1, :], products(js, v01_codes[:], 0, bank_number)[:])
-        nc.sync.dma_start(out_rows[:, 0:3, 0 : 2 * P], early_out[:])
-        values_gather(3, own("v_picked3"))
-        values_turn(3, 4, own("v_bf3")[:])
-        values_quantise(2, guest_words(V_AT[3], 1, "v_codes2"))
-        weights_quantise(3, guest_words(V_AT[3], 2, "y_codes3"))
-        store(products([0, 1, 2], v_codes[2][:], 2 * P, 6), [0, 1, 2], 2 * P, nc.scalar.copy, nc.sync)
-        rest_ps = bank(7, [P, 1, 3 * P], "rest_ps")
-        product(rest_ps[:, 0, 0 : 2 * P], 3, v01_codes[:], 0)
-        product(rest_ps[:, 0, 2 * P : 3 * P], 3, v_codes[2][:], 2 * P)
-        store(rest_ps, [3], 0, nc.scalar.copy, nc.sync)
-        values_quantise(3, guest_words(V_AT[3], 0, "v_codes3"))
-        store(products([0, 1], v_codes[3][:], 3 * P, 2), [0, 1], 3 * P, nc.vector.tensor_copy, nc.sync)
-        store(products([2, 3], v_codes[3][:], 3 * P, 3), [2, 3], 3 * P, nc.scalar.copy, nc.scalar)
+        def weights_quantise(pair, codes):
+            nc.vector.quantize_mx(codes[:].bitcast(FP8X4), y_scale[:, 2 * P * pair : 2 * P * (pair + 1)],
+                                  y_bf[:, 2 * pair : 2 * pair + 2].rearrange("p a q t -> p (a q t)"))
+            for n in range(2):
+                y_codes[2 * pair + n] = codes[:, n * P : (n + 1) * P]
+
+        weights_quantise(0, aligned([P, 2 * P], U32, "y_codes01"))
+        values_gather(1, aligned([P, N], BF16, "v_picked1"), ["scalar"])
+        v0_bf = guest(V_AT[1], [P, N], BF16, "v0_bf")
+        values_turn(0, 4, v0_bf[:])
+        values_gather(2, aligned([P, N], BF16, "v_picked2"), ["vector", "scalar"])
+        weights_quantise(1, guest(V_AT[2], [P, 2 * P], U32, "y_codes23"))
+        v1_bf = guest(V_AT[2] + ROOM, [P, N], BF16, "v1_bf")
+        values_turn(1, 1, v1_bf[:])
+        v01_codes = guest(V_AT[2] + 2 * ROOM, [P, 2 * P], U32, "v01_codes")
+        values_quantise(v0_bf[:], v01_codes[:, 0:P], 0)
+        values_quantise(v1_bf[:], v01_codes[:, P : 2 * P], P)
+        v2_bf = aligned([P, N], BF16, "v2_bf")
+        values_turn(2, 5, v2_bf[:])
+        early_a = products([0, 1], v01_codes, 0, 2)
+        early_b = products([2, 3], v01_codes, 0, 3)
+        values_gather(3, guest(LAST_AT, [P, N], BF16, "v_picked3"), ["vector", "scalar"])
+        v2_codes = guest(V_AT[3], [P, P], U32, "v2_codes")
+        values_quantise(v2_bf[:], v2_codes[:], 2 * P)
+        store(early_a, guest(V_AT[3] + ROOM, [P, 2, 2 * P], F32, "out_a"), [0, 1], 0, nc.scalar.copy, nc.sync)
+        store(early_b, guest(V_AT[3] + 2 * ROOM, [P, 2, 2 * P], F32, "out_b"), [2, 3], 0, nc.vector.tensor_copy, nc.sync)
+        v3_bf = aligned([P, N], BF16, "v3_bf")
+        values_turn(3, 0, v3_bf[:])
+        middle = products([0, 1, 2, 3], v2_codes, 2 * P, 6)
+        v3_codes = aligned([P, P], U32, "v3_codes")
+        values_quantise(v3_bf[:], v3_codes[:], 3 * P)
+        store(middle, guest(LAST_AT, [P, BLOCKS, P], F32, "out_middle"), [0, 1, 2, 3], 2 * P, nc.scalar.copy, nc.sync)
+        last_a = products([0, 1], v3_codes, 3 * P, 7)
+        last_b = products([2, 3], v3_codes, 3 * P, 4)
+        store(last_a, held.tile([P, 2, P], F32, name="out_last_a"), [0, 1], 3 * P, nc.vector.tensor_copy, nc.sync)
+        store(last_b, held.tile([P, 2, P], F32, name="out_last_b"), [2, 3], 3 * P, nc.scalar.copy, nc.scalar)

@@ -21,13 +21,14 @@ FLOPS = 2 * 2 * N * D * NQ + 2 * N * NQ * DV
 
 WINDOW_BYTES = 4 * T
 C_AT = 0
-V_AT = [WINDOW_BYTES * (1 + e) for e in range(BLOCKS)]
-LAST_AT = 5 * WINDOW_BYTES
+ROWS_AT = WINDOW_BYTES
+V_AT = [WINDOW_BYTES * (2 + e) for e in range(BLOCKS)]
+LAST_AT = 6 * WINDOW_BYTES
 EXPONENT_AT = LAST_AT + 2048
 ROOM = 2048
+K_AT = 7 * WINDOW_BYTES
 BANK_BYTES = 2048
 C_ROW = 8
-LS_ROW = 16
 APART = 2
 
 
@@ -51,13 +52,16 @@ def tile_attend_at_cfg_topk_kernel(tc, qT, k_words, k_scales, c_words, c_scales,
         ident = held.tile([P, P], F32, name="ident")
         ks_win = held.tile([P, T // 4], I32, name="ks_win")
         cs_win = held.tile([P, T // 4], I32, name="cs_win")
-        ls_rows = held.tile([P, P], F32, name="ls_rows")
+        ls_sb = held.tile([P, BLOCKS], F32, name="ls_sb")
+        zero = held.tile([P, 8], F32, name="zero")
+        c_plane = aligned([P, N // 4], I32, "c_plane")
         nc.vector.memset(ks_win[:], 0)
-        nc.vector.memset(ls_rows[:], 0.0)
         nc.vector.memset(cs_win[:], 0)
+        nc.vector.memset(zero[:], 0.0)
+        nc.vector.memset(c_plane[:], 0)
         make_identity(nc, ident[:])
         warm = held.tile([P, 8], F32, name="warm")
-        nc.scalar.activation(warm[32:64, 0:1], ls_rows[32:64, 0:1], ACT.Exp)
+        nc.scalar.activation(warm[:, 0:1], zero[:, 0:1], ACT.Exp)
 
         def load_scales(win, scales, first_row):
             for quad in range(4):
@@ -69,61 +73,58 @@ def tile_attend_at_cfg_topk_kernel(tc, qT, k_words, k_scales, c_words, c_scales,
 
         q_raw = held.tile([P, PLACES, NQ], F32, name="q_raw")
         q_rows = qT[0].rearrange("(p t) q -> p t q", t=PLACES)
-        k_win = held.tile([P, T], I32, name="k_win")
+        k_win = guest(K_AT, [P, T], I32, "k_win")
         c_win = guest(C_AT, [P, T], I32, "c_win")
         us_sb = held.tile([P, PLACES], F32, name="us_sb")
         v_win = [guest(V_AT[e], [P, T], F32, f"v_win{e}") for e in range(BLOCKS)]
-        nc.sync.dma_start(q_raw[:, 0:2, :], q_rows[:, 0:2, :])
         nc.sync.dma_start(offsets[:], offs)
+        nc.sync.dma_start(q_raw[:, 0:2, :], q_rows[:, 0:2, :])
         load_scales(ks_win, k_scales, 0)
+        nc.sync.dma_start(cs_win[4:P:8, :], c_scales[0].bitcast(I32))
         nc.sync.dma_start(q_raw[:, 2:4, :], q_rows[:, 2:4, :])
         load_words(k_win, k_words)
-        nc.sync.dma_start(ls_rows[LS_ROW : LS_ROW + BLOCKS, :], ls[0, 0].rearrange("(j m) -> j m", j=BLOCKS))
-        load_scales(cs_win, c_scales, C_ROW)
+        nc.sync.dma_start(ls_sb[:], ls[0, 0].rearrange("(m j) -> m j", j=BLOCKS))
         load_words(c_win, c_words)
-        nc.sync.dma_start(us_sb[:], us[0].rearrange("(p t) o -> p (t o)", t=PLACES))
-        for e in range(BLOCKS):
-            nc.sync.dma_start(v_win[e][:], vT[e * P : (e + 1) * P, :])
 
-        def gather(win, dtype, name):
-            picked = aligned([P, N], dtype, name)
+        def gather(win, dtype, picked):
             nc.vector.tensor_copy(picked[:], win[:].bitcast(dtype).indirect(offsets[:]))
             return picked
 
-        k_scale = gather(ks_win, U8, "k_scale")
+        c_rows = gather(cs_win, U8, guest(ROWS_AT, [P, N], U8, "c_rows"))[:].bitcast(I32)
+        for r in range(4):
+            nc.sync.dma_start(c_plane[C_ROW + r : P : 32, :], c_rows[4 + 8 * r : P : 32, :])
+        for e in range(BLOCKS):
+            nc.sync.dma_start(v_win[e][:], vT[e * P : (e + 1) * P, :])
+            if e == 0:
+                nc.sync.dma_start(us_sb[:], us[0].rearrange("(p t) o -> p (t o)", t=PLACES))
+        k_scale = gather(ks_win, U8, aligned([P, N], U8, "k_scale"))
 
-        q_turned = q_raw[:].rearrange("p t q -> p q t")
+        q_dealt = q_raw[:].rearrange("p t (m j) -> p m t j", j=BLOCKS)
         q_words, q_scales = {}, {}
 
-        def queries_round(copy, rounded, j, count):
-            copy(rounded.rearrange("p (q t) -> p q t", t=PLACES), q_turned[:, j * P : (j + count) * P, :])
+        def queries_round(rounded, j):
+            nc.scalar.copy(rounded.rearrange("p j (m t) -> p m t j", t=PLACES), q_dealt[:, :, :, j : j + 2])
 
         def queries_quantise(rounded, codes, names):
             scale = aligned([P, len(names) * P], U8, f"q_scale_{names[0]}")
-            nc.vector.quantize_mx(codes[:].bitcast(FP8X4), scale[:], rounded[:].rearrange("p a b -> p (a b)"))
+            nc.vector.quantize_mx(codes[:].bitcast(FP8X4), scale[:], rounded.rearrange("p a b -> p (a b)"))
             for n, name in enumerate(names):
                 q_words[name], q_scales[name] = codes[:, n * P : (n + 1) * P], scale[:, n * P : (n + 1) * P]
 
-        first_bf = aligned([P, 3, PLACES * P], BF16, "first_bf")
-        second_bf = aligned([P, 2, PLACES * P], BF16, "second_bf")
-        late_bf = aligned([P, 2, PLACES * P], BF16, "late_bf")
-        queries_round(nc.scalar.copy, first_bf[:, APART, :], APART, 1)
-        queries_round(nc.vector.tensor_copy, first_bf[:, 0:2, :].rearrange("p a b -> p (a b)"), 0, 2)
-        nc.vector.tensor_scalar_mul(second_bf[:], first_bf[:, 0:2, :], -0.25)
-        queries_round(nc.scalar.copy, late_bf[:, 0, :], 3, 1)
-        nc.scalar.mul(late_bf[:, 1, :], late_bf[:, 0, :], -0.25)
-        queries_quantise(first_bf, aligned([P, 3 * P], U32, "q_first"), ["q0", "q1", "q2"])
-        queries_quantise(second_bf, aligned([P, 2 * P], U32, "q_second"), ["m0", "m1"])
-
+        first_bf = aligned([P, 2, PLACES * P], BF16, "first_bf")
+        other_bf = aligned([P, 5, PLACES * P], BF16, "other_bf")
+        queries_round(first_bf[:], 0)
+        queries_round(other_bf[:, 2:4, :], 2)
+        nc.scalar.mul(other_bf[:, 4, :], other_bf[:, 3, :], -0.25)
+        queries_quantise(first_bf[:], aligned([P, 2 * P], U32, "q_first"), ["q0", "q1"])
+        nc.vector.tensor_scalar_mul(other_bf[:, 0:2, :], first_bf[:], -0.25)
         neg_ls = held.tile([P, BLOCKS], F32, name="neg_ls")
-        ls_ps = bank(7, [P, P], "ls_ps")
-        nc.tensor.transpose(ls_ps[:], ls_rows[:], ident[:])
-        nc.scalar.mul(neg_ls[:], ls_ps[:, LS_ROW : LS_ROW + BLOCKS], -1.0)
+        nc.scalar.mul(neg_ls[:], ls_sb[:], -1.0)
 
-        k_keys = (gather(k_win, U32, "k_codes"), k_scale[:])
-        c_scale = gather(cs_win, U8, "c_scale")
-        c_keys = (gather(c_win, U32, "c_codes"), c_scale[C_ROW:P, :])
-        queries_quantise(late_bf, guest(C_AT, [P, 2 * P], U32, "q_late"), ["q3", "m3"])
+        k_keys = (gather(k_win, U32, aligned([P, N], U32, "k_codes")), k_scale[:])
+        queries_quantise(other_bf[:, 0:3, :], guest(K_AT, [P, 3 * P], U32, "q_second"), ["m0", "m1", "q2"])
+        c_keys = (gather(c_win, U32, aligned([P, N], U32, "c_codes")), c_plane[C_ROW:P, :].bitcast(U8))
+        queries_quantise(other_bf[:, 3:5, :], guest(ROWS_AT - 512, [P, 2 * P], U32, "q_late"), ["q3", "m3"])
 
         def score_pass(ps, queries, keys, start, stop):
             codes, scale = keys
@@ -150,12 +151,15 @@ def tile_attend_at_cfg_topk_kernel(tc, qT, k_words, k_scales, c_words, c_scales,
             to_turn[j] = exps
             nc.scalar.activation(to_turn[j][:], by_place(joint[j]), ACT.Exp, bias=neg_ls[:, j : j + 1], scale=2.0)
 
+        for j in range(2):
+            joint[j] = bank(1 + j, [P, N], f"joint{j}")
+            score_pass(joint[j], f"q{j}", k_keys, True, False)
         a_ps = bank(0, [P, N], "a_apart")
         score_pass(a_ps, f"q{APART}", k_keys, True, True)
         a_term = planes("a_term")
         nc.scalar.activation(a_term[:], by_place(a_ps), ACT.Identity, bias=neg_ls[:, APART : APART + 1], scale=1.5)
-        joint_open(0, 1)
-        joint_open(1, 2)
+        for j in range(2):
+            score_pass(joint[j], f"m{j}", k_keys, False, False)
         z_ps = bank(4, [P, N], "z_apart")
         score_pass(z_ps, f"q{APART}", c_keys, True, True)
         to_turn[APART] = guest(EXPONENT_AT, [P, PLACES, P], F32, "exponent")
@@ -204,7 +208,7 @@ def tile_attend_at_cfg_topk_kernel(tc, qT, k_words, k_scales, c_words, c_scales,
             weights_turn(j, bank_number)
             nc.vector.tensor_tensor(y_bf[:, j], turned[j], us_places, ALU.mult)
         v_scale = aligned([P, DV], U8, "v_scale")
-        out_rows = out[0].rearrange("(j m) e -> m j e", m=P)
+        out_rows = out[0].rearrange("(m j) e -> m j e", j=BLOCKS)
 
         def values_quantise(rounded, codes, first):
             nc.vector.quantize_mx(codes.bitcast(FP8X4), v_scale[:, first : first + codes.shape[1]], rounded)

@@ -26,6 +26,7 @@ V_AT = [WINDOW_BYTES * (2 + e) for e in range(BLOCKS)]
 LAST_AT = 6 * WINDOW_BYTES
 EXPONENT_AT = LAST_AT + 2048
 ROOM = 2048
+V3_BF_AT = LAST_AT + 2 * ROOM
 K_AT = 7 * WINDOW_BYTES
 BANK_BYTES = 2048
 C_ROW = 8
@@ -255,12 +256,14 @@ def tile_attend_at_cfg_topk_kernel(tc, qT, k_words, k_scales, c_words, c_scales,
         values_quantise(v2_bf[:], v2_codes[:], 2 * P)
         store(early_a, guest(V_AT[3] + ROOM, [P, 2, 2 * P], F32, "out_a"), [0, 1], 0, nc.scalar.copy, nc.sync)
         store(early_b, guest(V_AT[3] + 2 * ROOM, [P, 2, 2 * P], F32, "out_b"), [2, 3], 0, nc.vector.tensor_copy, nc.sync)
-        v3_bf = aligned([P, N], BF16, "v3_bf")
+        v3_bf = guest(V3_BF_AT, [P, N], BF16, "v3_bf")
         values_turn(3, 0, v3_bf[:])
-        middle = products([0, 1, 2, 3], v2_codes, 2 * P, 6)
+        middle_a = products([0, 1], v2_codes, 2 * P, 6)
+        middle_b = products([2, 3], v2_codes, 2 * P, 1)
         v3_codes = aligned([P, P], U32, "v3_codes")
         values_quantise(v3_bf[:], v3_codes[:], 3 * P)
-        store(middle, guest(LAST_AT, [P, BLOCKS, P], F32, "out_middle"), [0, 1, 2, 3], 2 * P, nc.scalar.copy, nc.sync)
+        store(middle_a, guest(LAST_AT, [P, 2, P], F32, "out_middle_a"), [0, 1], 2 * P, nc.scalar.copy, nc.sync)
+        store(middle_b, guest(V3_BF_AT, [P, 2, P], F32, "out_middle_b"), [2, 3], 2 * P, nc.vector.tensor_copy, nc.sync)
         last_a = products([0, 1], v3_codes, 3 * P, 7)
         last_b = products([2, 3], v3_codes, 3 * P, 4)
         store(last_a, held.tile([P, 2, P], F32, name="out_last_a"), [0, 1], 3 * P, nc.vector.tensor_copy, nc.sync)

from contextlib import ExitStack

import concourse.mybir as mybir
from concourse.masks import make_identity

F32 = mybir.dt.float32
BF16 = mybir.dt.bfloat16
I32 = mybir.dt.int32
U32 = mybir.dt.uint32
U16 = mybir.dt.uint16
U8 = mybir.dt.uint8
FP8X4 = mybir.dt.float8_e4m3fn_x4
ACT = mybir.ActivationFunctionType
ALU = mybir.AluOpType

P = 128
N, T, D, NQ, DV = 512, 2048, 512, 512, 512
BLOCKS = 4
PLACES = 4
FLOPS = 2 * 2 * N * D * NQ + 2 * N * NQ * DV

WINDOW_BYTES = 4 * T
C_AT = 0
ROWS_AT = WINDOW_BYTES
V_AT = [WINDOW_BYTES * (2 + e) for e in range(BLOCKS)]
LAST_AT = 6 * WINDOW_BYTES
EXPONENT_AT = LAST_AT + 2048
ROOM = 2048
V3_BF_AT = LAST_AT + 2 * ROOM
K_AT = 7 * WINDOW_BYTES
BANK_BYTES = 2048
C_ROW = 8
APART = 2


def tile_attend_at_cfg_topk_kernel(tc, qT, k_words, k_scales, c_words, c_scales, vT, ls, us, offs, out):
    nc = tc.nc
    with ExitStack() as ctx:
        held = ctx.enter_context(tc.tile_pool(name="held", bufs=1))
        reused = ctx.enter_context(tc.tile_pool(name="reused", bufs=1))
        psum = ctx.enter_context(tc.psum_pool(name="psum", bufs=1))

        def bank(number, shape, name):
            return psum.tile(shape, F32, name=name, offset=number * BANK_BYTES)

        def guest(at, shape, dtype, name):
            return reused.tile(shape, dtype, name=name, offset=at, align_bytes=64)

        def aligned(shape, dtype, name):
            return held.tile(shape, dtype, name=name, align_bytes=64)

        offsets = held.tile([P, N // 16], U16, name="offsets")
        ident = held.tile([P, P], F32, name="ident")
        ks_win = held.tile([P, T // 4], I32, name="ks_win")
        cs_win = held.tile([P, T // 4], I32, name="cs_win")
        ls_sb = held.tile([P, BLOCKS], F32, name="ls_sb")
        zero = held.tile([P, 8], F32, name="zero")
        c_plane = aligned([P, N // 4], I32, "c_plane")
        nc.vector.memset(ks_win[:], 0)
        nc.vector.memset(cs_win[:], 0)
        nc.vector.memset(zero[:], 0.0)
        nc.vector.memset(c_plane[:], 0)
        make_identity(nc, ident[:])
        warm = held.tile([P, 8], F32, name="warm")
        nc.scalar.activation(warm[:, 0:1], zero[:, 0:1], ACT.Exp)

        def load_scales(win, scales, first_row):
            for quad in range(4):
                row = 32 * quad + first_row
                nc.sync.dma_start(win[row : row + 4, :], scales[0, 4 * quad : 4 * quad + 4, :].bitcast(I32))

        def load_words(win, packed):
            nc.sync.dma_start(win[:], packed[0].rearrange("p t r -> p (t r)").bitcast(I32))

        q_raw = held.tile([P, PLACES, NQ], F32, name="q_raw")
        q_rows = qT[0].rearrange("(p t) q -> p t q", t=PLACES)
        k_win = guest(K_AT, [P, T], I32, "k_win")
        c_win = guest(C_AT, [P, T], I32, "c_win")
        us_sb = held.tile([P, PLACES], F32, name="us_sb")
        v_win = [guest(V_AT[e], [P, T], F32, f"v_win{e}") for e in range(BLOCKS)]
        nc.sync.dma_start(offsets[:], offs)
        nc.sync.dma_start(q_raw[:, 0:2, :], q_rows[:, 0:2, :])
        load_scales(ks_win, k_scales, 0)
        nc.sync.dma_start(cs_win[4:P:8, :], c_scales[0].bitcast(I32))
        nc.sync.dma_start(q_raw[:, 2:4, :], q_rows[:, 2:4, :])
        load_words(k_win, k_words)
        nc.sync.dma_start(ls_sb[:], ls[0, 0].rearrange("(m j) -> m j", j=BLOCKS))
        load_words(c_win, c_words)

        def gather(win, dtype, picked):
            nc.vector.tensor_copy(picked[:], win[:].bitcast(dtype).indirect(offsets[:]))
            return picked

        c_rows = gather(cs_win, U8, guest(ROWS_AT, [P, N], U8, "c_rows"))[:].bitcast(I32)
        for r in range(4):
            nc.sync.dma_start(c_plane[C_ROW + r : P : 32, :], c_rows[4 + 8 * r : P : 32, :])
        for e in range(BLOCKS):
            nc.sync.dma_start(v_win[e][:], vT[e * P : (e + 1) * P, :])
            if e == 0:
                nc.sync.dma_start(us_sb[:], us[0].rearrange("(p t) o -> p (t o)", t=PLACES))
        k_scale = gather(ks_win, U8, aligned([P, N], U8, "k_scale"))

        q_dealt = q_raw[:].rearrange("p t (m j) -> p m t j", j=BLOCKS)
        q_words, q_scales = {}, {}

        def queries_round(rounded, j):
            nc.scalar.copy(rounded.rearrange("p j (m t) -> p m t j", t=PLACES), q_dealt[:, :, :, j : j + 2])

        def queries_quantise(rounded, codes, names):
            scale = aligned([P, len(names) * P], U8, f"q_scale_{names[0]}")
            nc.vector.quantize_mx(codes[:].bitcast(FP8X4), scale[:], rounded.rearrange("p a b -> p (a b)"))
            for n, name in enumerate(names):
                q_words[name], q_scales[name] = codes[:, n * P : (n + 1) * P], scale[:, n * P : (n + 1) * P]

        first_bf = aligned([P, 2, PLACES * P], BF16, "first_bf")
        other_bf = aligned([P, 5, PLACES * P], BF16, "other_bf")
        queries_round(first_bf[:], 0)
        queries_round(other_bf[:, 2:4, :], 2)
        nc.scalar.mul(other_bf[:, 4, :], other_bf[:, 3, :], -0.25)
        queries_quantise(first_bf[:], aligned([P, 2 * P], U32, "q_first"), ["q0", "q1"])
        nc.vector.tensor_scalar_mul(other_bf[:, 0:2, :], first_bf[:], -0.25)
        neg_ls = held.tile([P, BLOCKS], F32, name="neg_ls")
        nc.scalar.mul(neg_ls[:], ls_sb[:], -1.0)

        k_keys = (gather(k_win, U32, aligned([P, N], U32, "k_codes")), k_scale[:])
        queries_quantise(other_bf[:, 0:3, :], guest(K_AT, [P, 3 * P], U32, "q_second"), ["m0", "m1", "q2"])
        c_keys = (gather(c_win, U32, aligned([P, N], U32, "c_codes")), c_plane[C_ROW:P, :].bitcast(U8))
        queries_quantise(other_bf[:, 3:5, :], guest(ROWS_AT - 512, [P, 2 * P], U32, "q_late"), ["q3", "m3"])

        def score_pass(ps, queries, keys, start, stop):
            codes, scale = keys
            nc.tensor.matmul_mx(ps[:], lhsT=q_words[queries].bitcast(FP8X4), lhsT_scale=q_scales[queries],
                                rhs=codes[:].bitcast(FP8X4), rhs_scale=scale, start=start, stop=stop)

        def by_place(ps):
            return ps[:].rearrange("q (p t) -> q t p", t=PLACES)

        def planes(name):
            return held.tile([P, PLACES, P], F32, name=name)

        joint, to_turn, turned = {}, {}, {}

        def joint_open(j, bank_number):
            joint[j] = bank(bank_number, [P, N], f"joint{j}")
            score_pass(joint[j], f"q{j}", k_keys, True, False)
            score_pass(joint[j], f"m{j}", k_keys, False, False)

        def joint_close(j):
            score_pass(joint[j], f"m{j}", c_keys, False, True)

        def joint_exp(j, exps):
            to_turn[j] = exps
            nc.scalar.activation(to_turn[j][:], by_place(joint[j]), ACT.Exp, bias=neg_ls[:, j : j + 1], scale=2.0)

        for j in range(2):
            joint[j] = bank(1 + j, [P, N], f"joint{j}")
            score_pass(joint[j], f"q{j}", k_keys, True, False)
        a_ps = bank(0, [P, N], "a_apart")
        score_pass(a_ps, f"q{APART}", k_keys, True, True)
        a_term = planes("a_term")
        nc.scalar.activation(a_term[:], by_place(a_ps), ACT.Identity, bias=neg_ls[:, APART : APART + 1], scale=1.5)
        for j in range(2):
            score_pass(joint[j], f"m{j}", k_keys, False, False)
        z_ps = bank(4, [P, N], "z_apart")
        score_pass(z_ps, f"q{APART}", c_keys, True, True)
        to_turn[APART] = guest(EXPONENT_AT, [P, PLACES, P], F32, "exponent")
        nc.vector.scalar_tensor_tensor(to_turn[APART][:], by_place(z_ps), -0.5, a_term[:], ALU.mult, ALU.add)
        joint_close(0)
        joint_exp(0, planes("exp0"))
        joint_close(1)
        joint_exp(1, planes("exp1"))
        joint_open(3, 3)
        joint_close(3)

        def weights_turn(j, bank_number):
            ps = bank(bank_number, [P, PLACES, P], f"turned{j}")
            for t in range(PLACES):
                nc.tensor.transpose(ps[:, t, :], to_turn[j][:, t, :], ident[:])
            turned[j] = ps[:].rearrange("p t q -> p q t")

        us_places = us_sb[:].unsqueeze(1).to_broadcast([P, P, PLACES])
        v_picked = {}

        def values_gather(e, picked, engines):
            v_picked[e] = picked
            share = N // len(engines)
            for n, engine in enumerate(engines):
                listed = v_win[e][:].indirect(offsets[:, n * share // 16 : (n + 1) * share // 16])
                if engine == "vector":
                    nc.vector.tensor_copy(picked[:, n * share : (n + 1) * share], listed)
                else:
                    nc.scalar.activation(picked[:, n * share : (n + 1) * share], listed, ACT.Copy)

        def values_turn(e, bank_number, rounded):
            pairs = v_picked[e][:].bitcast(F32)
            ps = bank(bank_number, [P, 2, P], f"v{e}")
            for u in range(2):
                nc.tensor.transpose(ps[:, u, :], pairs[:, u : 2 * P : 2], ident[:])
            nc.scalar.copy(rounded.bitcast(F32).rearrange("p (e u) -> p e u", u=2), ps[:].rearrange("p u e -> p e u"))

        values_gather(0, aligned([P, N], BF16, "v_picked0"), ["vector"])
        y_bf = guest(V_AT[0], [P, BLOCKS, P, PLACES], BF16, "y_bf")
        joint_exp(3, planes("exp3"))
        weights_turn(APART, 0)
        exp_apart = held.tile([P, P, PLACES], F32, name="exp_apart")
        nc.scalar.activation(exp_apart[:], turned[APART], ACT.Exp)
        nc.gpsimd.tensor_tensor(y_bf[:, APART], exp_apart[:], us_places, ALU.mult)
        for j, bank_number in ((0, 5), (1, 6), (3, 7)):
            weights_turn(j, bank_number)
            nc.vector.tensor_tensor(y_bf[:, j], turned[j], us_places, ALU.mult)
        v_scale = aligned([P, DV], U8, "v_scale")
        out_rows = out[0].rearrange("(m j) e -> m j e", j=BLOCKS)

        def values_quantise(rounded, codes, first):
            nc.vector.quantize_mx(codes.bitcast(FP8X4), v_scale[:, first : first + codes.shape[1]], rounded)

        def products(js, codes, first, bank_number):
            width = codes.shape[1]
            ps = bank(bank_number, [P, len(js), width], f"out_ps{js[0]}_{first}")
            for n, j in enumerate(js):
                cols = slice(j * P, (j + 1) * P)
                nc.tensor.matmul_mx(ps[:, n, :], lhsT=y_codes[j].bitcast(FP8X4), lhsT_scale=y_scale[:, cols],
                                    rhs=codes[:].bitcast(FP8X4), rhs_scale=v_scale[:, first : first + width], start=True, stop=True)
            return ps

        def store(ps, staged, js, first, copy, queue):
            copy(staged[:], ps[:])
            queue.dma_start(out_rows[:, js[0] : js[-1] + 1, first : first + ps.shape[2]], staged[:])

        y_scale = aligned([P, NQ], U8, "y_scale")
        y_codes = {}

        def weights_quantise(pair, codes):
            nc.vector.quantize_mx(codes[:].bitcast(FP8X4), y_scale[:, 2 * P * pair : 2 * P * (pair + 1)],
                                  y_bf[:, 2 * pair : 2 * pair + 2].rearrange("p a q t -> p (a q t)"))
            for n in range(2):
                y_codes[2 * pair + n] = codes[:, n * P : (n + 1) * P]

        weights_quantise(0, aligned([P, 2 * P], U32, "y_codes01"))
        values_gather(1, aligned([P, N], BF16, "v_picked1"), ["scalar"])
        v0_bf = guest(V_AT[1], [P, N], BF16, "v0_bf")
        values_turn(0, 4, v0_bf[:])
        values_gather(2, aligned([P, N], BF16, "v_picked2"), ["vector", "scalar"])
        weights_quantise(1, guest(V_AT[2], [P, 2 * P], U32, "y_codes23"))
        v1_bf = guest(V_AT[2] + ROOM, [P, N], BF16, "v1_bf")
        values_turn(1, 1, v1_bf[:])
        v01_codes = guest(V_AT[2] + 2 * ROOM, [P, 2 * P], U32, "v01_codes")
        values_quantise(v0_bf[:], v01_codes[:, 0:P], 0)
        values_quantise(v1_bf[:], v01_codes[:, P : 2 * P], P)
        v2_bf = aligned([P, N], BF16, "v2_bf")
        values_turn(2, 5, v2_bf[:])
        early_a = products([0, 1], v01_codes, 0, 2)
        early_b = products([2, 3], v01_codes, 0, 3)
        values_gather(3, guest(LAST_AT, [P, N], BF16, "v_picked3"), ["vector", "scalar"])
        v2_codes = guest(V_AT[3], [P, P], U32, "v2_codes")
        values_quantise(v2_bf[:], v2_codes[:], 2 * P)
        store(early_a, guest(V_AT[3] + ROOM, [P, 2, 2 * P], F32, "out_a"), [0, 1], 0, nc.scalar.copy, nc.sync)
        store(early_b, guest(V_AT[3] + 2 * ROOM, [P, 2, 2 * P], F32, "out_b"), [2, 3], 0, nc.vector.tensor_copy, nc.sync)
        v3_bf = guest(V3_BF_AT, [P, N], BF16, "v3_bf")
        values_turn(3, 0, v3_bf[:])
        middle_a = products([0, 1], v2_codes, 2 * P, 6)
        middle_b = products([2, 3], v2_codes, 2 * P, 1)
        v3_codes = aligned([P, P], U32, "v3_codes")
        values_quantise(v3_bf[:], v3_codes[:], 3 * P)
        store(middle_a, guest(LAST_AT, [P, 2, P], F32, "out_middle_a"), [0, 1], 2 * P, nc.scalar.copy, nc.sync)
        store(middle_b, guest(V3_BF_AT, [P, 2, P], F32, "out_middle_b"), [2, 3], 2 * P, nc.vector.tensor_copy, nc.sync)
        last_a = products([0, 1], v3_codes, 3 * P, 7)
        last_b = products([2, 3], v3_codes, 3 * P, 4)
        store(last_a, held.tile([P, 2, P], F32, name="out_last_a"), [0, 1], 3 * P, nc.vector.tensor_copy, nc.sync)
        store(last_b, held.tile([P, 2, P], F32, name="out_last_b"), [2, 3], 3 * P, nc.scalar.copy, nc.scalar)
